import numpy as np, ml_dtypes
CORES = [40,41,42,43,44,45,46,47]
N = 8
import mx_ref
BF = ml_dtypes.bfloat16
def entries(a):
    return np.ascontiguousarray(a.T).reshape(-1)
def table(e):
    return np.ascontiguousarray(np.reshape(e, (-1, 16)).T).astype(np.int32)
def cols(t, e):
    v = np.concatenate([t.reshape(128, -1, 4), np.zeros((128, 1, 4), BF)], axis=1)
    return np.ascontiguousarray(v[:, e]).reshape(128, -1)
def f(rng, *shape):
    return mx_ref.flush((rng.standard_normal(shape, dtype=np.float32) * np.exp2(rng.integers(-2, 3, shape[:-1] + (1,)))).astype(BF))
def wide(rng, *shape, cols=0):
    v = rng.standard_normal(shape, dtype=np.float32) * np.exp2(rng.integers(-12, 13, shape)).astype(np.float32)
    if cols: v *= np.repeat(np.exp2(rng.integers(-cols, cols + 1, shape[:-2] + (1, shape[-1] // 4))) * (rng.random(shape[:-2] + (1, shape[-1] // 4)) > 0.0625), 4, axis=-1).astype(np.float32)
    return mx_ref.flush(v.astype(BF))
T, S, CAPP, CL, K, O = 256, 256, 48, 48, 1024, 2
H = 65536 // (N * K)
def counts(rng, tot, cap, lead=None, least=2):
    n = np.full(N, least)
    if lead is not None:
        for i in range(N):
            q = (lead + i) % N; n[q] += min(cap - n[q], tot - n.sum())
    while n.sum() < tot:
        q = rng.integers(0, N)
        if n[q] < cap: n[q] += 1
    return n
def lists(rng, full=False, hot=False, other=False, few=False):
    a, b = rng.integers(1, N, 2); z = rng.integers(0, N); least = 0 if full else 2
    n = np.stack([counts(rng, T, CAPP, (r + a) % N if full or other else z if hot else None, least) for r in range(N)])
    part, pool = [], []
    for q in range(N):
        c = n[:, q].sum(); p = rng.permutation(K)[:c]
        key = q + N * (p + K * rng.integers(0, H, c))
        part.append(np.split(key, np.cumsum(n[:, q])[:-1])); pool.append(rng.choice(key, 1) if few else key)
    has = [np.concatenate([part[q][r] for q in range(N)]) for r in range(N)]
    ky, lk = [], []
    for r in range(N):
        ky.append(table(rng.permutation(has[r])))
        if other:
            s = (r + a) % N; e = rng.permutation(has[s])[:S]; m = np.bincount(e & (N - 1), minlength=N); e = [e]
            for q in ((s + a) % N, (s + a + 1) % N):
                more = rng.permutation(np.setdiff1d(pool[q], part[q][s]))[:CL - m[q]]
                e.append(more); m[q] += len(more)
            while m.sum() < S:
                q = rng.integers(0, N)
                if m[q] < CL: m[q] += 1; e.append(rng.choice(part[q][s], 1))
            u = np.unique(np.concatenate(e)); lead = part[(s + a) % N][s]
            assert len(lead) == CAPP and np.isin(lead, u).all()
            assert any(q != r and m[q] == CL and ((u & (N - 1)) == q).sum() == CL for q in range(N))
        else:
            m = counts(rng, S, CL, (r + b) % N if full else z if hot else None, least)
            e = [rng.choice(pool[q], m[q]) for q in range(N)]
        lk.append(table(rng.permutation(np.concatenate(e))))
    return {"ky": np.stack(ky), "lk": np.stack(lk)}
def setup_inputs(rng):
    d = lists(rng)
    return {"x": f(rng, N, 128, 4 * T), "ky": d["ky"], "lk": d["lk"], "w": f(rng, N, 128, 512 * O)}
def setup_inputs_full(rng):
    return {**setup_inputs(rng), **lists(rng, full=True)}
def setup_inputs_hot(rng):
    return {**setup_inputs(rng), **lists(rng, hot=True)}
def setup_inputs_other(rng):
    return {**setup_inputs(rng), **lists(rng, other=True)}
def setup_inputs_repeats(rng):
    return {**setup_inputs(rng), **lists(rng, few=True)}
def setup_inputs_spread(rng):
    d = setup_inputs(rng); d["x"] = wide(rng, N, 128, 4 * T, cols=8); return d
def check_inputs(d):
    b = []
    keys = np.stack([entries(d["ky"][r]) for r in range(N)]).astype(np.int64)
    if keys.min() < 0 or keys.max() > 65535: b.append("ky")
    if len(np.unique(keys & (N * K - 1))) != N * T: b.append("owner and place")
    for r in range(N):
        l = entries(d["lk"][r]).astype(np.int64)
        if np.bincount(keys[r] & (N - 1), minlength=N).max() > CAPP: b.append("CAPP")
        if not np.isin(l, keys).all(): b.append("lk")
        if np.bincount(l & (N - 1), minlength=N).max() > CL: b.append("CL")
    return b
def reference(x, ky, lk, w):
    every = np.concatenate([x[r] for r in range(N)], axis=1)
    number = np.full(65536, -1); number[np.concatenate([entries(ky[r]) for r in range(N)])] = np.arange(N * T)
    y = np.zeros((N, 128, O * S), np.float32)
    for r in range(N):
        v = mx_ref.quantize(cols(every, number[entries(lk[r])]))
        for o in range(O): y[r][:, S * o:S * o + S] = mx_ref.matmul(mx_ref.quantize(np.ascontiguousarray(w[r][:, 512 * o:512 * o + 512])), v)
    return {"y": y}

@@ -1,0 +1,327 @@
+from concourse.bass import DstId, RemoteDMATransfer
+from concourse.mybir import dt, AluOpType, ActivationFunctionType
+
+N, S, CAP, K, O = 8, 256, 48, 1024, 2
+SL = N * CAP
+HALF = SL // 2
+RL = N * 64
+TAB = K + SL
+F8, F32, BF, I32, U16 = "float8_e4m3fn_x4", "float32", "bfloat16", "int32", "uint16"
+
+SCRATCH = {
+    "xb": ("sbuf", [128, 4 * S], BF), "wb": ("sbuf", [128, 512 * O], BF),
+    "xq": ("sbuf", [128, S], F8), "xs": ("sbuf", [128, S], "uint8"),
+    "wq": ("sbuf", [128, 128 * O], F8), "ws": ("sbuf", [128, 128 * O], "uint8"),
+    "kx": ("sbuf", [128, 64], I32), "ko": ("sbuf", [128, 64], I32), "kt": ("sbuf", [128, 64], I32),
+    "kf": ("sbuf", [128, 256], I32), "pl": ("sbuf", [128, 256], I32),
+    "pio": ("sbuf", [128, 4], I32), "two": ("sbuf", [128, 4], I32), "kf0": ("sbuf", [128, 128], I32),
+    "cq": ("sbuf", [128, 64], F32), "m64": ("sbuf", [128, 64], F32), "sv": ("sbuf", [128, SL], BF),
+    "hh": ("sbuf", [128, 4], I32), "h3": ("sbuf", [128, 4], I32),
+    "p31": ("sbuf", [128, 4], I32), "c4": ("sbuf", [128, 4], I32), "c64": ("sbuf", [128, 4], U16),
+    "ev": ("sbuf", [128, 1], F32), "od": ("sbuf", [128, 1], F32), "h8": ("sbuf", [128, 1], F32),
+    "ini": ("sbuf", [128, 1], F32), "zz": ("sbuf", [128, 256], BF),
+    "win_k": ("sbuf", [128, SL], F32), "win_l": ("sbuf", [128, SL], F32),
+    "d_k": ("sbuf", [128, 24, 32], "float16"), "t_k": ("sbuf", [128, 24, 32], "float16"),
+    "t_l": ("sbuf", [128, SL], F32),
+    "mn": ("sbuf", [128, 24, 2], F32), "co": ("sbuf", [128, 24], U16), "co_me": ("sbuf", [128, 4], U16),
+    "ks": ("sbuf", [128, 24], U16), "rsf": ("sbuf", [128, 12], F32), "rs": ("sbuf", [128, 24], U16),
+    "x2": ("sbuf", [128, 32], BF), "x2t": ("sbuf", [128, 32], BF), "fof": ("sbuf", [128, 16], F32), "fo": ("sbuf", [128, 16], U16),
+    "kin": ("sbuf", [128, 8, 8], U16), "rin": ("sbuf", [128, 8, 8], U16),
+    "kofs": ("sbuf", [128, 24], U16), "rofs": ("sbuf", [128, 32], U16),
+    "tab": ("sbuf", [128, TAB], BF), "d_s": ("sbuf", [128, RL], BF), "t_s": ("sbuf", [128, 8, 64], BF),
+    "so": ("sbuf", [128, 24], U16), "so_me": ("sbuf", [128, 4], U16),
+    "pk_q": ("sbuf", [128, SL], F8), "pk_s": ("sbuf", [128, SL], "uint8"),
+    "in_q": ("sbuf", [128, SL], F8), "in_s": ("sbuf", [128, SL], "uint8"),
+    "p2_q": ("sbuf", [128, SL], F8), "p2_s": ("sbuf", [128, SL], "uint8"),
+    "bk_q": ("sbuf", [128, SL], F8), "bk_s": ("sbuf", [128, SL], "uint8"),
+    "fp_q": ("sbuf", [128, S], F8), "fp_s": ("sbuf", [128, S], "uint8"),
+    "ps": ("psum", [128, 2048], F32), "yb": ("sbuf", [128, S * O], F32),
+}
+for _c in "kl":
+    SCRATCH["e_" + _c] = ("sbuf", [128, 256], BF)
+    SCRATCH["ef_" + _c] = ("sbuf", [128, 256], BF)
+    SCRATCH["cu_" + _c] = ("sbuf", [128, 256], BF)
+    SCRATCH["ct_" + _c] = ("sbuf", [128, 256], BF)
+    SCRATCH["pr_" + _c] = ("sbuf", [128, 64], F32)
+    SCRATCH["rk_" + _c] = ("sbuf", [128, 64], F32)
+    SCRATCH["po_" + _c] = ("sbuf", [128, 8], U16)
+SEMAPHORES = ["v", "a", "t", "gi", "ld_x", "ld_w", "ld_t", "ld_k", "ld_l", "kin", "rin", "q1", "s1", "q2", "s2", "out", "st"]
+
+
+def rank_program(g, core, T, topo):
+    me = T.rank_of(core)
+    if me is None:
+        return
+    A = AluOpType
+    COPY = ActivationFunctionType.Copy
+    vec, act, ten, syn, sem = g.vector, g.scalar, g.tensor, g.sync, T.sem
+    nv, na, sent, seen = [0], [0], [0], {}
+
+    def V(ins):
+        ins.then_inc(sem.v, 1)
+        nv[0] += 1
+        return nv[0]
+
+    def C(ins):
+        ins.then_inc(sem.a, 1)
+        na[0] += 1
+        return na[0]
+
+    def W(q, name, s, k):
+        if seen.get((name, s), 0) < k:
+            q.wait_ge(sem[s], k)
+            seen[(name, s)] = k
+
+    def vw(k, s="v"):
+        W(vec, "v", s, k)
+
+    def aw(k, s="a"):
+        W(act, "a", s, k)
+
+    def sw(k, s):
+        W(syn, "s", s, k)
+
+    def gw(k, s):
+        W(g, "g", s, k)
+
+    near, far = 0, 0
+    dests = []
+    for i in range(1, N):
+        q = (me + i) % N
+        dst = T.cores[q]
+        eng = topo.engines(core, dst)
+        if topo.die(dst) == topo.die(core):
+            pick = eng[0::2][2 * near:2 * near + 2]
+            near += 1
+        else:
+            pick = eng[1::2][2 * far:2 * far + 2]
+            far += 1
+        rid, pid, _ = topo.addr(dst)
+        dests.append((q, DstId(rid=rid, pnc=pid), sum(1 << e for e in pick)))
+    EACH = 2 * (N - 1)
+
+    def send(src, dst, s):
+        g.remote_dma_fused([RemoteDMATransfer(dst_ids=[d], dma_engine_mask=m, remote_sem=sem[s], src=src(q), dst=dst)
+                            for q, d, m in dests], local_sem=sem.out)
+        sent[0] += EACH
+
+    def codes(out, win, off):
+        return V(vec.tensor_copy(out.bitcast(dt.uint32), win.bitcast(dt.uint32).indirect(off)))
+
+    def scales(out, win, off):
+        return C(act.activation(out, win.indirect(off), COPY))
+
+    i_kx = V(vec.memset(T.kx[:], 0))
+    sw(i_kx, "v")
+    aw(i_kx, "v")
+    for src, c0 in ((T.ky, 0), (T.lk, 32)):
+        for b in range(4):
+            (syn if b < 2 else act).dma_start(T.kx[32 * b:32 * b + 8, c0:c0 + 32], src[:]).then_inc(sem.ld_t, 16)
+    act.dma_start(T.xb[:], T.x[:]).then_inc(sem.ld_x, 16)
+
+    def iota(ap, pattern, base, cm=0, small=True):
+        (g.iota(ap, pattern, base, cm, allow_small_or_imprecise_dtypes=True) if small else g.iota(ap, pattern, base, cm)).then_inc(sem.gi, 1)
+    iota(T.pio[:], [[0, 4]], 0, 1, small=False)
+    iota(T.kf0[:], [[16, 8], [128, 16]], 0, small=False)
+    iota(T.two[:], [[2, 4]], 0, small=False)
+    iota(T.cq[:], [[0, 8], [1, 8]], 0)
+    iota(T.win_k[:], [[0, 8], [1, CAP]], K + CAP * me)
+    iota(T.win_l[:], [[0, SL]], K)
+    iota(T.sv[:], [[1, SL]], -HALF)
+    i_zz = V(vec.memset(T.zz[:], 0.0))
+    V(vec.memset(T.kf[:, 128:256], 0))
+    vw(1, "gi")
+    i_hh = V(vec.tensor_scalar(T.hh[:], T.pio[:], 4, 1, A.logical_shift_right, A.bitwise_and))
+    V(vec.tensor_scalar(T.h3[:], T.pio[:], 3, 1, A.logical_shift_right, A.bitwise_and))
+    i_31 = V(vec.tensor_scalar(T.p31[:], T.pio[:], 31, None, A.bitwise_and))
+    vw(i_hh)
+    i_h8 = V(vec.tensor_scalar(T.h8[:], T.hh[:, 0:1], 8.0, None, A.mult))
+    vw(i_h8)
+    vw(2, "gi")
+    i_kf = V(vec.tensor_scalar(T.kf[:, 0:128], T.kf0[:], T.h8[:, 0:1], None, A.add))
+    sw(i_kf, "v")
+    aw(i_kf, "v")
+    for src, c0, s in ((T.ky, 0, "ld_k"), (T.lk, 128, "ld_l")):
+        for b in range(4):
+            for h in range(2):
+                p = 32 * b + 16 * h + 1
+                (syn if b < 2 else act).dma_start(T.kf[p:p + 1, c0:c0 + 128], src[h:16:2, :]).then_inc(sem[s], 16)
+    syn.dma_start(T.wb[:], T.w[:]).then_inc(sem.ld_w, 16)
+    aw(i_zz, "v")
+    for c0 in range(0, TAB, 256):
+        a_tab = C(act.activation(T.tab[:, c0:min(TAB, c0 + 256)], T.zz[:, 0:min(256, TAB - c0)], COPY))
+    vw(3, "gi")
+    vw(i_31)
+    i = V(vec.tensor_tensor(T.c4[:], T.h3[:], T.two[:], A.add))
+    V(vec.tensor_scalar(T.ini[:], T.p31[:, 0:1], float(CAP // 4), float(-HALF - 1), A.mult, A.add))
+    V(vec.memset(T.e_k[:], 0.0))
+    V(vec.memset(T.e_l[:], 0.0))
+    vw(i)
+    V(vec.tensor_copy(T.c64[:], T.c4[:]))
+    vw(4, "gi")
+    i_con = V(vec.tensor_scalar(T.m64[:], T.cq[:], 1.0, None, A.min))
+
+    vw(i_con)
+    vw(128, "ld_t")
+    i = V(vec.tensor_scalar(T.ko[:], T.kx[:], N - 1, None, A.bitwise_and))
+    vw(i)
+    i = V(vec.transpose(T.kt[:], T.ko[:]))
+    vw(i)
+    kl = ("k", "l")
+    last = {}
+    for c, w0 in (("k", 0), ("l", 32)):
+        last[c] = V(vec.tensor_tensor(T["e_" + c][:, 0:256:4], T.kt[:, w0:w0 + 8].indirect(T.c64[:, 0:4]), T.cq[:], A.is_equal))
+    for c in kl:
+        vw(last[c])
+        last[c] = V(vec.transpose(T["ef_" + c][:], T["e_" + c][:]))
+    for c in kl:
+        vw(last[c])
+        last[c] = V(vec.tensor_tensor_scan(T["cu_" + c][:], T["ef_" + c][:], T.zz[:], T.ini[:, 0:1], A.add, A.add))
+    for c in kl:
+        vw(last[c])
+        last[c] = V(vec.transpose(T["ct_" + c][:], T["cu_" + c][:]))
+    for c in kl:
+        vw(last[c])
+        last[c] = V(vec.tensor_tensor(T["pr_" + c][:], T["e_" + c][:, 0:256:4], T["ct_" + c][:, 0:256:4], A.mult))
+    for c in kl:
+        vw(last[c])
+        last[c] = V(vec.tensor_tensor_scan(T["rk_" + c][:], T.m64[:], T["pr_" + c][:], 0.0, A.mult, A.add))
+    i_rkl = last["l"]
+    vw(128, "ld_k")
+    V(vec.tensor_scalar(T.pl[:, 0:128], T.kf[:, 0:128], 3, K - 1, A.logical_shift_right, A.bitwise_and))
+    for c in kl:
+        vw(last[c])
+        last[c] = V(vec.tensor_scalar(T["po_" + c][:], T["rk_" + c][:, 7:64:8], float(HALF), None, A.add))
+
+    vw(5, "gi")
+    vw(last["l"])
+    i_sk = V(vec.tensor_copy(T.win_k[:, 0:SL].indirect(T.po_k[:, 0:8]), T.pl[:, 0:128]))
+    vw(128, "ld_l")
+    i_pll = V(vec.tensor_scalar(T.pl[:, 128:256], T.kf[:, 128:256], 3, K - 1, A.logical_shift_right, A.bitwise_and))
+    vw(i_sk)
+    i = V(vec.tensor_copy(T.d_k[:, :, 0:16], T.win_k[:]))
+    vw(16, "ld_x")
+    i_xq = V(vec.quantize_mx(T.xq[:], T.xs[:], T.xb[:]))
+    vw(i)
+    i = V(vec.tensor_copy(T.d_k[:, :, 16:32], T.d_k[:, :, 0:16]))
+    vw(i)
+    i = V(vec.transpose(T.t_k[:], T.d_k[:]))
+    vw(i)
+    i_mn = V(vec.tensor_tensor(T.mn[:], T.t_k[:, :, 0:2], T.t_k[:, :, 16:18], A.min))
+    vw(i_mn)
+    i_ks = V(vec.tensor_copy(T.ks[:], T.mn[:, :, 1]))
+    gw(i_ks, "v")
+    send(lambda q: T.ks[:, 3 * q:3 * q + 3], T.kin[:, me, 0:3], "kin")
+    i_co = V(vec.tensor_scalar(T.co[:], T.mn[:, :, 0], float(S - 1), None, A.min))
+
+    vw(6, "gi")
+    vw(i_pll)
+    i = V(vec.tensor_copy(T.win_l[:, 0:SL].indirect(T.po_l[:, 0:8]), T.pl[:, 128:256]))
+    vw(i)
+    i = V(vec.transpose(T.t_l[:], T.win_l[:]))
+    vw(i)
+    i = V(vec.tensor_tensor(T.rsf[:], T.t_l[:, 1:SL:32], T.t_l[:, 17:SL:32], A.min))
+    vw(i)
+    V(vec.tensor_copy(T.rs[:, 0:24:2], T.rsf[:]))
+    i_rs = V(vec.tensor_copy(T.rs[:, 1:24:2], T.rsf[:]))
+    gw(i_rs, "v")
+    send(lambda q: T.rs[:, 3 * q - q % 2:3 * q - q % 2 + 4], T.rin[:, me, 0:4], "rin")
+
+    mine = slice(CAP * me, CAP * me + CAP)
+    aw(max(i_xq, i_co), "v")
+    a_pk = scales(T.pk_s[:, 0:SL], T.xs[:, 0:S], T.co[:, 0:24])
+    i_pk = codes(T.pk_q[:, 0:SL], T.xq[:, 0:S], T.co[:, 0:24])
+    gw(a_pk, "a")
+    send(lambda q: T.pk_s[:, CAP * q:CAP * q + CAP], T.in_s[:, mine], "s1")
+    gw(i_pk, "v")
+    send(lambda q: T.pk_q[:, CAP * q:CAP * q + CAP].bitcast(dt.uint8), T.in_q[:, mine].bitcast(dt.uint8), "q1")
+
+    i = V(vec.tensor_scalar(T.co_me[:, 0:3], T.mn[:, 3 * me:3 * me + 3, 0], float(S - 1), None, A.min))
+    V(vec.tensor_copy(T.kin[:, me, 0:3], T.ks[:, 3 * me:3 * me + 3]))
+    V(vec.tensor_copy(T.od[:], T.hh[:, 0:1]))
+    i_ev = V(vec.tensor_scalar(T.ev[:], T.hh[:, 0:1], -1.0, 1.0, A.mult, A.add))
+    vw(i_rs)
+    i_own = V(vec.tensor_copy(T.rin[:, me, 0:4], T.rs[:, 3 * me - me % 2:3 * me - me % 2 + 4]))
+    aw(max(i_ev, i_rkl), "v")
+    a_own = scales(T.in_s[:, mine], T.xs[:, 0:S], T.co_me[:, 0:3])
+    for c0 in (0, 16):
+        C(act.activation(T.x2[:, c0:c0 + 16:2], T.rk_l[:, 7:64:8], COPY, scale=T.ev[:, 0:1]))
+        a_x2 = C(act.activation(T.x2[:, c0 + 1:c0 + 16:2], T.rk_l[:, 7:64:8], COPY, scale=T.od[:, 0:1]))
+    vw(i)
+    i_own1 = codes(T.in_q[:, mine], T.xq[:, 0:S], T.co_me[:, 0:3])
+
+    vw(7, "gi")
+    vw(a_tab, "a")
+    vw(i_own)
+    vw(EACH, "kin")
+    i = V(vec.tensor_copy(T.kofs[:], T.kin[:, :, 0:3]))
+    vw(i)
+    i_tab = V(vec.tensor_copy(T.tab[:, 0:TAB].indirect(T.kofs[:, 0:24]), T.sv[:]))
+    vw(EACH, "rin")
+    i = V(vec.tensor_copy(T.rofs[:], T.rin[:, :, 0:4]))
+    aw(i, "v")
+    a_g = C(act.activation(T.d_s[:, RL // 2:RL], T.tab[:, 0:TAB].indirect(T.rofs[:, 16:32]), COPY))
+    vw(i)
+    i = V(vec.tensor_copy(T.d_s[:, 0:RL // 2], T.tab[:, 0:TAB].indirect(T.rofs[:, 0:16])))
+    vw(i)
+    vw(a_g, "a")
+    i = V(vec.transpose(T.t_s[:], T.d_s[:]))
+    vw(i)
+    m0 = 16 * (me % 2)
+    i_so = V(vec.tensor_scalar(T.so[:], T.t_s[:, :, m0:m0 + 48:16], float(HALF), None, A.add))
+
+    vw(i_so)
+    vw(a_own, "a")
+    vw(EACH, "q1")
+    aw(max(i_so, i_own1), "v")
+    aw(a_own)
+    aw(EACH, "s1")
+    i_p2 = codes(T.p2_q[:, 0:SL], T.in_q[:, 0:SL], T.so[:, 0:24])
+    a_p2 = scales(T.p2_s[:, 0:SL], T.in_s[:, 0:SL], T.so[:, 0:24])
+    gw(i_p2, "v")
+    send(lambda q: T.p2_q[:, CAP * q:CAP * q + CAP].bitcast(dt.uint8), T.bk_q[:, mine].bitcast(dt.uint8), "q2")
+    gw(a_p2, "a")
+    send(lambda q: T.p2_s[:, CAP * q:CAP * q + CAP], T.bk_s[:, mine], "s2")
+    i_sm = V(vec.tensor_scalar(T.so_me[:, 0:3], T.t_s[:, me, m0:m0 + 48:16], float(HALF), None, A.add))
+    vw(i_sm)
+    i_own2 = codes(T.bk_q[:, mine], T.in_q[:, 0:SL], T.so_me[:, 0:3])
+    aw(i_sm, "v")
+    a_own2 = scales(T.bk_s[:, mine], T.in_s[:, 0:SL], T.so_me[:, 0:3])
+    vw(16, "ld_w")
+    V(vec.quantize_mx(T.wq[:], T.ws[:], T.wb[:]))
+    vw(a_x2, "a")
+    i = V(vec.transpose(T.x2t[:], T.x2[:]))
+    vw(i)
+    i = V(vec.tensor_tensor(T.fof[:], T.x2t[:, 0:16], T.x2t[:, 16:32], A.add))
+    vw(i)
+    i_fo = V(vec.tensor_scalar(T.fo[:], T.fof[:], float(HALF), None, A.add))
+
+    vw(max(i_own2, i_fo))
+    vw(EACH, "q2")
+    aw(i_fo, "v")
+    aw(a_own2)
+    aw(EACH, "s2")
+    done = []
+    for f in range(2):
+        c = slice(128 * f, 128 * f + 128)
+        off = T.fo[:, 8 * f:8 * f + 8]
+        done.append((codes(T.fp_q[:, c], T.bk_q[:, 0:SL], off), scales(T.fp_s[:, c], T.bk_s[:, 0:SL], off)))
+    for f in range(2):
+        c = slice(128 * f, 128 * f + 128)
+        W(ten, "t", "v", done[f][0])
+        W(ten, "t", "a", done[f][1])
+        for o in range(O):
+            ws = slice(128 * o, 128 * o + 128)
+            b0 = 512 * (O * f + o)
+            ten.matmul_mx(T.ps[:, b0:b0 + 128], T.wq[:, ws], T.ws[:, ws], T.fp_q[:, c], T.fp_s[:, c], True, True).then_inc(sem.t, 1)
+    for f in range(2):
+        vw(O * f + 1, "t")
+        iv = V(vec.tensor_copy(T.yb[:, 128 * f:128 * f + 128], T.ps[:, 1024 * f:1024 * f + 128]))
+        aw(O * f + 2, "t")
+        ia = C(act.activation(T.yb[:, S + 128 * f:S + 128 * f + 128], T.ps[:, 1024 * f + 512:1024 * f + 640], COPY))
+    sw(iv, "v")
+    syn.dma_start(T.y[:, 0:S], T.yb[:, 0:S]).then_inc(sem.st, 16)
+    aw(ia)
+    act.dma_start(T.y[:, S:2 * S], T.yb[:, S:2 * S]).then_inc(sem.st, 16)
+    sw(32, "st")
+    gw(sent[0], "out")

@@ -3,49 +3,45 @@ from concourse.mybir import dt, AluOpType, ActivationFunctionType
 
 N, S, CAP, K, O = 8, 256, 48, 1024, 2
 SL = N * CAP
-HALF = SL // 2
+WIN = SL + 32
+NB = WIN // 32
+LAND = SL + 16
+MID = LAND // 2
+TAB = K + 16 * N
 RL = N * 64
-TAB = K + SL
 F8, F32, BF, I32, U16 = "float8_e4m3fn_x4", "float32", "bfloat16", "int32", "uint16"
 
 SCRATCH = {
     "xb": ("sbuf", [128, 4 * S], BF), "wb": ("sbuf", [128, 512 * O], BF),
     "xq": ("sbuf", [128, S], F8), "xs": ("sbuf", [128, S], "uint8"),
     "wq": ("sbuf", [128, 128 * O], F8), "ws": ("sbuf", [128, 128 * O], "uint8"),
-    "kx": ("sbuf", [128, 64], I32), "ko": ("sbuf", [128, 64], I32), "kt": ("sbuf", [128, 64], I32),
-    "kf": ("sbuf", [128, 256], I32), "pl": ("sbuf", [128, 256], I32),
-    "pio": ("sbuf", [128, 4], I32), "two": ("sbuf", [128, 4], I32), "kf0": ("sbuf", [128, 128], I32),
-    "cq": ("sbuf", [128, 64], F32), "m64": ("sbuf", [128, 64], F32), "sv": ("sbuf", [128, SL], BF),
-    "hh": ("sbuf", [128, 4], I32), "h3": ("sbuf", [128, 4], I32),
-    "p31": ("sbuf", [128, 4], I32), "c4": ("sbuf", [128, 4], I32), "c64": ("sbuf", [128, 4], U16),
-    "ev": ("sbuf", [128, 1], F32), "od": ("sbuf", [128, 1], F32), "h8": ("sbuf", [128, 1], F32),
-    "ini": ("sbuf", [128, 1], F32), "zz": ("sbuf", [128, 256], BF),
-    "win_k": ("sbuf", [128, SL], F32), "win_l": ("sbuf", [128, SL], F32),
-    "d_k": ("sbuf", [128, 24, 32], "float16"), "t_k": ("sbuf", [128, 24, 32], "float16"),
-    "t_l": ("sbuf", [128, SL], F32),
-    "mn": ("sbuf", [128, 24, 2], F32), "co": ("sbuf", [128, 24], U16), "co_me": ("sbuf", [128, 4], U16),
-    "ks": ("sbuf", [128, 24], U16), "rsf": ("sbuf", [128, 12], F32), "rs": ("sbuf", [128, 24], U16),
-    "x2": ("sbuf", [128, 32], BF), "x2t": ("sbuf", [128, 32], BF), "fof": ("sbuf", [128, 16], F32), "fo": ("sbuf", [128, 16], U16),
-    "kin": ("sbuf", [128, 8, 8], U16), "rin": ("sbuf", [128, 8, 8], U16),
-    "kofs": ("sbuf", [128, 24], U16), "rofs": ("sbuf", [128, 32], U16),
-    "tab": ("sbuf", [128, TAB], BF), "d_s": ("sbuf", [128, RL], BF), "t_s": ("sbuf", [128, 8, 64], BF),
-    "so": ("sbuf", [128, 24], U16), "so_me": ("sbuf", [128, 4], U16),
-    "pk_q": ("sbuf", [128, SL], F8), "pk_s": ("sbuf", [128, SL], "uint8"),
-    "in_q": ("sbuf", [128, SL], F8), "in_s": ("sbuf", [128, SL], "uint8"),
-    "p2_q": ("sbuf", [128, SL], F8), "p2_s": ("sbuf", [128, SL], "uint8"),
-    "bk_q": ("sbuf", [128, SL], F8), "bk_s": ("sbuf", [128, SL], "uint8"),
+    "kx": ("sbuf", [128, 32], I32), "ko": ("sbuf", [128, 32], I32), "kt": ("sbuf", [128, 32], I32),
+    "kf": ("sbuf", [128, 128], I32), "pl": ("sbuf", [128, 128], I32),
+    "pio": ("sbuf", [128, 4], I32), "lane": ("sbuf", [128, 1], I32), "hh": ("sbuf", [128, 1], I32),
+    "two": ("sbuf", [128, 4], F32), "cq": ("sbuf", [128, 64], F32), "m64": ("sbuf", [128, 64], F32),
+    "lanef": ("sbuf", [128, 1], F32), "h3": ("sbuf", [128, 1], F32), "c64": ("sbuf", [128, 4], U16),
+    "ev": ("sbuf", [128, 1], F32), "od": ("sbuf", [128, 1], F32), "eb": ("sbuf", [128, 1], F32),
+    "tent": ("sbuf", [128, 1], F32), "ini": ("sbuf", [128, 1], F32), "fd": ("sbuf", [128, 4], F32),
+    "cv": ("sbuf", [128, 2], F32), "cm": ("sbuf", [128, 2], F32), "cw": ("sbuf", [128, 2], F32), "cot": ("sbuf", [128, 2], U16),
+    "zz": ("sbuf", [128, TAB // 4], BF), "sv0": ("sbuf", [128, 128], F32), "sv": ("sbuf", [128, 128], BF),
+    "e": ("sbuf", [128, 128], BF), "ef": ("sbuf", [128, 128], BF), "cu": ("sbuf", [128, 128], BF),
+    "ct": ("sbuf", [128, 128], BF), "pr": ("sbuf", [128, 64], F32), "rk": ("sbuf", [128, 64], F32),
+    "tb": ("sbuf", [128, 1], F32), "pob": ("sbuf", [128, 8], BF),
+    "po": ("sbuf", [128, 8], U16), "win": ("sbuf", [128, WIN], F32), "tw": ("sbuf", [128, NB, 32], F32),
+    "ab": ("sbuf", [128, 16], F32), "z": ("sbuf", [128, 32], F32), "co": ("sbuf", [128, 32], U16),
+    "x2": ("sbuf", [128, 32], BF), "x2t": ("sbuf", [128, 32], BF), "fof": ("sbuf", [128, 16], F32),
+    "fom": ("sbuf", [128, 16], F32), "fos": ("sbuf", [128, 16], F32), "fo": ("sbuf", [128, 16], U16),
+    "kr": ("sbuf", [128, N, 4], F32), "kofs": ("sbuf", [128, 8], U16), "rofs": ("sbuf", [128, 32], U16),
+    "tab": ("sbuf", [128, 2 * TAB], BF), "d_s": ("sbuf", [128, RL], BF), "t_s": ("sbuf", [128, 8, 64], BF),
+    "mx1": ("sbuf", [128, 24], F32), "mx2": ("sbuf", [128, 24], F32), "so": ("sbuf", [128, 26], U16),
+    "pk_q": ("sbuf", [128, SL - CAP], F8), "pk_s": ("sbuf", [128, SL - CAP], "uint8"),
+    "in_q": ("sbuf", [128, LAND], F8), "in_s": ("sbuf", [128, LAND], "uint8"),
+    "p2_q": ("sbuf", [128, SL - CAP], F8), "p2_s": ("sbuf", [128, SL - CAP], "uint8"),
+    "bk_q": ("sbuf", [128, LAND], F8), "bk_s": ("sbuf", [128, LAND], "uint8"),
     "fp_q": ("sbuf", [128, S], F8), "fp_s": ("sbuf", [128, S], "uint8"),
     "ps": ("psum", [128, 2048], F32), "yb": ("sbuf", [128, S * O], F32),
 }
-for _c in "kl":
-    SCRATCH["e_" + _c] = ("sbuf", [128, 256], BF)
-    SCRATCH["ef_" + _c] = ("sbuf", [128, 256], BF)
-    SCRATCH["cu_" + _c] = ("sbuf", [128, 256], BF)
-    SCRATCH["ct_" + _c] = ("sbuf", [128, 256], BF)
-    SCRATCH["pr_" + _c] = ("sbuf", [128, 64], F32)
-    SCRATCH["rk_" + _c] = ("sbuf", [128, 64], F32)
-    SCRATCH["po_" + _c] = ("sbuf", [128, 8], U16)
-SEMAPHORES = ["v", "a", "t", "gi", "ld_x", "ld_w", "ld_t", "ld_k", "ld_l", "kin", "rin", "q1", "s1", "q2", "s2", "out", "st"]
+SEMAPHORES = ["v", "a", "t", "gi", "ld_x", "ld_w", "ld_t", "ld_f", "kr", "q1", "s1", "q2", "s2", "out", "st"]
 
 
 def rank_program(g, core, T, topo):
@@ -53,7 +49,7 @@ def rank_program(g, core, T, topo):
     if me is None:
         return
     A = AluOpType
-    COPY = ActivationFunctionType.Copy
+    F = ActivationFunctionType
     vec, act, ten, syn, sem = g.vector, g.scalar, g.tensor, g.sync, T.sem
     nv, na, sent, seen = [0], [0], [0], {}
 
@@ -84,6 +80,9 @@ def rank_program(g, core, T, topo):
     def gw(k, s):
         W(g, "g", s, k)
 
+    def quad(b, n=1):
+        return slice(32 * b, 32 * (b + n))
+
     near, far = 0, 0
     dests = []
     for i in range(1, N):
@@ -97,170 +96,183 @@ def rank_program(g, core, T, topo):
             pick = eng[1::2][2 * far:2 * far + 2]
             far += 1
         rid, pid, _ = topo.addr(dst)
-        dests.append((q, DstId(rid=rid, pnc=pid), sum(1 << e for e in pick)))
+        dests.append((i, DstId(rid=rid, pnc=pid), sum(1 << e for e in pick)))
     EACH = 2 * (N - 1)
 
     def send(src, dst, s):
-        g.remote_dma_fused([RemoteDMATransfer(dst_ids=[d], dma_engine_mask=m, remote_sem=sem[s], src=src(q), dst=dst)
-                            for q, d, m in dests], local_sem=sem.out)
+        g.remote_dma_fused([RemoteDMATransfer(dst_ids=[d], dma_engine_mask=m, remote_sem=sem[s], src=src(i), dst=dst(i))
+                            for i, d, m in dests], local_sem=sem.out)
         sent[0] += EACH
 
     def codes(out, win, off):
         return V(vec.tensor_copy(out.bitcast(dt.uint32), win.bitcast(dt.uint32).indirect(off)))
 
     def scales(out, win, off):
-        return C(act.activation(out, win.indirect(off), COPY))
+        return C(act.activation(out, win.indirect(off), F.Copy))
 
-    i_kx = V(vec.memset(T.kx[:], 0))
-    sw(i_kx, "v")
-    aw(i_kx, "v")
-    for src, c0 in ((T.ky, 0), (T.lk, 32)):
-        for b in range(4):
-            (syn if b < 2 else act).dma_start(T.kx[32 * b:32 * b + 8, c0:c0 + 32], src[:]).then_inc(sem.ld_t, 16)
-    act.dma_start(T.xb[:], T.x[:]).then_inc(sem.ld_x, 16)
+    def slot(i):
+        return slice(16 + CAP * i, 16 + CAP * i + CAP)
+
+    def part(i):
+        return slice(CAP * (i - 1), CAP * i)
 
     def iota(ap, pattern, base, cm=0, small=True):
         (g.iota(ap, pattern, base, cm, allow_small_or_imprecise_dtypes=True) if small else g.iota(ap, pattern, base, cm)).then_inc(sem.gi, 1)
-    iota(T.pio[:], [[0, 4]], 0, 1, small=False)
-    iota(T.kf0[:], [[16, 8], [128, 16]], 0, small=False)
-    iota(T.two[:], [[2, 4]], 0, small=False)
-    iota(T.cq[:], [[0, 8], [1, 8]], 0)
-    iota(T.win_k[:], [[0, 8], [1, CAP]], K + CAP * me)
-    iota(T.win_l[:], [[0, SL]], K)
-    iota(T.sv[:], [[1, SL]], -HALF)
-    i_zz = V(vec.memset(T.zz[:], 0.0))
-    V(vec.memset(T.kf[:, 128:256], 0))
-    vw(1, "gi")
-    i_hh = V(vec.tensor_scalar(T.hh[:], T.pio[:], 4, 1, A.logical_shift_right, A.bitwise_and))
-    V(vec.tensor_scalar(T.h3[:], T.pio[:], 3, 1, A.logical_shift_right, A.bitwise_and))
-    i_31 = V(vec.tensor_scalar(T.p31[:], T.pio[:], 31, None, A.bitwise_and))
-    vw(i_hh)
-    i_h8 = V(vec.tensor_scalar(T.h8[:], T.hh[:, 0:1], 8.0, None, A.mult))
-    vw(i_h8)
-    vw(2, "gi")
-    i_kf = V(vec.tensor_scalar(T.kf[:, 0:128], T.kf0[:], T.h8[:, 0:1], None, A.add))
-    sw(i_kf, "v")
-    aw(i_kf, "v")
-    for src, c0, s in ((T.ky, 0, "ld_k"), (T.lk, 128, "ld_l")):
-        for b in range(4):
-            for h in range(2):
-                p = 32 * b + 16 * h + 1
-                (syn if b < 2 else act).dma_start(T.kf[p:p + 1, c0:c0 + 128], src[h:16:2, :]).then_inc(sem[s], 16)
-    syn.dma_start(T.wb[:], T.w[:]).then_inc(sem.ld_w, 16)
-    aw(i_zz, "v")
-    for c0 in range(0, TAB, 256):
-        a_tab = C(act.activation(T.tab[:, c0:min(TAB, c0 + 256)], T.zz[:, 0:min(256, TAB - c0)], COPY))
-    vw(3, "gi")
-    vw(i_31)
-    i = V(vec.tensor_tensor(T.c4[:], T.h3[:], T.two[:], A.add))
-    V(vec.tensor_scalar(T.ini[:], T.p31[:, 0:1], float(CAP // 4), float(-HALF - 1), A.mult, A.add))
-    V(vec.memset(T.e_k[:], 0.0))
-    V(vec.memset(T.e_l[:], 0.0))
-    vw(i)
-    V(vec.tensor_copy(T.c64[:], T.c4[:]))
-    vw(4, "gi")
-    i_con = V(vec.tensor_scalar(T.m64[:], T.cq[:], 1.0, None, A.min))
 
-    vw(i_con)
-    vw(128, "ld_t")
+    i_kx = V(vec.memset(T.kx[:], 0))
+    iota(T.kf[:], [[16, 8], [128, 16]], -8, 1, small=False)
+    iota(T.pio[:], [[0, 4]], 0, 1, small=False)
+    iota(T.two[:], [[2, 4]], 0)
+    iota(T.cq[:], [[0, 8], [1, 8]], 0)
+    iota(T.win[:], [[0, WIN // 16], [1, 16]], K + 16 * me)
+    iota(T.sv0[:], [[CAP, 8], [1, 16]], 16 - MID, 1)
+    G_KF, G_P, G_TWO, G_CQ, G_WIN, G_SV = range(1, 7)
+    i_zz = V(vec.memset(T.zz[:], 0.0))
+    V(vec.memset(T.e[:], 0.0))
+    V(vec.memset(T.z[:], 0.0))
+    V(vec.memset(T.so[:], 0))
+    vw(G_KF, "gi")
+    i_kf = V(vec.tensor_copy(T.kf[quad(1)], T.kf[quad(0)]))
+    sw(i_kx, "v")
+    aw(i_kx, "v")
+    for b in range(4):
+        (syn if b < 2 else act).dma_start(T.kx[32 * b:32 * b + 8, :], (T.ky if b < 2 else T.lk)[:]).then_inc(sem.ld_t, 16)
+    aw(G_KF, "gi")
+    sw(i_kf, "v")
+    for b in range(4):
+        for h in range(2):
+            p = 32 * b + 8 * h + 9
+            (syn if b < 2 else act).dma_start(T.kf[p:p + 1, :], (T.ky if b < 2 else T.lk)[h:16:2, :]).then_inc(sem.ld_f, 16)
+    act.dma_start(T.xb[:], T.x[:]).then_inc(sem.ld_x, 16)
+    syn.dma_start(T.wb[:], T.w[:]).then_inc(sem.ld_w, 16)
+
+    vw(G_P, "gi")
+    V(vec.tensor_scalar(T.lane[:], T.pio[:, 0:1], 15, None, A.bitwise_and))
+    i = V(vec.tensor_scalar(T.hh[:], T.pio[:, 0:1], 4, 1, A.logical_shift_right, A.bitwise_and))
+    vw(i)
+    V(vec.tensor_copy(T.lanef[:], T.lane[:]))
+    i_od = V(vec.tensor_copy(T.od[:], T.hh[:]))
+    i = V(vec.tensor_scalar(T.h3[:], T.lane[:], 8.0, None, A.is_ge))
+    vw(i)
+    vw(G_TWO, "gi")
+    i_c64 = V(vec.tensor_scalar(T.c64[:], T.two[:], T.h3[:, 0:1], None, A.add))
+    i_cv = V(vec.tensor_scalar(T.cv[:], T.two[:, 0:2], 8.0, T.lanef[:, 0:1], A.mult, A.add))
+    aw(i_od, "v")
+    top = (SL - CAP - 1) / 2
+    for b, n, sh in ((0, 1, 0), (1, 1, 16), (2, 2, 0)):
+        i = C(act.activation(T.tb[quad(b, n)], T.od[quad(b, n)], F.Identity, bias=float(sh - MID - 1 - top), scale=float(SL)))
+    aw(i)
+    i = C(act.activation(T.tent[:], T.lanef[:], F.Abs, bias=T.tb[:, 0:1], scale=float(CAP // 2)))
+    for b, n, sh in ((0, 1, 0), (1, 1, 1), (2, 2, 0)):
+        a_eb = C(act.activation(T.eb[quad(b, n)], T.od[quad(b, n)], F.Identity, bias=float(1 + sh), scale=-1.0))
+    aw(i)
+    a_ini = C(act.activation(T.ini[:], T.tent[:], F.Identity, bias=float(top), scale=-1.0))
+    aw(G_CQ, "gi")
+    a_m64 = C(act.activation(T.m64[:], T.cq[:], F.Sign))
+    a_ev = C(act.activation(T.ev[:], T.od[:], F.Identity, bias=1.0, scale=-1.0))
+    kops = [(0, 0, 2, 1), (2, 0, 2, 0)] if me % 2 == 0 else [(0, 0, 2, 1), (2, 0, 1, 0), (3, 1, 1, 2)]
+    third = {}
+    for n_op, (bo, bi, n, j) in enumerate(kops):
+        for d in range(n):
+            col = 2 * (3 * me // 2 + j) - (bi + d) - 3 * me
+            us = [col, col + 1]
+            ok = [0 <= u < 3 for u in us]
+            third[bo + d] = (us[0], 0) if ok[0] else (us[1], 1)
+            C(act.activation(T.fd[quad(bi + d), n_op:n_op + 1], T.od[quad(bi + d)], F.Identity,
+                             bias=0.0 if ok[0] else float(TAB), scale=float(TAB) * (ok[0] - ok[1])))
+    aw(i_zz, "v")
+    for c0 in range(0, TAB, TAB // 4):
+        C(act.activation(T.tab[:, c0:c0 + TAB // 4], T.zz[:], F.Identity, bias=float(-MID)))
+    aw(G_SV, "gi")
+    for b in range(4):
+        u, h = third[b]
+        a_tab = C(act.activation(T.sv[quad(b)], T.sv0[quad(b)], F.Identity, bias=float(16 * u - 32 * b - 16 * h)))
+
+    vw(64, "ld_t")
     i = V(vec.tensor_scalar(T.ko[:], T.kx[:], N - 1, None, A.bitwise_and))
     vw(i)
     i = V(vec.transpose(T.kt[:], T.ko[:]))
+    i_cm = V(vec.tensor_scalar(T.cm[:], T.cv[:], float(25 - 3 * me), -24.0, A.is_ge, A.mult))
     vw(i)
-    kl = ("k", "l")
-    last = {}
-    for c, w0 in (("k", 0), ("l", 32)):
-        last[c] = V(vec.tensor_tensor(T["e_" + c][:, 0:256:4], T.kt[:, w0:w0 + 8].indirect(T.c64[:, 0:4]), T.cq[:], A.is_equal))
-    for c in kl:
-        vw(last[c])
-        last[c] = V(vec.transpose(T["ef_" + c][:], T["e_" + c][:]))
-    for c in kl:
-        vw(last[c])
-        last[c] = V(vec.tensor_tensor_scan(T["cu_" + c][:], T["ef_" + c][:], T.zz[:], T.ini[:, 0:1], A.add, A.add))
-    for c in kl:
-        vw(last[c])
-        last[c] = V(vec.transpose(T["ct_" + c][:], T["cu_" + c][:]))
-    for c in kl:
-        vw(last[c])
-        last[c] = V(vec.tensor_tensor(T["pr_" + c][:], T["e_" + c][:, 0:256:4], T["ct_" + c][:, 0:256:4], A.mult))
-    for c in kl:
-        vw(last[c])
-        last[c] = V(vec.tensor_tensor_scan(T["rk_" + c][:], T.m64[:], T["pr_" + c][:], 0.0, A.mult, A.add))
-    i_rkl = last["l"]
-    vw(128, "ld_k")
-    V(vec.tensor_scalar(T.pl[:, 0:128], T.kf[:, 0:128], 3, K - 1, A.logical_shift_right, A.bitwise_and))
-    for c in kl:
-        vw(last[c])
-        last[c] = V(vec.tensor_scalar(T["po_" + c][:], T["rk_" + c][:, 7:64:8], float(HALF), None, A.add))
+    vw(G_CQ, "gi")
+    i = V(vec.tensor_tensor(T.e[:, 0:128:2], T.kt[:, 0:8].indirect(T.c64[:, 0:4]), T.cq[:], A.is_equal))
+    vw(i_cm)
+    i_cw = V(vec.tensor_tensor(T.cw[:], T.cv[:], T.cm[:], A.add))
+    vw(i)
+    i = V(vec.transpose(T.ef[:], T.e[:]))
+    vw(i_cw)
+    vw(a_eb, "a")
+    V(vec.tensor_scalar(T.cot[:], T.cw[:], T.eb[:, 0:1], float(3 * me - 1), A.add, A.add))
+    vw(i)
+    vw(a_ini, "a")
+    i = V(vec.tensor_tensor_scan(T.cu[:], T.ef[:], T.zz[:, 0:128], T.ini[:, 0:1], A.add, A.add))
+    vw(i)
+    i = V(vec.transpose(T.ct[:], T.cu[:]))
+    vw(i)
+    i = V(vec.tensor_tensor(T.pr[:], T.e[:, 0:128:2], T.ct[:, 0:128:2], A.mult))
+    vw(128, "ld_f")
+    V(vec.tensor_scalar(T.pl[:], T.kf[:], 3, K - 1, A.logical_shift_right, A.bitwise_and))
+    vw(i)
+    vw(a_m64, "a")
+    i = V(vec.tensor_tensor_scan(T.rk[:], T.m64[:], T.pr[:], 0.0, A.mult, A.add))
+    vw(i)
+    V(vec.tensor_scalar(T.po[:, 0:8:2], T.rk[:, 7:64:16], float(MID), None, A.add))
+    i = V(vec.tensor_scalar(T.po[:, 1:8:2], T.rk[:, 15:64:16], -1.0, float(MID), A.mult, A.add))
 
-    vw(5, "gi")
-    vw(last["l"])
-    i_sk = V(vec.tensor_copy(T.win_k[:, 0:SL].indirect(T.po_k[:, 0:8]), T.pl[:, 0:128]))
-    vw(128, "ld_l")
-    i_pll = V(vec.tensor_scalar(T.pl[:, 128:256], T.kf[:, 128:256], 3, K - 1, A.logical_shift_right, A.bitwise_and))
-    vw(i_sk)
-    i = V(vec.tensor_copy(T.d_k[:, :, 0:16], T.win_k[:]))
+    vw(i)
+    vw(G_WIN, "gi")
+    i = V(vec.tensor_copy(T.win[:, 0:WIN].indirect(T.po[:, 0:8]), T.pl[:]))
+    vw(i)
+    i = V(vec.transpose(T.tw[:], T.win[:]))
+    vw(i)
+    i_ab = V(vec.tensor_tensor(T.ab[:, 0:NB], T.tw[:, :, 9], T.tw[:, :, 17], A.min))
+
+    def three(q):
+        return T.ab[:, 3 * q // 2:3 * q // 2 + 3]
+    gw(i_ab, "v")
+    send(lambda i: three((me + i) % N), lambda i: T.kr[:, i, 0:3], "kr")
+    for po, c0, pi in ((quad(0, 2), 1, quad(0, 2)), (quad(0), 0, quad(1)), (quad(1), 2, quad(0))):
+        i = V(vec.tensor_tensor(T.z[po, c0:c0 + 2 * NB:2], T.tw[pi, :, 8], T.tw[pi, :, 16], A.min))
     vw(16, "ld_x")
-    i_xq = V(vec.quantize_mx(T.xq[:], T.xs[:], T.xb[:]))
+    V(vec.quantize_mx(T.xq[:, 0:128], T.xs[:, 0:128], T.xb[:, 0:512]))
     vw(i)
-    i = V(vec.tensor_copy(T.d_k[:, :, 16:32], T.d_k[:, :, 0:16]))
+    i = V(vec.tensor_scalar(T.co[:], T.z[:, 0:32].indirect(T.cot[:, 0:2]), float(S - 1), None, A.min))
+    V(vec.quantize_mx(T.xq[:, 128:256], T.xs[:, 128:256], T.xb[:, 512:1024]))
     vw(i)
-    i = V(vec.transpose(T.t_k[:], T.d_k[:]))
-    vw(i)
-    i_mn = V(vec.tensor_tensor(T.mn[:], T.t_k[:, :, 0:2], T.t_k[:, :, 16:18], A.min))
-    vw(i_mn)
-    i_ks = V(vec.tensor_copy(T.ks[:], T.mn[:, :, 1]))
-    gw(i_ks, "v")
-    send(lambda q: T.ks[:, 3 * q:3 * q + 3], T.kin[:, me, 0:3], "kin")
-    i_co = V(vec.tensor_scalar(T.co[:], T.mn[:, :, 0], float(S - 1), None, A.min))
+    i_co = V(vec.tensor_copy(T.co[quad(2, 2)], T.co[quad(0, 2)]))
 
-    vw(6, "gi")
-    vw(i_pll)
-    i = V(vec.tensor_copy(T.win_l[:, 0:SL].indirect(T.po_l[:, 0:8]), T.pl[:, 128:256]))
-    vw(i)
-    i = V(vec.transpose(T.t_l[:], T.win_l[:]))
-    vw(i)
-    i = V(vec.tensor_tensor(T.rsf[:], T.t_l[:, 1:SL:32], T.t_l[:, 17:SL:32], A.min))
-    vw(i)
-    V(vec.tensor_copy(T.rs[:, 0:24:2], T.rsf[:]))
-    i_rs = V(vec.tensor_copy(T.rs[:, 1:24:2], T.rsf[:]))
-    gw(i_rs, "v")
-    send(lambda q: T.rs[:, 3 * q - q % 2:3 * q - q % 2 + 4], T.rin[:, me, 0:4], "rin")
-
-    mine = slice(CAP * me, CAP * me + CAP)
-    aw(max(i_xq, i_co), "v")
-    a_pk = scales(T.pk_s[:, 0:SL], T.xs[:, 0:S], T.co[:, 0:24])
-    i_pk = codes(T.pk_q[:, 0:SL], T.xq[:, 0:S], T.co[:, 0:24])
-    gw(a_pk, "a")
-    send(lambda q: T.pk_s[:, CAP * q:CAP * q + CAP], T.in_s[:, mine], "s1")
+    vw(i_co)
+    aw(i_co, "v")
+    i_pk = codes(T.pk_q[:], T.xq[:, 0:S], T.co[:, 4:25])
+    a_pk = scales(T.pk_s[:], T.xs[:, 0:S], T.co[:, 4:25])
     gw(i_pk, "v")
-    send(lambda q: T.pk_q[:, CAP * q:CAP * q + CAP].bitcast(dt.uint8), T.in_q[:, mine].bitcast(dt.uint8), "q1")
+    send(lambda i: T.pk_q[:, part(i)].bitcast(dt.uint8), lambda i: T.in_q[:, slot(i)].bitcast(dt.uint8), "q1")
+    gw(a_pk, "a")
+    send(lambda i: T.pk_s[:, part(i)], lambda i: T.in_s[:, slot(i)], "s1")
 
-    i = V(vec.tensor_scalar(T.co_me[:, 0:3], T.mn[:, 3 * me:3 * me + 3, 0], float(S - 1), None, A.min))
-    V(vec.tensor_copy(T.kin[:, me, 0:3], T.ks[:, 3 * me:3 * me + 3]))
-    V(vec.tensor_copy(T.od[:], T.hh[:, 0:1]))
-    i_ev = V(vec.tensor_scalar(T.ev[:], T.hh[:, 0:1], -1.0, 1.0, A.mult, A.add))
-    vw(i_rs)
-    i_own = V(vec.tensor_copy(T.rin[:, me, 0:4], T.rs[:, 3 * me - me % 2:3 * me - me % 2 + 4]))
-    aw(max(i_ev, i_rkl), "v")
-    a_own = scales(T.in_s[:, mine], T.xs[:, 0:S], T.co_me[:, 0:3])
+    i_own = V(vec.tensor_copy(T.kr[:, 0, 0:3], three(me)))
+    i_own1 = codes(T.in_q[:, 0:64], T.xq[:, 0:S], T.co[:, 0:4])
+    a_own = scales(T.in_s[:, 0:64], T.xs[:, 0:S], T.co[:, 0:4])
+    i = V(vec.tensor_scalar(T.pob[:], T.po[:], float(-MID), None, A.add))
+    aw(a_ev)
+    aw(i, "v")
     for c0 in (0, 16):
-        C(act.activation(T.x2[:, c0:c0 + 16:2], T.rk_l[:, 7:64:8], COPY, scale=T.ev[:, 0:1]))
-        a_x2 = C(act.activation(T.x2[:, c0 + 1:c0 + 16:2], T.rk_l[:, 7:64:8], COPY, scale=T.od[:, 0:1]))
-    vw(i)
-    i_own1 = codes(T.in_q[:, mine], T.xq[:, 0:S], T.co_me[:, 0:3])
+        C(act.activation(T.x2[:, c0:c0 + 16:2], T.pob[:], F.Copy, scale=T.ev[:, 0:1]))
+        a_x2 = C(act.activation(T.x2[:, c0 + 1:c0 + 16:2], T.pob[:], F.Copy, scale=T.od[:, 0:1]))
 
-    vw(7, "gi")
     vw(a_tab, "a")
     vw(i_own)
-    vw(EACH, "kin")
-    i = V(vec.tensor_copy(T.kofs[:], T.kin[:, :, 0:3]))
+    vw(EACH, "kr")
+    for n_op, (bo, bi, n, j) in enumerate(kops):
+        i = V(vec.tensor_scalar(T.kofs[quad(bo, n)], T.kr[quad(bi, n), :, j], T.fd[quad(bi, n), n_op:n_op + 1], None, A.add))
+    V(vec.tensor_copy(T.rofs[quad(2, 2), 0:32:2], T.kr[quad(2, 2), :, 0:2]))
     vw(i)
-    i_tab = V(vec.tensor_copy(T.tab[:, 0:TAB].indirect(T.kofs[:, 0:24]), T.sv[:]))
-    vw(EACH, "rin")
-    i = V(vec.tensor_copy(T.rofs[:], T.rin[:, :, 0:4]))
+    V(vec.tensor_copy(T.tab[:, 0:2 * TAB].indirect(T.kofs[:, 0:8]), T.sv[:]))
+    V(vec.tensor_copy(T.rofs[quad(2, 2), 1:32:2], T.kr[quad(2, 2), :, 0:2]))
+    V(vec.tensor_copy(T.rofs[quad(0, 2), 0:32:2], T.kr[quad(2, 2), :, 0:2]))
+    i = V(vec.tensor_copy(T.rofs[quad(0, 2), 1:32:2], T.kr[quad(2, 2), :, 0:2]))
     aw(i, "v")
-    a_g = C(act.activation(T.d_s[:, RL // 2:RL], T.tab[:, 0:TAB].indirect(T.rofs[:, 16:32]), COPY))
+    a_g = C(act.activation(T.d_s[:, RL // 2:RL], T.tab[:, 0:TAB].indirect(T.rofs[:, 16:32]), F.Copy))
     vw(i)
     i = V(vec.tensor_copy(T.d_s[:, 0:RL // 2], T.tab[:, 0:TAB].indirect(T.rofs[:, 0:16])))
     vw(i)
@@ -268,33 +280,40 @@ def rank_program(g, core, T, topo):
     i = V(vec.transpose(T.t_s[:], T.d_s[:]))
     vw(i)
     m0 = 16 * (me % 2)
-    i_so = V(vec.tensor_scalar(T.so[:], T.t_s[:, :, m0:m0 + 48:16], float(HALF), None, A.add))
+    i = V(vec.tensor_tensor(T.mx1[quad(0, 2)], T.t_s[quad(0, 2), :, m0:m0 + 48:16], T.t_s[quad(2, 2), :, m0:m0 + 48:16], A.max))
+    vw(i)
+    for b in range(2):
+        i = V(vec.tensor_tensor(T.mx2[quad(b)], T.mx1[quad(0)], T.mx1[quad(1)], A.max))
+    vw(i)
+    for b in (0, 2):
+        i_so = V(vec.tensor_scalar(T.so[quad(b, 2), 1:25], T.mx2[quad(0, 2)], float(MID), None, A.add))
 
-    vw(i_so)
-    vw(a_own, "a")
+    vw(max(i_so, i_own1))
     vw(EACH, "q1")
-    aw(max(i_so, i_own1), "v")
+    aw(i_so, "v")
     aw(a_own)
     aw(EACH, "s1")
-    i_p2 = codes(T.p2_q[:, 0:SL], T.in_q[:, 0:SL], T.so[:, 0:24])
-    a_p2 = scales(T.p2_s[:, 0:SL], T.in_s[:, 0:SL], T.so[:, 0:24])
+    i_p2 = codes(T.p2_q[:], T.in_q[:, 0:LAND], T.so[:, 4:25])
+    a_p2 = scales(T.p2_s[:], T.in_s[:, 0:LAND], T.so[:, 4:25])
     gw(i_p2, "v")
-    send(lambda q: T.p2_q[:, CAP * q:CAP * q + CAP].bitcast(dt.uint8), T.bk_q[:, mine].bitcast(dt.uint8), "q2")
+    send(lambda i: T.p2_q[:, part(N - i)].bitcast(dt.uint8), lambda i: T.bk_q[:, slot(N - i)].bitcast(dt.uint8), "q2")
     gw(a_p2, "a")
-    send(lambda q: T.p2_s[:, CAP * q:CAP * q + CAP], T.bk_s[:, mine], "s2")
-    i_sm = V(vec.tensor_scalar(T.so_me[:, 0:3], T.t_s[:, me, m0:m0 + 48:16], float(HALF), None, A.add))
-    vw(i_sm)
-    i_own2 = codes(T.bk_q[:, mine], T.in_q[:, 0:SL], T.so_me[:, 0:3])
-    aw(i_sm, "v")
-    a_own2 = scales(T.bk_s[:, mine], T.in_s[:, 0:SL], T.so_me[:, 0:3])
-    vw(16, "ld_w")
-    V(vec.quantize_mx(T.wq[:], T.ws[:], T.wb[:]))
+    send(lambda i: T.p2_s[:, part(N - i)], lambda i: T.bk_s[:, slot(N - i)], "s2")
+    i_own2 = codes(T.bk_q[:, 0:64], T.in_q[:, 0:LAND], T.so[:, 0:4])
+    a_own2 = scales(T.bk_s[:, 0:64], T.in_s[:, 0:LAND], T.so[:, 0:4])
     vw(a_x2, "a")
     i = V(vec.transpose(T.x2t[:], T.x2[:]))
+    vw(16, "ld_w")
+    V(vec.quantize_mx(T.wq[:], T.ws[:], T.wb[:]))
     vw(i)
     i = V(vec.tensor_tensor(T.fof[:], T.x2t[:, 0:16], T.x2t[:, 16:32], A.add))
     vw(i)
-    i_fo = V(vec.tensor_scalar(T.fo[:], T.fof[:], float(HALF), None, A.add))
+    i = V(vec.tensor_scalar(T.fom[:], T.fof[:], float(CAP * me - MID), float(SL), A.is_lt, A.mult))
+    vw(i)
+    i = V(vec.tensor_tensor(T.fos[:], T.fof[:], T.fom[:], A.add))
+    vw(i)
+    for b in (0, 2):
+        i_fo = V(vec.tensor_scalar(T.fo[quad(b, 2)], T.fos[quad(2, 2)], float(MID + 16 - CAP * me), None, A.add))
 
     vw(max(i_own2, i_fo))
     vw(EACH, "q2")
@@ -305,7 +324,7 @@ def rank_program(g, core, T, topo):
     for f in range(2):
         c = slice(128 * f, 128 * f + 128)
         off = T.fo[:, 8 * f:8 * f + 8]
-        done.append((codes(T.fp_q[:, c], T.bk_q[:, 0:SL], off), scales(T.fp_s[:, c], T.bk_s[:, 0:SL], off)))
+        done.append((codes(T.fp_q[:, c], T.bk_q[:, 0:LAND], off), scales(T.fp_s[:, c], T.bk_s[:, 0:LAND], off)))
     for f in range(2):
         c = slice(128 * f, 128 * f + 128)
         W(ten, "t", "v", done[f][0])
@@ -318,7 +337,7 @@ def rank_program(g, core, T, topo):
         vw(O * f + 1, "t")
         iv = V(vec.tensor_copy(T.yb[:, 128 * f:128 * f + 128], T.ps[:, 1024 * f:1024 * f + 128]))
         aw(O * f + 2, "t")
-        ia = C(act.activation(T.yb[:, S + 128 * f:S + 128 * f + 128], T.ps[:, 1024 * f + 512:1024 * f + 640], COPY))
+        ia = C(act.activation(T.yb[:, S + 128 * f:S + 128 * f + 128], T.ps[:, 1024 * f + 512:1024 * f + 640], F.Copy))
     sw(iv, "v")
     syn.dma_start(T.y[:, 0:S], T.yb[:, 0:S]).then_inc(sem.st, 16)
     aw(ia)

@@ -9,29 +9,31 @@ LAND = SL + 16
 MID = LAND // 2
 TAB = K + 16 * N
 RL = N * 64
-F8, F32, BF, I32, U16 = "float8_e4m3fn_x4", "float32", "bfloat16", "int32", "uint16"
+FIRST = 4
+F8, F32, BF, F16, I32, U16 = "float8_e4m3fn_x4", "float32", "bfloat16", "float16", "int32", "uint16"
 
 SCRATCH = {
     "xb": ("sbuf", [128, 4 * S], BF), "wb": ("sbuf", [128, 512 * O], BF),
     "xq": ("sbuf", [128, S], F8), "xs": ("sbuf", [128, S], "uint8"),
     "wq": ("sbuf", [128, 128 * O], F8), "ws": ("sbuf", [128, 128 * O], "uint8"),
-    "kx": ("sbuf", [128, 32], I32), "ko": ("sbuf", [128, 32], I32), "kt": ("sbuf", [128, 32], I32),
+    "kt": ("sbuf", [128, 8], I32), "ko": ("sbuf", [128, 8], I32),
     "kf": ("sbuf", [128, 128], I32), "pl": ("sbuf", [128, 128], I32),
-    "pio": ("sbuf", [128, 4], I32), "lane": ("sbuf", [128, 1], I32), "hh": ("sbuf", [128, 1], I32),
-    "two": ("sbuf", [128, 4], F32), "cq": ("sbuf", [128, 64], F32), "m64": ("sbuf", [128, 64], F32),
-    "lanef": ("sbuf", [128, 1], F32), "h3": ("sbuf", [128, 1], F32), "c64": ("sbuf", [128, 4], U16),
-    "ev": ("sbuf", [128, 1], F32), "od": ("sbuf", [128, 1], F32), "eb": ("sbuf", [128, 1], F32),
-    "tent": ("sbuf", [128, 1], F32), "ini": ("sbuf", [128, 1], F32), "fd": ("sbuf", [128, 4], F32),
+    "pio": ("sbuf", [128, 1], I32), "lane": ("sbuf", [128, 1], I32), "hh": ("sbuf", [128, 1], I32),
+    "cq0": ("sbuf", [128, 64], F32), "cqn": ("sbuf", [128, 64], F32), "cq": ("sbuf", [128, 64], F32),
+    "lanef": ("sbuf", [128, 1], F32), "lane8": ("sbuf", [128, 1], F32), "h3": ("sbuf", [128, 1], F32), "nh3": ("sbuf", [128, 1], F32),
+    "c64": ("sbuf", [128, 4], U16), "turn": ("sbuf", [128, 8], U16),
+    "od": ("sbuf", [128, 1], F32), "eb": ("sbuf", [128, 1], F32),
+    "tb": ("sbuf", [128, 1], F32), "ini": ("sbuf", [128, 1], F32), "fd": ("sbuf", [128, 4], F32),
     "cv": ("sbuf", [128, 2], F32), "cm": ("sbuf", [128, 2], F32), "cw": ("sbuf", [128, 2], F32), "cot": ("sbuf", [128, 2], U16),
     "zz": ("sbuf", [128, TAB // 4], BF), "sv0": ("sbuf", [128, 128], F32), "sv": ("sbuf", [128, 128], BF),
     "e": ("sbuf", [128, 128], BF), "ef": ("sbuf", [128, 128], BF), "cu": ("sbuf", [128, 128], BF),
-    "ct": ("sbuf", [128, 128], BF), "pr": ("sbuf", [128, 64], F32), "rk": ("sbuf", [128, 64], F32),
-    "tb": ("sbuf", [128, 1], F32), "pob": ("sbuf", [128, 8], BF),
+    "ct": ("sbuf", [128, 128], BF), "big": ("sbuf", [128, 64], BF), "rk": ("sbuf", [128, 64], BF),
     "po": ("sbuf", [128, 8], U16), "win": ("sbuf", [128, WIN], F32), "tw": ("sbuf", [128, NB, 32], F32),
-    "ab": ("sbuf", [128, 16], F32), "z": ("sbuf", [128, 32], F32), "co": ("sbuf", [128, 32], U16),
-    "x2": ("sbuf", [128, 32], BF), "x2t": ("sbuf", [128, 32], BF), "fof": ("sbuf", [128, 16], F32),
+    "ab": ("sbuf", [128, NB, 2], F16), "z": ("sbuf", [128, 32], F32), "co": ("sbuf", [128, 32], U16),
+    "x2": ("sbuf", [128, 32], BF), "x2t": ("sbuf", [128, 32], BF), "xa": ("sbuf", [128, 16], BF), "xc": ("sbuf", [128, 16], BF),
+    "x3": ("sbuf", [128, 32], BF), "x3t": ("sbuf", [128, 32], BF),
     "fom": ("sbuf", [128, 16], F32), "fos": ("sbuf", [128, 16], F32), "fo": ("sbuf", [128, 16], U16),
-    "kr": ("sbuf", [128, N, 4], F32), "kofs": ("sbuf", [128, 8], U16), "rofs": ("sbuf", [128, 32], U16),
+    "kr": ("sbuf", [128, N, 8], F16), "kofs": ("sbuf", [128, 8], U16), "rofs": ("sbuf", [128, 32], U16),
     "tab": ("sbuf", [128, 2 * TAB], BF), "d_s": ("sbuf", [128, RL], BF), "t_s": ("sbuf", [128, 8, 64], BF),
     "mx1": ("sbuf", [128, 24], F32), "mx2": ("sbuf", [128, 24], F32), "so": ("sbuf", [128, 26], U16),
     "pk_q": ("sbuf", [128, SL - CAP], F8), "pk_s": ("sbuf", [128, SL - CAP], "uint8"),
@@ -51,7 +53,7 @@ def rank_program(g, core, T, topo):
     A = AluOpType
     F = ActivationFunctionType
     vec, act, ten, syn, sem = g.vector, g.scalar, g.tensor, g.sync, T.sem
-    nv, na, sent, seen = [0], [0], [0], {}
+    nv, na, sent, seen, lands = [0], [0], [0], {}, {}
 
     def V(ins):
         ins.then_inc(sem.v, 1)
@@ -83,26 +85,41 @@ def rank_program(g, core, T, topo):
     def quad(b, n=1):
         return slice(32 * b, 32 * (b + n))
 
-    near, far = 0, 0
-    dests = []
-    for i in range(1, N):
-        q = (me + i) % N
-        dst = T.cores[q]
-        eng = topo.engines(core, dst)
-        if topo.die(dst) == topo.die(core):
-            pick = eng[0::2][2 * near:2 * near + 2]
-            near += 1
-        else:
-            pick = eng[1::2][2 * far:2 * far + 2]
-            far += 1
-        rid, pid, _ = topo.addr(dst)
-        dests.append((i, DstId(rid=rid, pnc=pid), sum(1 << e for e in pick)))
-    EACH = 2 * (N - 1)
+    def same_die(a, b):
+        return topo.die(T.cores[a]) == topo.die(T.cores[b])
 
-    def send(src, dst, s):
-        g.remote_dma_fused([RemoteDMATransfer(dst_ids=[d], dma_engine_mask=m, remote_sem=sem[s], src=src(i), dst=dst(i))
-                            for i, d, m in dests], local_sem=sem.out)
-        sent[0] += EACH
+    def order(a):
+        near = [(a + i) % N for i in range(1, N) if same_die(a, (a + i) % N)]
+        far = [(a + i) % N for i in range(1, N) if not same_die(a, (a + i) % N)]
+        return far[:FIRST // 2] + near[:FIRST // 2] + far[FIRST // 2:] + near[FIRST // 2:]
+
+    def masks(a, ranks, most):
+        out = {}
+        for near in (True, False):
+            qs = [q for q in ranks if same_die(a, q) == near]
+            if not qs:
+                continue
+            free = topo.engines(T.cores[a], T.cores[qs[0]])[0 if near else 1::2]
+            n = most
+            while n * len(qs) > len(free):
+                n //= 2
+            spare = len(free) - n * len(qs)
+            for q in qs:
+                k = 2 * n if 2 * n <= most and spare >= n else n
+                spare -= k - n
+                out[q], free = free[:k], free[k:]
+        return out
+
+    def send(ranks, most, src, dst, s):
+        ms = masks(me, ranks(me), most)
+        g.remote_dma_fused([RemoteDMATransfer(dst_ids=[DstId(rid=topo.addr(T.cores[q])[0], pnc=topo.addr(T.cores[q])[1])],
+                                              dma_engine_mask=sum(1 << e for e in ms[q]), remote_sem=sem[s], src=src(q), dst=dst(q))
+                            for q in ranks(me)], local_sem=sem.out)
+        sent[0] += sum(len(m) for m in ms.values())
+        lands[s] = lands.get(s, 0) + sum(len(masks(a, ranks(a), most)[me]) for a in range(N) if me in ranks(a))
+
+    def at(q):
+        return order(q).index(me) + 1
 
     def codes(out, win, off):
         return V(vec.tensor_copy(out.bitcast(dt.uint32), win.bitcast(dt.uint32).indirect(off)))
@@ -119,57 +136,55 @@ def rank_program(g, core, T, topo):
     def iota(ap, pattern, base, cm=0, small=True):
         (g.iota(ap, pattern, base, cm, allow_small_or_imprecise_dtypes=True) if small else g.iota(ap, pattern, base, cm)).then_inc(sem.gi, 1)
 
-    i_kx = V(vec.memset(T.kx[:], 0))
-    iota(T.kf[:], [[16, 8], [128, 16]], -8, 1, small=False)
-    iota(T.pio[:], [[0, 4]], 0, 1, small=False)
-    iota(T.two[:], [[2, 4]], 0)
-    iota(T.cq[:], [[0, 8], [1, 8]], 0)
+    for b in range(4):
+        (syn if b < 2 else act).dma_start(T.kt[quad(b)], (T.ky if b < 2 else T.lk)[:]).then_inc(sem.ld_t, 16)
+    iota(T.kf[:], [[8, 8], [1024, 2], [128, 8]], 0, 4, small=False)
+    iota(T.pio[:], [[0, 1]], 0, 1, small=False)
+    iota(T.cq0[:], [[0, 4], [1 - N, 2], [1, 8]], 0)
     iota(T.win[:], [[0, WIN // 16], [1, 16]], K + 16 * me)
     iota(T.sv0[:], [[CAP, 8], [1, 16]], 16 - MID, 1)
-    G_KF, G_P, G_TWO, G_CQ, G_WIN, G_SV = range(1, 7)
-    i_zz = V(vec.memset(T.zz[:], 0.0))
+    G_KF, G_P, G_CQ, G_WIN, G_SV = range(1, 6)
     V(vec.memset(T.e[:], 0.0))
+    i_zz = V(vec.memset(T.zz[:], 0.0))
     V(vec.memset(T.z[:], 0.0))
     V(vec.memset(T.so[:], 0))
+    V(vec.memset(T.x2[:], 0.0))
     vw(G_KF, "gi")
-    i_kf = V(vec.tensor_copy(T.kf[quad(1)], T.kf[quad(0)]))
-    sw(i_kx, "v")
-    aw(i_kx, "v")
-    for b in range(4):
-        (syn if b < 2 else act).dma_start(T.kx[32 * b:32 * b + 8, :], (T.ky if b < 2 else T.lk)[:]).then_inc(sem.ld_t, 16)
+    i_kf = V(vec.tensor_scalar(T.kf[quad(1)], T.kf[quad(1)], -128.0, None, A.add))
     aw(G_KF, "gi")
-    sw(i_kf, "v")
+    sw(G_KF, "gi")
     for b in range(4):
+        if b == 1:
+            sw(i_kf, "v")
         for h in range(2):
-            p = 32 * b + 8 * h + 9
-            (syn if b < 2 else act).dma_start(T.kf[p:p + 1, :], (T.ky if b < 2 else T.lk)[h:16:2, :]).then_inc(sem.ld_f, 16)
-    act.dma_start(T.xb[:], T.x[:]).then_inc(sem.ld_x, 16)
+            p = 32 * b + 16 * h + 1
+            (syn if b < 2 else act).dma_start(T.kf[p:p + 1, :], (T.ky if b < 2 else T.lk)[8 * h:8 * h + 8, :]).then_inc(sem.ld_f, 16)
+    syn.dma_start(T.xb[:], T.x[:]).then_inc(sem.ld_x, 16)
     syn.dma_start(T.wb[:], T.w[:]).then_inc(sem.ld_w, 16)
 
     vw(G_P, "gi")
-    V(vec.tensor_scalar(T.lane[:], T.pio[:, 0:1], 15, None, A.bitwise_and))
-    i = V(vec.tensor_scalar(T.hh[:], T.pio[:, 0:1], 4, 1, A.logical_shift_right, A.bitwise_and))
+    V(vec.tensor_scalar(T.lane[:], T.pio[:], 15, None, A.bitwise_and))
+    i = V(vec.tensor_scalar(T.hh[:], T.pio[:], 4, 1, A.logical_shift_right, A.bitwise_and))
     vw(i)
     V(vec.tensor_copy(T.lanef[:], T.lane[:]))
     i_od = V(vec.tensor_copy(T.od[:], T.hh[:]))
-    i = V(vec.tensor_scalar(T.h3[:], T.lane[:], 8.0, None, A.is_ge))
+    V(vec.tensor_scalar(T.h3[:], T.lane[:], 8.0, None, A.is_ge))
+    i = V(vec.tensor_scalar(T.lane8[:], T.lane[:], 8.0, None, A.mult))
+    vw(G_CQ, "gi")
+    i_cq = V(vec.tensor_scalar(T.cqn[:], T.cq0[:], -1.0, None, A.mult))
     vw(i)
-    vw(G_TWO, "gi")
-    i_c64 = V(vec.tensor_scalar(T.c64[:], T.two[:], T.h3[:, 0:1], None, A.add))
-    i_cv = V(vec.tensor_scalar(T.cv[:], T.two[:, 0:2], 8.0, T.lanef[:, 0:1], A.mult, A.add))
+    V(vec.tensor_scalar(T.c64[:], T.cq0[:, 0:8:2], T.h3[:, 0:1], None, A.add))
+    vw(i_cq)
+    V(vec.tensor_tensor(T.cq[:], T.cq0[:], T.cqn[:], A.max))
+    V(vec.tensor_scalar(T.turn[:], T.cq0[:, 0:8], T.lane8[:, 0:1], None, A.add))
+    i_cv = V(vec.tensor_scalar(T.cv[:], T.cq0[:, 0:2], 16.0, T.lanef[:, 0:1], A.mult, A.add))
     aw(i_od, "v")
-    top = (SL - CAP - 1) / 2
     for b, n, sh in ((0, 1, 0), (1, 1, 16), (2, 2, 0)):
-        i = C(act.activation(T.tb[quad(b, n)], T.od[quad(b, n)], F.Identity, bias=float(sh - MID - 1 - top), scale=float(SL)))
-    aw(i)
-    i = C(act.activation(T.tent[:], T.lanef[:], F.Abs, bias=T.tb[:, 0:1], scale=float(CAP // 2)))
+        i = C(act.activation(T.tb[quad(b, n)], T.od[quad(b, n)], F.Identity, bias=float(sh - MID - 1), scale=float(2 * MID - 2 * sh - SL + 1)))
     for b, n, sh in ((0, 1, 0), (1, 1, 1), (2, 2, 0)):
-        a_eb = C(act.activation(T.eb[quad(b, n)], T.od[quad(b, n)], F.Identity, bias=float(1 + sh), scale=-1.0))
+        C(act.activation(T.eb[quad(b, n)], T.od[quad(b, n)], F.Identity, bias=float(1 + sh), scale=-1.0))
     aw(i)
-    a_ini = C(act.activation(T.ini[:], T.tent[:], F.Identity, bias=float(top), scale=-1.0))
-    aw(G_CQ, "gi")
-    a_m64 = C(act.activation(T.m64[:], T.cq[:], F.Sign))
-    a_ev = C(act.activation(T.ev[:], T.od[:], F.Identity, bias=1.0, scale=-1.0))
+    a_ini = C(act.activation(T.ini[:], T.lanef[:], F.Identity, bias=T.tb[:, 0:1], scale=float(CAP // 2)))
     kops = [(0, 0, 2, 1), (2, 0, 2, 0)] if me % 2 == 0 else [(0, 0, 2, 1), (2, 0, 1, 0), (3, 1, 1, 2)]
     third = {}
     for n_op, (bo, bi, n, j) in enumerate(kops):
@@ -189,32 +204,32 @@ def rank_program(g, core, T, topo):
         a_tab = C(act.activation(T.sv[quad(b)], T.sv0[quad(b)], F.Identity, bias=float(16 * u - 32 * b - 16 * h)))
 
     vw(64, "ld_t")
-    i = V(vec.tensor_scalar(T.ko[:], T.kx[:], N - 1, None, A.bitwise_and))
-    vw(i)
-    i = V(vec.transpose(T.kt[:], T.ko[:]))
+    i = V(vec.tensor_scalar(T.ko[:], T.kt[:], N - 1, None, A.bitwise_and))
+    vw(i_cv)
     i_cm = V(vec.tensor_scalar(T.cm[:], T.cv[:], float(25 - 3 * me), -24.0, A.is_ge, A.mult))
     vw(i)
-    vw(G_CQ, "gi")
-    i = V(vec.tensor_tensor(T.e[:, 0:128:2], T.kt[:, 0:8].indirect(T.c64[:, 0:4]), T.cq[:], A.is_equal))
+    i = V(vec.tensor_tensor(T.e[:, 0:128:2], T.ko[:, 0:8].indirect(T.c64[:, 0:4]), T.cq[:], A.is_equal))
     vw(i_cm)
-    i_cw = V(vec.tensor_tensor(T.cw[:], T.cv[:], T.cm[:], A.add))
+    V(vec.tensor_tensor(T.cw[:], T.cv[:], T.cm[:], A.add))
     vw(i)
     i = V(vec.transpose(T.ef[:], T.e[:]))
-    vw(i_cw)
-    vw(a_eb, "a")
-    V(vec.tensor_scalar(T.cot[:], T.cw[:], T.eb[:, 0:1], float(3 * me - 1), A.add, A.add))
+    V(vec.tensor_scalar(T.big[:], T.e[:, 0:128:2], 512.0, None, A.mult))
     vw(i)
     vw(a_ini, "a")
     i = V(vec.tensor_tensor_scan(T.cu[:], T.ef[:], T.zz[:, 0:128], T.ini[:, 0:1], A.add, A.add))
+    V(vec.tensor_scalar(T.cot[:], T.cw[:], T.eb[:, 0:1], float(3 * me - 1), A.add, A.add))
+    V(vec.tensor_scalar(T.nh3[:], T.lane[:], 8.0, None, A.is_lt))
     vw(i)
     i = V(vec.transpose(T.ct[:], T.cu[:]))
-    vw(i)
-    i = V(vec.tensor_tensor(T.pr[:], T.e[:, 0:128:2], T.ct[:, 0:128:2], A.mult))
     vw(128, "ld_f")
-    V(vec.tensor_scalar(T.pl[:], T.kf[:], 3, K - 1, A.logical_shift_right, A.bitwise_and))
+
+    def places(f):
+        V(vec.tensor_scalar(T.pl[:, 64 * f:64 * f + 64], T.kf[:, 0:128].indirect(T.turn[:, 4 * f:4 * f + 4]), 3, K - 1,
+                            A.logical_shift_right, A.bitwise_and))
+    places(0)
     vw(i)
-    vw(a_m64, "a")
-    i = V(vec.tensor_tensor_scan(T.rk[:], T.m64[:], T.pr[:], 0.0, A.mult, A.add))
+    i = V(vec.tensor_tensor_scan(T.rk[:], T.big[:], T.ct[:, 0:128:2], 0.0, A.add, A.min))
+    places(1)
     vw(i)
     V(vec.tensor_scalar(T.po[:, 0:8:2], T.rk[:, 7:64:16], float(MID), None, A.add))
     i = V(vec.tensor_scalar(T.po[:, 1:8:2], T.rk[:, 15:64:16], -1.0, float(MID), A.mult, A.add))
@@ -222,17 +237,22 @@ def rank_program(g, core, T, topo):
     vw(i)
     vw(G_WIN, "gi")
     i = V(vec.tensor_copy(T.win[:, 0:WIN].indirect(T.po[:, 0:8]), T.pl[:]))
+    for c0 in (0, 8):
+        i_x2 = V(vec.tensor_scalar(T.x2[:, c0:c0 + 8], T.po[:], float(-MID), None, A.add))
     vw(i)
     i = V(vec.transpose(T.tw[:], T.win[:]))
+    vw(i_x2)
+    V(vec.transpose(T.x2t[:], T.x2[:]))
     vw(i)
-    i_ab = V(vec.tensor_tensor(T.ab[:, 0:NB], T.tw[:, :, 9], T.tw[:, :, 17], A.min))
+    for d in range(2):
+        i_ab = V(vec.tensor_tensor(T.ab[:, :, d], T.tw[:, :, 1], T.tw[:, :, 17], A.min))
 
     def three(q):
-        return T.ab[:, 3 * q // 2:3 * q // 2 + 3]
+        return T.ab[:, 3 * q // 2:3 * q // 2 + 3, :]
     gw(i_ab, "v")
-    send(lambda i: three((me + i) % N), lambda i: T.kr[:, i, 0:3], "kr")
+    send(order, 2, three, lambda q: T.kr[:, at(q), 0:6], "kr")
     for po, c0, pi in ((quad(0, 2), 1, quad(0, 2)), (quad(0), 0, quad(1)), (quad(1), 2, quad(0))):
-        i = V(vec.tensor_tensor(T.z[po, c0:c0 + 2 * NB:2], T.tw[pi, :, 8], T.tw[pi, :, 16], A.min))
+        i = V(vec.tensor_tensor(T.z[po, c0:c0 + 2 * NB:2], T.tw[pi, :, 0], T.tw[pi, :, 16], A.min))
     vw(16, "ld_x")
     V(vec.quantize_mx(T.xq[:, 0:128], T.xs[:, 0:128], T.xb[:, 0:512]))
     vw(i)
@@ -246,35 +266,31 @@ def rank_program(g, core, T, topo):
     i_pk = codes(T.pk_q[:], T.xq[:, 0:S], T.co[:, 4:25])
     a_pk = scales(T.pk_s[:], T.xs[:, 0:S], T.co[:, 4:25])
     gw(i_pk, "v")
-    send(lambda i: T.pk_q[:, part(i)].bitcast(dt.uint8), lambda i: T.in_q[:, slot(i)].bitcast(dt.uint8), "q1")
+    send(order, 4, lambda q: T.pk_q[:, part((q - me) % N)].bitcast(dt.uint8), lambda q: T.in_q[:, slot(at(q))].bitcast(dt.uint8), "q1")
     gw(a_pk, "a")
-    send(lambda i: T.pk_s[:, part(i)], lambda i: T.in_s[:, slot(i)], "s1")
+    send(order, 4, lambda q: T.pk_s[:, part((q - me) % N)], lambda q: T.in_s[:, slot(at(q))], "s1")
 
-    i_own = V(vec.tensor_copy(T.kr[:, 0, 0:3], three(me)))
+    i_own = V(vec.tensor_copy(T.kr[:, 0, 0:6], three(me)))
     i_own1 = codes(T.in_q[:, 0:64], T.xq[:, 0:S], T.co[:, 0:4])
     a_own = scales(T.in_s[:, 0:64], T.xs[:, 0:S], T.co[:, 0:4])
-    i = V(vec.tensor_scalar(T.pob[:], T.po[:], float(-MID), None, A.add))
-    aw(a_ev)
-    aw(i, "v")
-    for c0 in (0, 16):
-        C(act.activation(T.x2[:, c0:c0 + 16:2], T.pob[:], F.Copy, scale=T.ev[:, 0:1]))
-        a_x2 = C(act.activation(T.x2[:, c0 + 1:c0 + 16:2], T.pob[:], F.Copy, scale=T.od[:, 0:1]))
+    V(vec.tensor_scalar(T.xa[:], T.x2t[:, 0:32:2], T.nh3[:, 0:1], None, A.mult))
+    V(vec.tensor_scalar(T.xc[:], T.x2t[:, 1:32:2], T.h3[:, 0:1], None, A.mult))
 
     vw(a_tab, "a")
     vw(i_own)
-    vw(EACH, "kr")
+    vw(lands["kr"], "kr")
     for n_op, (bo, bi, n, j) in enumerate(kops):
-        i = V(vec.tensor_scalar(T.kofs[quad(bo, n)], T.kr[quad(bi, n), :, j], T.fd[quad(bi, n), n_op:n_op + 1], None, A.add))
-    V(vec.tensor_copy(T.rofs[quad(2, 2), 0:32:2], T.kr[quad(2, 2), :, 0:2]))
+        i = V(vec.tensor_scalar(T.kofs[quad(bo, n)], T.kr[quad(bi, n), :, 2 * j], T.fd[quad(bi, n), n_op:n_op + 1], None, A.add))
+    for b in (0, 2):
+        V(vec.tensor_copy(T.rofs[quad(b, 2)], T.kr[quad(2, 2), :, 0:4]))
     vw(i)
-    V(vec.tensor_copy(T.tab[:, 0:2 * TAB].indirect(T.kofs[:, 0:8]), T.sv[:]))
-    V(vec.tensor_copy(T.rofs[quad(2, 2), 1:32:2], T.kr[quad(2, 2), :, 0:2]))
-    V(vec.tensor_copy(T.rofs[quad(0, 2), 0:32:2], T.kr[quad(2, 2), :, 0:2]))
-    i = V(vec.tensor_copy(T.rofs[quad(0, 2), 1:32:2], T.kr[quad(2, 2), :, 0:2]))
+    i = V(vec.tensor_copy(T.tab[:, 0:2 * TAB].indirect(T.kofs[:, 0:8]), T.sv[:]))
     aw(i, "v")
     a_g = C(act.activation(T.d_s[:, RL // 2:RL], T.tab[:, 0:TAB].indirect(T.rofs[:, 16:32]), F.Copy))
+    V(vec.tensor_tensor(T.x3[:, 0:16], T.xa[:], T.xc[:], A.add))
     vw(i)
     i = V(vec.tensor_copy(T.d_s[:, 0:RL // 2], T.tab[:, 0:TAB].indirect(T.rofs[:, 0:16])))
+    V(vec.tensor_tensor(T.x3[:, 16:32], T.xa[:], T.xc[:], A.add))
     vw(i)
     vw(a_g, "a")
     i = V(vec.transpose(T.t_s[:], T.d_s[:]))
@@ -289,37 +305,42 @@ def rank_program(g, core, T, topo):
         i_so = V(vec.tensor_scalar(T.so[quad(b, 2), 1:25], T.mx2[quad(0, 2)], float(MID), None, A.add))
 
     vw(max(i_so, i_own1))
-    vw(EACH, "q1")
+    vw(lands["q1"], "q1")
     aw(i_so, "v")
     aw(a_own)
-    aw(EACH, "s1")
-    i_p2 = codes(T.p2_q[:], T.in_q[:, 0:LAND], T.so[:, 4:25])
-    a_p2 = scales(T.p2_s[:], T.in_s[:, 0:LAND], T.so[:, 4:25])
-    gw(i_p2, "v")
-    send(lambda i: T.p2_q[:, part(N - i)].bitcast(dt.uint8), lambda i: T.bk_q[:, slot(N - i)].bitcast(dt.uint8), "q2")
+    aw(lands["s1"], "s1")
+
+    def answer(buf, r):
+        return buf[:, part(order(me).index(r) + 1)]
+
+    def back(buf, r):
+        return buf[:, slot((me - r) % N)]
+    for k0, k1 in ((0, FIRST), (FIRST, N - 1)):
+        off = T.so[:, 4 + 3 * k0:4 + 3 * k1]
+        i_p2 = codes(T.p2_q[:, CAP * k0:CAP * k1], T.in_q[:, 0:LAND], off)
+        a_p2 = scales(T.p2_s[:, CAP * k0:CAP * k1], T.in_s[:, 0:LAND], off)
+        gw(i_p2, "v")
+        send(lambda a: order(a)[k0:k1], 4, lambda r: answer(T.p2_q, r).bitcast(dt.uint8), lambda r: back(T.bk_q, r).bitcast(dt.uint8), "q2")
     gw(a_p2, "a")
-    send(lambda i: T.p2_s[:, part(N - i)], lambda i: T.bk_s[:, slot(N - i)], "s2")
+    send(order, 4, lambda r: answer(T.p2_s, r), lambda r: back(T.bk_s, r), "s2")
     i_own2 = codes(T.bk_q[:, 0:64], T.in_q[:, 0:LAND], T.so[:, 0:4])
     a_own2 = scales(T.bk_s[:, 0:64], T.in_s[:, 0:LAND], T.so[:, 0:4])
-    vw(a_x2, "a")
-    i = V(vec.transpose(T.x2t[:], T.x2[:]))
+    i = V(vec.transpose(T.x3t[:], T.x3[:]))
     vw(16, "ld_w")
     V(vec.quantize_mx(T.wq[:], T.ws[:], T.wb[:]))
     vw(i)
-    i = V(vec.tensor_tensor(T.fof[:], T.x2t[:, 0:16], T.x2t[:, 16:32], A.add))
+    i = V(vec.tensor_scalar(T.fom[:], T.x3t[:, 0:16], float(CAP * me - MID), float(SL), A.is_lt, A.mult))
     vw(i)
-    i = V(vec.tensor_scalar(T.fom[:], T.fof[:], float(CAP * me - MID), float(SL), A.is_lt, A.mult))
-    vw(i)
-    i = V(vec.tensor_tensor(T.fos[:], T.fof[:], T.fom[:], A.add))
+    i = V(vec.tensor_tensor(T.fos[:], T.x3t[:, 0:16], T.fom[:], A.add))
     vw(i)
     for b in (0, 2):
         i_fo = V(vec.tensor_scalar(T.fo[quad(b, 2)], T.fos[quad(2, 2)], float(MID + 16 - CAP * me), None, A.add))
 
     vw(max(i_own2, i_fo))
-    vw(EACH, "q2")
+    vw(lands["q2"], "q2")
     aw(i_fo, "v")
     aw(a_own2)
-    aw(EACH, "s2")
+    aw(lands["s2"], "s2")
     done = []
     for f in range(2):
         c = slice(128 * f, 128 * f + 128)

@@ -8,7 +8,7 @@ NB = WIN // 32
 LAND = SL + 16
 MID = LAND // 2
 TAB = K + 16 * N
-RL = N * 64
+RL = N * 32
 FIRST = 4
 F8, F32, BF, F16, I32, U16 = "float8_e4m3fn_x4", "float32", "bfloat16", "float16", "int32", "uint16"
 
@@ -17,10 +17,12 @@ SCRATCH = {
     "xq": ("sbuf", [128, S], F8), "xs": ("sbuf", [128, S], "uint8"),
     "wq": ("sbuf", [128, 128 * O], F8), "ws": ("sbuf", [128, 128 * O], "uint8"),
     "kt": ("sbuf", [128, 8], I32), "ko": ("sbuf", [128, 8], I32),
-    "kf": ("sbuf", [128, 128], I32), "pl": ("sbuf", [128, 128], I32),
+    "kf": ("sbuf", [128, 128], I32), "kp": ("sbuf", [128, 128], I32), "pl": ("sbuf", [128, 128], F32),
+    "cc0": ("sbuf", [128, 128], F32), "cc": ("sbuf", [128, 128], F32),
+    "b8": ("sbuf", [128, 1], F32), "od8": ("sbuf", [128, 1], F32),
     "pio": ("sbuf", [128, 1], I32), "lane": ("sbuf", [128, 1], I32), "hh": ("sbuf", [128, 1], I32),
     "cq0": ("sbuf", [128, 64], F32), "cqn": ("sbuf", [128, 64], F32), "cq": ("sbuf", [128, 64], F32),
-    "lanef": ("sbuf", [128, 1], F32), "lane8": ("sbuf", [128, 1], F32), "h3": ("sbuf", [128, 1], F32), "nh3": ("sbuf", [128, 1], F32),
+    "lanef": ("sbuf", [128, 1], F32), "lane8": ("sbuf", [128, 1], F32), "h3": ("sbuf", [128, 1], F32),
     "c64": ("sbuf", [128, 4], U16), "turn": ("sbuf", [128, 8], U16),
     "od": ("sbuf", [128, 1], F32), "eb": ("sbuf", [128, 1], F32),
     "tb": ("sbuf", [128, 1], F32), "ini": ("sbuf", [128, 1], F32), "fd": ("sbuf", [128, 4], F32),
@@ -29,13 +31,14 @@ SCRATCH = {
     "e": ("sbuf", [128, 128], BF), "ef": ("sbuf", [128, 128], BF), "cu": ("sbuf", [128, 128], BF),
     "ct": ("sbuf", [128, 128], BF), "big": ("sbuf", [128, 64], BF), "rk": ("sbuf", [128, 64], BF),
     "po": ("sbuf", [128, 8], U16), "win": ("sbuf", [128, WIN], F32), "tw": ("sbuf", [128, NB, 32], F32),
-    "ab": ("sbuf", [128, NB, 2], F16), "z": ("sbuf", [128, 32], F32), "co": ("sbuf", [128, 32], U16),
-    "x2": ("sbuf", [128, 32], BF), "x2t": ("sbuf", [128, 32], BF), "xa": ("sbuf", [128, 16], BF), "xc": ("sbuf", [128, 16], BF),
-    "x3": ("sbuf", [128, 32], BF), "x3t": ("sbuf", [128, 32], BF),
+    "c3": ("sbuf", [128, 2], I32), "c4": ("sbuf", [128, 2], F32), "ev2": ("sbuf", [128, 1], F32), "sot": ("sbuf", [128, 2], U16),
+    "ab": ("sbuf", [128, 16], F16), "z": ("sbuf", [128, 32], F32), "co": ("sbuf", [128, 32], U16),
+    "x2": ("sbuf", [128, 32], BF), "x2t": ("sbuf", [128, 32], BF), "l2": ("sbuf", [128, 1], F32), "fot": ("sbuf", [128, 2], U16),
+    "x3": ("sbuf", [128, 32], BF), "x3t": ("sbuf", [128, 2, 16], BF),
     "fom": ("sbuf", [128, 16], F32), "fos": ("sbuf", [128, 16], F32), "fo": ("sbuf", [128, 16], U16),
-    "kr": ("sbuf", [128, N, 8], F16), "kofs": ("sbuf", [128, 8], U16), "rofs": ("sbuf", [128, 32], U16),
-    "tab": ("sbuf", [128, 2 * TAB], BF), "d_s": ("sbuf", [128, RL], BF), "t_s": ("sbuf", [128, 8, 64], BF),
-    "mx1": ("sbuf", [128, 24], F32), "mx2": ("sbuf", [128, 24], F32), "so": ("sbuf", [128, 26], U16),
+    "kr": ("sbuf", [128, N, 8], F16), "kofs": ("sbuf", [128, 8], U16), "rofs": ("sbuf", [128, 16], U16),
+    "tab": ("sbuf", [128, 2 * TAB], BF), "d_s": ("sbuf", [128, RL + 32], BF), "t_s": ("sbuf", [128, 2 * N + 2, 32], BF),
+    "mx1": ("sbuf", [128, 4 * N + 2], F32), "mx2": ("sbuf", [128, 48], F32), "so": ("sbuf", [128, 32], U16),
     "pk_q": ("sbuf", [128, SL - CAP], F8), "pk_s": ("sbuf", [128, SL - CAP], "uint8"),
     "in_q": ("sbuf", [128, LAND], F8), "in_s": ("sbuf", [128, LAND], "uint8"),
     "p2_q": ("sbuf", [128, SL - CAP], F8), "p2_s": ("sbuf", [128, SL - CAP], "uint8"),
@@ -91,15 +94,15 @@ def rank_program(g, core, T, topo):
     def order(a):
         near = [(a + i) % N for i in range(1, N) if same_die(a, (a + i) % N)]
         far = [(a + i) % N for i in range(1, N) if not same_die(a, (a + i) % N)]
-        return far[:FIRST // 2] + near[:FIRST // 2] + far[FIRST // 2:] + near[FIRST // 2:]
+        return far[:1] + near[:1] + far[1:2] + near[1:2] + far[2:] + near[2:]
 
-    def masks(a, ranks, most):
+    def masks(a, ranks, most, swap):
         out = {}
         for near in (True, False):
             qs = [q for q in ranks if same_die(a, q) == near]
             if not qs:
                 continue
-            free = topo.engines(T.cores[a], T.cores[qs[0]])[0 if near else 1::2]
+            free = topo.engines(T.cores[a], T.cores[qs[0]])[0 if near != swap else 1::2]
             n = most
             while n * len(qs) > len(free):
                 n //= 2
@@ -110,13 +113,13 @@ def rank_program(g, core, T, topo):
                 out[q], free = free[:k], free[k:]
         return out
 
-    def send(ranks, most, src, dst, s):
-        ms = masks(me, ranks(me), most)
+    def send(ranks, most, src, dst, s, swap=False):
+        ms = masks(me, ranks(me), most, swap)
         g.remote_dma_fused([RemoteDMATransfer(dst_ids=[DstId(rid=topo.addr(T.cores[q])[0], pnc=topo.addr(T.cores[q])[1])],
                                               dma_engine_mask=sum(1 << e for e in ms[q]), remote_sem=sem[s], src=src(q), dst=dst(q))
                             for q in ranks(me)], local_sem=sem.out)
         sent[0] += sum(len(m) for m in ms.values())
-        lands[s] = lands.get(s, 0) + sum(len(masks(a, ranks(a), most)[me]) for a in range(N) if me in ranks(a))
+        lands[s] = lands.get(s, 0) + sum(len(masks(a, ranks(a), most, swap)[me]) for a in range(N) if me in ranks(a))
 
     def at(q):
         return order(q).index(me) + 1
@@ -138,53 +141,52 @@ def rank_program(g, core, T, topo):
 
     for b in range(4):
         (syn if b < 2 else act).dma_start(T.kt[quad(b)], (T.ky if b < 2 else T.lk)[:]).then_inc(sem.ld_t, 16)
-    iota(T.kf[:], [[8, 8], [1024, 2], [128, 8]], 0, 4, small=False)
     iota(T.pio[:], [[0, 1]], 0, 1, small=False)
     iota(T.cq0[:], [[0, 4], [1 - N, 2], [1, 8]], 0)
+    iota(T.cc0[:], [[16, 8], [1, 8], [128, 2]], 0)
     iota(T.win[:], [[0, WIN // 16], [1, 16]], K + 16 * me)
     iota(T.sv0[:], [[CAP, 8], [1, 16]], 16 - MID, 1)
-    G_KF, G_P, G_CQ, G_WIN, G_SV = range(1, 6)
+    G_P, G_CQ, G_CC, G_WIN, G_SV = range(1, 6)
+    i_kf = V(vec.memset(T.kf[:], 0))
     V(vec.memset(T.e[:], 0.0))
-    i_zz = V(vec.memset(T.zz[:], 0.0))
-    V(vec.memset(T.z[:], 0.0))
-    V(vec.memset(T.so[:], 0))
-    V(vec.memset(T.x2[:], 0.0))
-    vw(G_KF, "gi")
-    i_kf = V(vec.tensor_scalar(T.kf[quad(1)], T.kf[quad(1)], -128.0, None, A.add))
-    aw(G_KF, "gi")
-    sw(G_KF, "gi")
+    aw(i_kf, "v")
+    sw(i_kf, "v")
     for b in range(4):
-        if b == 1:
-            sw(i_kf, "v")
-        for h in range(2):
-            p = 32 * b + 16 * h + 1
-            (syn if b < 2 else act).dma_start(T.kf[p:p + 1, :], (T.ky if b < 2 else T.lk)[8 * h:8 * h + 8, :]).then_inc(sem.ld_f, 16)
+        (syn if b < 2 else act).dma_start(T.kf[32 * b + 1:32 * b + 32:16, :], (T.ky if b < 2 else T.lk)[:]).then_inc(sem.ld_f, 16)
     syn.dma_start(T.xb[:], T.x[:]).then_inc(sem.ld_x, 16)
     syn.dma_start(T.wb[:], T.w[:]).then_inc(sem.ld_w, 16)
 
     vw(G_P, "gi")
     V(vec.tensor_scalar(T.lane[:], T.pio[:], 15, None, A.bitwise_and))
     i = V(vec.tensor_scalar(T.hh[:], T.pio[:], 4, 1, A.logical_shift_right, A.bitwise_and))
+    i_zz = V(vec.memset(T.zz[:], 0.0))
     vw(i)
-    V(vec.tensor_copy(T.lanef[:], T.lane[:]))
-    i_od = V(vec.tensor_copy(T.od[:], T.hh[:]))
-    V(vec.tensor_scalar(T.h3[:], T.lane[:], 8.0, None, A.is_ge))
-    i = V(vec.tensor_scalar(T.lane8[:], T.lane[:], 8.0, None, A.mult))
+    i = V(vec.tensor_scalar(T.h3[:], T.lane[:], 8.0, None, A.is_ge))
     vw(G_CQ, "gi")
     i_cq = V(vec.tensor_scalar(T.cqn[:], T.cq0[:], -1.0, None, A.mult))
+    i_od = V(vec.tensor_copy(T.od[:], T.hh[:]))
     vw(i)
     V(vec.tensor_scalar(T.c64[:], T.cq0[:, 0:8:2], T.h3[:, 0:1], None, A.add))
     vw(i_cq)
     V(vec.tensor_tensor(T.cq[:], T.cq0[:], T.cqn[:], A.max))
-    V(vec.tensor_scalar(T.turn[:], T.cq0[:, 0:8], T.lane8[:, 0:1], None, A.add))
-    i_cv = V(vec.tensor_scalar(T.cv[:], T.cq0[:, 0:2], 16.0, T.lanef[:, 0:1], A.mult, A.add))
+    i_lane = V(vec.tensor_copy(T.lanef[:], T.lane[:]))
     aw(i_od, "v")
     for b, n, sh in ((0, 1, 0), (1, 1, 16), (2, 2, 0)):
         i = C(act.activation(T.tb[quad(b, n)], T.od[quad(b, n)], F.Identity, bias=float(sh - MID - 1), scale=float(2 * MID - 2 * sh - SL + 1)))
-    for b, n, sh in ((0, 1, 0), (1, 1, 1), (2, 2, 0)):
-        C(act.activation(T.eb[quad(b, n)], T.od[quad(b, n)], F.Identity, bias=float(1 + sh), scale=-1.0))
-    aw(i)
+    i = C(act.activation(T.od8[:], T.od[:], F.Identity, scale=8.0))
+    aw(i_lane, "v")
+    aw(i - 1)
     a_ini = C(act.activation(T.ini[:], T.lanef[:], F.Identity, bias=T.tb[:, 0:1], scale=float(CAP // 2)))
+    aw(i)
+    i = C(act.activation(T.b8[:], T.lanef[:], F.Identity, bias=T.od8[:, 0:1], scale=float(-S)))
+    aw(G_CC, "gi")
+    aw(i)
+    a_cc = C(act.activation(T.cc[:], T.cc0[:], F.Identity, bias=T.b8[:, 0:1]))
+    I_EQ = i_lane + 3
+    aw(I_EQ, "v")
+    a_big = C(act.activation(T.big[:], T.e[:, 0:128:2], F.Identity, scale=512.0))
+    for b, n, sh in ((0, 1, 0), (1, 1, 1), (2, 2, 0)):
+        a_eb = C(act.activation(T.eb[quad(b, n)], T.od[quad(b, n)], F.Identity, bias=float(1 + sh), scale=-1.0))
     kops = [(0, 0, 2, 1), (2, 0, 2, 0)] if me % 2 == 0 else [(0, 0, 2, 1), (2, 0, 1, 0), (3, 1, 1, 2)]
     third = {}
     for n_op, (bo, bi, n, j) in enumerate(kops):
@@ -195,7 +197,12 @@ def rank_program(g, core, T, topo):
             third[bo + d] = (us[0], 0) if ok[0] else (us[1], 1)
             C(act.activation(T.fd[quad(bi + d), n_op:n_op + 1], T.od[quad(bi + d)], F.Identity,
                              bias=0.0 if ok[0] else float(TAB), scale=float(TAB) * (ok[0] - ok[1])))
-    aw(i_zz, "v")
+    C(act.activation(T.ev2[:], T.od[:], F.Identity, bias=float(1 + me % 2), scale=-2.0))
+    C(act.activation(T.l2[:], T.lanef[:], F.Identity, bias=T.od[:, 0:1], scale=2.0))
+    a_z = C(act.activation(T.z[:], T.zz[:, 0:32], F.Copy))
+    C(act.activation(T.x2[:], T.zz[:, 0:32], F.Copy))
+    for ap in (T.d_s[:, 0:16], T.d_s[:, 16 + RL:32 + RL], T.mx2[:, 32:48]):
+        C(act.activation(ap, T.zz[:, 0:16], F.Identity, bias=float(-MID)))
     for c0 in range(0, TAB, TAB // 4):
         C(act.activation(T.tab[:, c0:c0 + TAB // 4], T.zz[:], F.Identity, bias=float(-MID)))
     aw(G_SV, "gi")
@@ -205,52 +212,58 @@ def rank_program(g, core, T, topo):
 
     vw(64, "ld_t")
     i = V(vec.tensor_scalar(T.ko[:], T.kt[:], N - 1, None, A.bitwise_and))
-    vw(i_cv)
-    i_cm = V(vec.tensor_scalar(T.cm[:], T.cv[:], float(25 - 3 * me), -24.0, A.is_ge, A.mult))
+    V(vec.tensor_scalar(T.lane8[:], T.lane[:], 8.0, None, A.mult))
     vw(i)
     i = V(vec.tensor_tensor(T.e[:, 0:128:2], T.ko[:, 0:8].indirect(T.c64[:, 0:4]), T.cq[:], A.is_equal))
-    vw(i_cm)
-    V(vec.tensor_tensor(T.cw[:], T.cv[:], T.cm[:], A.add))
+    assert i == I_EQ
+    vw(i - 1)
+    V(vec.tensor_scalar(T.turn[:], T.cq0[:, 0:8], T.lane8[:, 0:1], None, A.add))
+    V(vec.tensor_scalar(T.cv[:], T.cq0[:, 0:2], 16.0, T.lanef[:, 0:1], A.mult, A.add))
     vw(i)
     i = V(vec.transpose(T.ef[:], T.e[:]))
-    V(vec.tensor_scalar(T.big[:], T.e[:, 0:128:2], 512.0, None, A.mult))
+    vw(64, "ld_f")
+    i_pl = V(vec.tensor_scalar(T.kp[:], T.kf[:], 3, K - 1, A.logical_shift_right, A.bitwise_and))
     vw(i)
     vw(a_ini, "a")
     i = V(vec.tensor_tensor_scan(T.cu[:], T.ef[:], T.zz[:, 0:128], T.ini[:, 0:1], A.add, A.add))
-    V(vec.tensor_scalar(T.cot[:], T.cw[:], T.eb[:, 0:1], float(3 * me - 1), A.add, A.add))
-    V(vec.tensor_scalar(T.nh3[:], T.lane[:], 8.0, None, A.is_lt))
+    vw(i_pl)
+    vw(a_cc, "a")
+
+    def places(m0, m1):
+        c = slice(16 * m0, 16 * m1)
+        V(vec.tensor_tensor(T.pl[:, c], T.kp[:, 0:128].indirect(T.turn[:, m0:m1]), T.cc[:, c], A.max))
+    places(0, 2)
     vw(i)
     i = V(vec.transpose(T.ct[:], T.cu[:]))
-    vw(128, "ld_f")
-
-    def places(f):
-        V(vec.tensor_scalar(T.pl[:, 64 * f:64 * f + 64], T.kf[:, 0:128].indirect(T.turn[:, 4 * f:4 * f + 4]), 3, K - 1,
-                            A.logical_shift_right, A.bitwise_and))
-    places(0)
+    places(2, 6)
     vw(i)
+    vw(a_big, "a")
     i = V(vec.tensor_tensor_scan(T.rk[:], T.big[:], T.ct[:, 0:128:2], 0.0, A.add, A.min))
-    places(1)
+    places(6, 8)
     vw(i)
     V(vec.tensor_scalar(T.po[:, 0:8:2], T.rk[:, 7:64:16], float(MID), None, A.add))
     i = V(vec.tensor_scalar(T.po[:, 1:8:2], T.rk[:, 15:64:16], -1.0, float(MID), A.mult, A.add))
+    V(vec.tensor_scalar(T.cm[:], T.cv[:], float(25 - 3 * me), -24.0, A.is_ge, A.mult))
 
     vw(i)
     vw(G_WIN, "gi")
     i = V(vec.tensor_copy(T.win[:, 0:WIN].indirect(T.po[:, 0:8]), T.pl[:]))
-    for c0 in (0, 8):
-        i_x2 = V(vec.tensor_scalar(T.x2[:, c0:c0 + 8], T.po[:], float(-MID), None, A.add))
+    vw(i - 1)
+    V(vec.tensor_tensor(T.cw[:], T.cv[:], T.cm[:], A.add))
     vw(i)
     i = V(vec.transpose(T.tw[:], T.win[:]))
-    vw(i_x2)
-    V(vec.transpose(T.x2t[:], T.x2[:]))
+    vw(i - 1)
+    vw(a_eb, "a")
+    V(vec.tensor_scalar(T.cot[:], T.cw[:], T.eb[:, 0:1], float(3 * me - 1), A.add, A.add))
     vw(i)
-    for d in range(2):
-        i_ab = V(vec.tensor_tensor(T.ab[:, :, d], T.tw[:, :, 1], T.tw[:, :, 17], A.min))
+    i_ab = V(vec.tensor_tensor(T.ab[:, 0:NB], T.tw[:, :, 1], T.tw[:, :, 17], A.min))
 
     def three(q):
-        return T.ab[:, 3 * q // 2:3 * q // 2 + 3, :]
+        return T.ab[:, 3 * q // 2:3 * q // 2 + 3]
     gw(i_ab, "v")
-    send(order, 2, three, lambda q: T.kr[:, at(q), 0:6], "kr")
+    for near in (False, True):
+        send(lambda a: [q for q in order(a) if same_die(a, q) == near], 2, three, lambda q: T.kr[:, at(q), 0:3], "kr")
+    vw(a_z, "a")
     for po, c0, pi in ((quad(0, 2), 1, quad(0, 2)), (quad(0), 0, quad(1)), (quad(1), 2, quad(0))):
         i = V(vec.tensor_tensor(T.z[po, c0:c0 + 2 * NB:2], T.tw[pi, :, 0], T.tw[pi, :, 16], A.min))
     vw(16, "ld_x")
@@ -270,39 +283,39 @@ def rank_program(g, core, T, topo):
     gw(a_pk, "a")
     send(order, 4, lambda q: T.pk_s[:, part((q - me) % N)], lambda q: T.in_s[:, slot(at(q))], "s1")
 
-    i_own = V(vec.tensor_copy(T.kr[:, 0, 0:6], three(me)))
+    i_own = V(vec.tensor_copy(T.kr[:, 0, 0:3], three(me)))
     i_own1 = codes(T.in_q[:, 0:64], T.xq[:, 0:S], T.co[:, 0:4])
     a_own = scales(T.in_s[:, 0:64], T.xs[:, 0:S], T.co[:, 0:4])
-    V(vec.tensor_scalar(T.xa[:], T.x2t[:, 0:32:2], T.nh3[:, 0:1], None, A.mult))
-    V(vec.tensor_scalar(T.xc[:], T.x2t[:, 1:32:2], T.h3[:, 0:1], None, A.mult))
 
-    vw(a_tab, "a")
     vw(i_own)
+    vw(a_tab, "a")
     vw(lands["kr"], "kr")
     for n_op, (bo, bi, n, j) in enumerate(kops):
-        i = V(vec.tensor_scalar(T.kofs[quad(bo, n)], T.kr[quad(bi, n), :, 2 * j], T.fd[quad(bi, n), n_op:n_op + 1], None, A.add))
+        i = V(vec.tensor_scalar(T.kofs[quad(bo, n)], T.kr[quad(bi, n), :, j], T.fd[quad(bi, n), n_op:n_op + 1], None, A.add))
     for b in (0, 2):
-        V(vec.tensor_copy(T.rofs[quad(b, 2)], T.kr[quad(2, 2), :, 0:4]))
+        V(vec.tensor_copy(T.rofs[quad(b, 2)], T.kr[quad(2, 2), :, 0:2]))
     vw(i)
     i = V(vec.tensor_copy(T.tab[:, 0:2 * TAB].indirect(T.kofs[:, 0:8]), T.sv[:]))
     aw(i, "v")
-    a_g = C(act.activation(T.d_s[:, RL // 2:RL], T.tab[:, 0:TAB].indirect(T.rofs[:, 16:32]), F.Copy))
-    V(vec.tensor_tensor(T.x3[:, 0:16], T.xa[:], T.xc[:], A.add))
+    a_g = C(act.activation(T.d_s[:, 16 + RL // 2:16 + RL], T.tab[:, 0:TAB].indirect(T.rofs[:, 8:16]), F.Copy))
+    i_c3 = V(vec.tensor_scalar(T.c3[:], T.cv[:], 1.0 / 3, -2.0 / 3, A.mult, A.add))
     vw(i)
-    i = V(vec.tensor_copy(T.d_s[:, 0:RL // 2], T.tab[:, 0:TAB].indirect(T.rofs[:, 0:16])))
-    V(vec.tensor_tensor(T.x3[:, 16:32], T.xa[:], T.xc[:], A.add))
+    i = V(vec.tensor_copy(T.d_s[:, 16:16 + RL // 2], T.tab[:, 0:TAB].indirect(T.rofs[:, 0:8])))
+    vw(i_c3)
+    i_c4 = V(vec.tensor_tensor(T.c4[:], T.cv[:], T.c3[:], A.add))
     vw(i)
     vw(a_g, "a")
-    i = V(vec.transpose(T.t_s[:], T.d_s[:]))
+    V(vec.transpose(T.t_s[:, 0:2 * N + 2:2, :], T.d_s[:]))
+    i = V(vec.transpose(T.t_s[:, 1:2 * N:2, :], T.d_s[:, 16:16 + RL]))
+    vw(i_c4)
+    V(vec.tensor_scalar(T.sot[:], T.c4[:], T.ev2[:, 0:1], None, A.add))
     vw(i)
-    m0 = 16 * (me % 2)
-    i = V(vec.tensor_tensor(T.mx1[quad(0, 2)], T.t_s[quad(0, 2), :, m0:m0 + 48:16], T.t_s[quad(2, 2), :, m0:m0 + 48:16], A.max))
+    i = V(vec.tensor_tensor(T.mx1[quad(0, 2)], T.t_s[quad(0, 2), 0:2 * N + 1, 0:32:16], T.t_s[quad(2, 2), 0:2 * N + 1, 0:32:16], A.max))
     vw(i)
-    for b in range(2):
-        i = V(vec.tensor_tensor(T.mx2[quad(b)], T.mx1[quad(0)], T.mx1[quad(1)], A.max))
+    for b in range(4):
+        i = V(vec.tensor_tensor(T.mx2[quad(b), 0:4 * N + 2], T.mx1[quad(0)], T.mx1[quad(1)], A.max))
     vw(i)
-    for b in (0, 2):
-        i_so = V(vec.tensor_scalar(T.so[quad(b, 2), 1:25], T.mx2[quad(0, 2)], float(MID), None, A.add))
+    i_so = V(vec.tensor_scalar(T.so[:], T.mx2[:, 0:48].indirect(T.sot[:, 0:2]), float(MID), None, A.add))
 
     vw(max(i_so, i_own1))
     vw(lands["q1"], "q1")
@@ -320,18 +333,27 @@ def rank_program(g, core, T, topo):
         i_p2 = codes(T.p2_q[:, CAP * k0:CAP * k1], T.in_q[:, 0:LAND], off)
         a_p2 = scales(T.p2_s[:, CAP * k0:CAP * k1], T.in_s[:, 0:LAND], off)
         gw(i_p2, "v")
-        send(lambda a: order(a)[k0:k1], 4, lambda r: answer(T.p2_q, r).bitcast(dt.uint8), lambda r: back(T.bk_q, r).bitcast(dt.uint8), "q2")
-    gw(a_p2, "a")
-    send(order, 4, lambda r: answer(T.p2_s, r), lambda r: back(T.bk_s, r), "s2")
+        send(lambda a: order(a)[k0:k1], 8, lambda r: answer(T.p2_q, r).bitcast(dt.uint8), lambda r: back(T.bk_q, r).bitcast(dt.uint8), "q2")
+        gw(a_p2, "a")
+        send(lambda a: order(a)[k0:k1], 8, lambda r: answer(T.p2_s, r), lambda r: back(T.bk_s, r), "s2", swap=True)
+    V(vec.tensor_scalar(T.fot[:], T.zz[:, 0:2], T.l2[:, 0:1], None, A.add))
+    for c0 in (0, 16):
+        i = V(vec.tensor_scalar(T.x2[:, c0:c0 + 8], T.po[:], float(-MID), None, A.add))
     i_own2 = codes(T.bk_q[:, 0:64], T.in_q[:, 0:LAND], T.so[:, 0:4])
     a_own2 = scales(T.bk_s[:, 0:64], T.in_s[:, 0:LAND], T.so[:, 0:4])
-    i = V(vec.transpose(T.x3t[:], T.x3[:]))
+    vw(i)
+    i = V(vec.transpose(T.x2t[:], T.x2[:]))
     vw(16, "ld_w")
-    V(vec.quantize_mx(T.wq[:], T.ws[:], T.wb[:]))
+    V(vec.quantize_mx(T.wq[:, 0:128], T.ws[:, 0:128], T.wb[:, 0:512]))
     vw(i)
-    i = V(vec.tensor_scalar(T.fom[:], T.x3t[:, 0:16], float(CAP * me - MID), float(SL), A.is_lt, A.mult))
+    i = V(vec.tensor_copy(T.x3[:], T.x2t[:, 0:32].indirect(T.fot[:, 0:2])))
+    V(vec.quantize_mx(T.wq[:, 128:256], T.ws[:, 128:256], T.wb[:, 512:1024]))
     vw(i)
-    i = V(vec.tensor_tensor(T.fos[:], T.x3t[:, 0:16], T.fom[:], A.add))
+    i = V(vec.transpose(T.x3t[:], T.x3[:]))
+    vw(i)
+    i = V(vec.tensor_scalar(T.fom[:], T.x3t[:, :, 0:8], float(CAP * me - MID), float(SL), A.is_lt, A.mult))
+    vw(i)
+    i = V(vec.tensor_tensor(T.fos[:], T.x3t[:, :, 0:8], T.fom[:], A.add))
     vw(i)
     for b in (0, 2):
         i_fo = V(vec.tensor_scalar(T.fo[quad(b, 2)], T.fos[quad(2, 2)], float(MID + 16 - CAP * me), None, A.add))
@@ -359,9 +381,12 @@ def rank_program(g, core, T, topo):
         iv = V(vec.tensor_copy(T.yb[:, 128 * f:128 * f + 128], T.ps[:, 1024 * f:1024 * f + 128]))
         aw(O * f + 2, "t")
         ia = C(act.activation(T.yb[:, S + 128 * f:S + 128 * f + 128], T.ps[:, 1024 * f + 512:1024 * f + 640], F.Copy))
-    sw(iv, "v")
-    syn.dma_start(T.y[:, 0:S], T.yb[:, 0:S]).then_inc(sem.st, 16)
-    aw(ia)
-    act.dma_start(T.y[:, S:2 * S], T.yb[:, S:2 * S]).then_inc(sem.st, 16)
-    sw(32, "st")
+        sw(iv, "v")
+        syn.dma_start(T.y[:, 128 * f:128 * f + 128], T.yb[:, 128 * f:128 * f + 128]).then_inc(sem.st, 16)
+        if f == 0:
+            sw(ia, "a")
+        else:
+            aw(ia)
+        (syn if f == 0 else act).dma_start(T.y[:, S + 128 * f:S + 128 * f + 128], T.yb[:, S + 128 * f:S + 128 * f + 128]).then_inc(sem.st, 16)
+    sw(64, "st")
     gw(sent[0], "out")

@@ -3,12 +3,14 @@ from concourse.mybir import dt, AluOpType, ActivationFunctionType
 
 N, S, CAP, K, O = 8, 256, 48, 1024, 2
 SL = N * CAP
-WIN = SL + 32
+PITCH = CAP + 16
+WIN = N * PITCH
 NB = WIN // 32
 LAND = SL + 16
 MID = LAND // 2
 TAB = K + 16 * N
 RL = N * 32
+WHOLE = 3.0 * 2 ** 22
 FIRST = 4
 F8, F32, BF, F16, I32, U16 = "float8_e4m3fn_x4", "float32", "bfloat16", "float16", "int32", "uint16"
 
@@ -25,24 +27,24 @@ SCRATCH = {
     "lanef": ("sbuf", [128, 1], F32), "lane8": ("sbuf", [128, 1], F32), "h3": ("sbuf", [128, 1], F32),
     "c64": ("sbuf", [128, 4], U16), "turn": ("sbuf", [128, 8], U16),
     "od": ("sbuf", [128, 1], F32), "eb": ("sbuf", [128, 1], F32),
-    "tb": ("sbuf", [128, 1], F32), "ini": ("sbuf", [128, 1], F32), "fd": ("sbuf", [128, 4], F32),
+    "tb": ("sbuf", [128, 1], F32), "ini": ("sbuf", [128, 1], F32),
     "cv": ("sbuf", [128, 2], F32), "cm": ("sbuf", [128, 2], F32), "cw": ("sbuf", [128, 2], F32), "cot": ("sbuf", [128, 2], U16),
     "zz": ("sbuf", [128, TAB // 4], BF), "sv0": ("sbuf", [128, 128], F32), "sv": ("sbuf", [128, 128], BF),
     "e": ("sbuf", [128, 128], BF), "ef": ("sbuf", [128, 128], BF), "cu": ("sbuf", [128, 128], BF),
     "ct": ("sbuf", [128, 128], BF), "big": ("sbuf", [128, 64], BF), "rk": ("sbuf", [128, 64], BF),
     "po": ("sbuf", [128, 8], U16), "win": ("sbuf", [128, WIN], F32), "tw": ("sbuf", [128, NB, 32], F32),
-    "c3": ("sbuf", [128, 2], I32), "c4": ("sbuf", [128, 2], F32), "ev2": ("sbuf", [128, 1], F32), "sot": ("sbuf", [128, 2], U16),
-    "ab": ("sbuf", [128, 16], F16), "z": ("sbuf", [128, 32], F32), "co": ("sbuf", [128, 32], U16),
+    "ev2": ("sbuf", [128, 1], F32), "sot": ("sbuf", [128, 2], U16),
+    "ab": ("sbuf", [128, 16], F16), "z": ("sbuf", [128, 40], F32), "c3": ("sbuf", [128, 2], F32), "cr": ("sbuf", [128, 2], F32), "cx": ("sbuf", [128, 2], F32), "co": ("sbuf", [128, 32], U16),
     "x2": ("sbuf", [128, 32], BF), "x2t": ("sbuf", [128, 32], BF), "l2": ("sbuf", [128, 1], F32), "fot": ("sbuf", [128, 2], U16),
     "x3": ("sbuf", [128, 32], BF), "x3t": ("sbuf", [128, 2, 16], BF),
     "fom": ("sbuf", [128, 16], F32), "fos": ("sbuf", [128, 16], F32), "fo": ("sbuf", [128, 16], U16),
     "kr": ("sbuf", [128, N, 8], F16), "kofs": ("sbuf", [128, 8], U16), "rofs": ("sbuf", [128, 16], U16),
-    "tab": ("sbuf", [128, 2 * TAB], BF), "d_s": ("sbuf", [128, RL + 32], BF), "t_s": ("sbuf", [128, 2 * N + 2, 32], BF),
+    "tab": ("sbuf", [128, TAB], BF), "d_s": ("sbuf", [128, RL + 32], BF), "t_s": ("sbuf", [128, 2 * N + 2, 32], BF),
     "mx1": ("sbuf", [128, 4 * N + 2], F32), "mx2": ("sbuf", [128, 48], F32), "so": ("sbuf", [128, 32], U16),
     "pk_q": ("sbuf", [128, SL - CAP], F8), "pk_s": ("sbuf", [128, SL - CAP], "uint8"),
     "in_q": ("sbuf", [128, LAND], F8), "in_s": ("sbuf", [128, LAND], "uint8"),
     "p2_q": ("sbuf", [128, SL - CAP], F8), "p2_s": ("sbuf", [128, SL - CAP], "uint8"),
-    "bk_q": ("sbuf", [128, LAND], F8), "bk_s": ("sbuf", [128, LAND], "uint8"),
+    "bk_q": ("sbuf", [128, WIN], F8), "bk_s": ("sbuf", [128, WIN], "uint8"),
     "fp_q": ("sbuf", [128, S], F8), "fp_s": ("sbuf", [128, S], "uint8"),
     "ps": ("psum", [128, 2048], F32), "yb": ("sbuf", [128, S * O], F32),
 }
@@ -96,30 +98,21 @@ def rank_program(g, core, T, topo):
         far = [(a + i) % N for i in range(1, N) if not same_die(a, (a + i) % N)]
         return far[:1] + near[:1] + far[1:2] + near[1:2] + far[2:] + near[2:]
 
-    def masks(a, ranks, most, swap):
+    def spread(a, ranks, swap):
+        every = topo.engines(T.cores[a], T.cores[ranks[0]])
+        free = (every[1::2] + every[0::2])[::-1 if swap else 1]
         out = {}
-        for near in (True, False):
-            qs = [q for q in ranks if same_die(a, q) == near]
-            if not qs:
-                continue
-            free = topo.engines(T.cores[a], T.cores[qs[0]])[0 if near != swap else 1::2]
-            n = most
-            while n * len(qs) > len(free):
-                n //= 2
-            spare = len(free) - n * len(qs)
-            for q in qs:
-                k = 2 * n if 2 * n <= most and spare >= n else n
-                spare -= k - n
-                out[q], free = free[:k], free[k:]
+        for k, q in enumerate(sorted(ranks, key=lambda q: same_die(a, q))):
+            n = len(every) // 4 * (2 if len(ranks) == 3 and k == 2 else 1)
+            out[q], free = free[:n], free[n:]
         return out
 
-    def send(ranks, most, src, dst, s, swap=False):
-        ms = masks(me, ranks(me), most, swap)
+    def send(plan, src, dst, s):
         g.remote_dma_fused([RemoteDMATransfer(dst_ids=[DstId(rid=topo.addr(T.cores[q])[0], pnc=topo.addr(T.cores[q])[1])],
-                                              dma_engine_mask=sum(1 << e for e in ms[q]), remote_sem=sem[s], src=src(q), dst=dst(q))
-                            for q in ranks(me)], local_sem=sem.out)
-        sent[0] += sum(len(m) for m in ms.values())
-        lands[s] = lands.get(s, 0) + sum(len(masks(a, ranks(a), most, swap)[me]) for a in range(N) if me in ranks(a))
+                                              dma_engine_mask=sum(1 << e for e in es), remote_sem=sem[s], src=src(q), dst=dst(q))
+                            for q, es in plan(me).items()], local_sem=sem.out)
+        sent[0] += sum(len(es) for es in plan(me).values())
+        lands[s] = lands.get(s, 0) + sum(len(plan(a).get(me, [])) for a in range(N))
 
     def at(q):
         return order(q).index(me) + 1
@@ -145,8 +138,10 @@ def rank_program(g, core, T, topo):
     iota(T.cq0[:], [[0, 4], [1 - N, 2], [1, 8]], 0)
     iota(T.cc0[:], [[16, 8], [1, 8], [128, 2]], 0)
     iota(T.win[:], [[0, WIN // 16], [1, 16]], K + 16 * me)
-    iota(T.sv0[:], [[CAP, 8], [1, 16]], 16 - MID, 1)
-    G_P, G_CQ, G_CC, G_WIN, G_SV = range(1, 6)
+    iota(T.sv0[:, 16 * me:128], [[CAP, N - me], [1, 16]], 16 - MID, 1)
+    if me:
+        iota(T.sv0[:, 0:16 * me], [[CAP, me], [1, 16]], 16 - MID + CAP * (N - me), 1)
+    G_P, G_CQ, G_CC, G_WIN, G_SV = 1, 2, 3, 4, 6 if me else 5
     i_kf = V(vec.memset(T.kf[:], 0))
     V(vec.memset(T.e[:], 0.0))
     aw(i_kf, "v")
@@ -172,150 +167,179 @@ def rank_program(g, core, T, topo):
     i_lane = V(vec.tensor_copy(T.lanef[:], T.lane[:]))
     aw(i_od, "v")
     for b, n, sh in ((0, 1, 0), (1, 1, 16), (2, 2, 0)):
-        i = C(act.activation(T.tb[quad(b, n)], T.od[quad(b, n)], F.Identity, bias=float(sh - MID - 1), scale=float(2 * MID - 2 * sh - SL + 1)))
+        i = C(act.activation(T.tb[quad(b, n)], T.od[quad(b, n)], F.Identity, bias=float(sh - WIN // 2 - 1), scale=float(PITCH - CAP - 2 * sh + 1)))
     i = C(act.activation(T.od8[:], T.od[:], F.Identity, scale=8.0))
     aw(i_lane, "v")
     aw(i - 1)
-    a_ini = C(act.activation(T.ini[:], T.lanef[:], F.Identity, bias=T.tb[:, 0:1], scale=float(CAP // 2)))
+    C(act.activation(T.ini[:], T.lanef[:], F.Identity, bias=T.tb[:, 0:1], scale=float(PITCH // 2)))
     aw(i)
     i = C(act.activation(T.b8[:], T.lanef[:], F.Identity, bias=T.od8[:, 0:1], scale=float(-S)))
     aw(G_CC, "gi")
     aw(i)
     a_cc = C(act.activation(T.cc[:], T.cc0[:], F.Identity, bias=T.b8[:, 0:1]))
-    I_EQ = i_lane + 3
+    i = C(act.activation(T.cv[:], T.cq0[:, 0:2], F.Identity, bias=T.lanef[:, 0:1], scale=16.0))
+    I_EQ = i_lane + 4
     aw(I_EQ, "v")
-    a_big = C(act.activation(T.big[:], T.e[:, 0:128:2], F.Identity, scale=512.0))
+    a_big = C(act.activation(T.big[:], T.e[:, 0:128:2], F.Identity, scale=2.0 * WIN))
+    aw(i)
+    i = C(act.activation(T.cm[:], T.cv[:], F.Sign, bias=3 * me - 24.5))
     for b, n, sh in ((0, 1, 0), (1, 1, 1), (2, 2, 0)):
-        a_eb = C(act.activation(T.eb[quad(b, n)], T.od[quad(b, n)], F.Identity, bias=float(1 + sh), scale=-1.0))
-    kops = [(0, 0, 2, 1), (2, 0, 2, 0)] if me % 2 == 0 else [(0, 0, 2, 1), (2, 0, 1, 0), (3, 1, 1, 2)]
-    third = {}
-    for n_op, (bo, bi, n, j) in enumerate(kops):
-        for d in range(n):
-            col = 2 * (3 * me // 2 + j) - (bi + d) - 3 * me
-            us = [col, col + 1]
-            ok = [0 <= u < 3 for u in us]
-            third[bo + d] = (us[0], 0) if ok[0] else (us[1], 1)
-            C(act.activation(T.fd[quad(bi + d), n_op:n_op + 1], T.od[quad(bi + d)], F.Identity,
-                             bias=0.0 if ok[0] else float(TAB), scale=float(TAB) * (ok[0] - ok[1])))
-    C(act.activation(T.ev2[:], T.od[:], F.Identity, bias=float(1 + me % 2), scale=-2.0))
+        C(act.activation(T.eb[quad(b, n)], T.od[quad(b, n)], F.Identity, bias=float(1 + sh), scale=-1.0))
+    aw(i)
+    for m in range(2):
+        i = C(act.activation(T.cw[:, m:m + 1], T.cm[:, m:m + 1], F.Identity, bias=T.cv[:, m:m + 1], scale=-12.0))
+    aw(i)
+    i = C(act.activation(T.c3[:], T.cw[:], F.Identity, bias=(3 * me - 14) / 3, scale=1.0 / 3))
+    C(act.activation(T.ev2[:], T.od[:], F.Identity, bias=2.0, scale=-2.0))
+    aw(i)
+    i = C(act.activation(T.cr[:], T.c3[:], F.Identity, bias=WHOLE))
     C(act.activation(T.l2[:], T.lanef[:], F.Identity, bias=T.od[:, 0:1], scale=2.0))
-    a_z = C(act.activation(T.z[:], T.zz[:, 0:32], F.Copy))
+    aw(i)
+    for m in range(2):
+        a_cx = C(act.activation(T.cx[:, m:m + 1], T.cr[:, m:m + 1], F.Identity, bias=T.cw[:, m:m + 1]))
     C(act.activation(T.x2[:], T.zz[:, 0:32], F.Copy))
+    a_z = C(act.activation(T.z[:], T.zz[:, 0:40], F.Copy))
     for ap in (T.d_s[:, 0:16], T.d_s[:, 16 + RL:32 + RL], T.mx2[:, 32:48]):
         C(act.activation(ap, T.zz[:, 0:16], F.Identity, bias=float(-MID)))
     for c0 in range(0, TAB, TAB // 4):
         C(act.activation(T.tab[:, c0:c0 + TAB // 4], T.zz[:], F.Identity, bias=float(-MID)))
     aw(G_SV, "gi")
-    for b in range(4):
-        u, h = third[b]
-        a_tab = C(act.activation(T.sv[quad(b)], T.sv0[quad(b)], F.Identity, bias=float(16 * u - 32 * b - 16 * h)))
+    for b, u in enumerate((2, 1, 0, -1)):
+        a_tab = C(act.activation(T.sv[quad(b)], T.sv0[quad(b)], F.Identity, bias=float(16 * u - 32 * b)))
 
+    V(vec.tensor_scalar(T.lane8[:], T.lane[:], 8.0, None, A.mult))
     vw(64, "ld_t")
     i = V(vec.tensor_scalar(T.ko[:], T.kt[:], N - 1, None, A.bitwise_and))
-    V(vec.tensor_scalar(T.lane8[:], T.lane[:], 8.0, None, A.mult))
+    vw(i - 1)
+    V(vec.tensor_scalar(T.turn[:], T.cq0[:, 0:8], T.lane8[:, 0:1], None, A.add))
     vw(i)
     i = V(vec.tensor_tensor(T.e[:, 0:128:2], T.ko[:, 0:8].indirect(T.c64[:, 0:4]), T.cq[:], A.is_equal))
     assert i == I_EQ
-    vw(i - 1)
-    V(vec.tensor_scalar(T.turn[:], T.cq0[:, 0:8], T.lane8[:, 0:1], None, A.add))
-    V(vec.tensor_scalar(T.cv[:], T.cq0[:, 0:2], 16.0, T.lanef[:, 0:1], A.mult, A.add))
+    vw(64, "ld_f")
+    V(vec.tensor_scalar(T.kp[:, 0:64], T.kf[:, 0:64], 3, K - 1, A.logical_shift_right, A.bitwise_and))
     vw(i)
     i = V(vec.transpose(T.ef[:], T.e[:]))
-    vw(64, "ld_f")
-    i_pl = V(vec.tensor_scalar(T.kp[:], T.kf[:], 3, K - 1, A.logical_shift_right, A.bitwise_and))
+    i_pl = V(vec.tensor_scalar(T.kp[:, 64:128], T.kf[:, 64:128], 3, K - 1, A.logical_shift_right, A.bitwise_and))
     vw(i)
-    vw(a_ini, "a")
+    vw(a_cc, "a")
     i = V(vec.tensor_tensor_scan(T.cu[:], T.ef[:], T.zz[:, 0:128], T.ini[:, 0:1], A.add, A.add))
     vw(i_pl)
-    vw(a_cc, "a")
 
     def places(m0, m1):
         c = slice(16 * m0, 16 * m1)
         V(vec.tensor_tensor(T.pl[:, c], T.kp[:, 0:128].indirect(T.turn[:, m0:m1]), T.cc[:, c], A.max))
-    places(0, 2)
+    places(0, 4)
     vw(i)
     i = V(vec.transpose(T.ct[:], T.cu[:]))
-    places(2, 6)
+    places(4, 6)
     vw(i)
     vw(a_big, "a")
     i = V(vec.tensor_tensor_scan(T.rk[:], T.big[:], T.ct[:, 0:128:2], 0.0, A.add, A.min))
     places(6, 8)
     vw(i)
-    V(vec.tensor_scalar(T.po[:, 0:8:2], T.rk[:, 7:64:16], float(MID), None, A.add))
-    i = V(vec.tensor_scalar(T.po[:, 1:8:2], T.rk[:, 15:64:16], -1.0, float(MID), A.mult, A.add))
-    V(vec.tensor_scalar(T.cm[:], T.cv[:], float(25 - 3 * me), -24.0, A.is_ge, A.mult))
+    V(vec.tensor_scalar(T.po[:, 0:8:2], T.rk[:, 7:64:16], float(WIN // 2), None, A.add))
+    i = V(vec.tensor_scalar(T.po[:, 1:8:2], T.rk[:, 15:64:16], -1.0, float(WIN // 2), A.mult, A.add))
 
     vw(i)
     vw(G_WIN, "gi")
     i = V(vec.tensor_copy(T.win[:, 0:WIN].indirect(T.po[:, 0:8]), T.pl[:]))
-    vw(i - 1)
-    V(vec.tensor_tensor(T.cw[:], T.cv[:], T.cm[:], A.add))
-    vw(i)
-    i = V(vec.transpose(T.tw[:], T.win[:]))
-    vw(i - 1)
-    vw(a_eb, "a")
-    V(vec.tensor_scalar(T.cot[:], T.cw[:], T.eb[:, 0:1], float(3 * me - 1), A.add, A.add))
-    vw(i)
-    i_ab = V(vec.tensor_tensor(T.ab[:, 0:NB], T.tw[:, :, 1], T.tw[:, :, 17], A.min))
-
-    def three(q):
-        return T.ab[:, 3 * q // 2:3 * q // 2 + 3]
-    gw(i_ab, "v")
-    for near in (False, True):
-        send(lambda a: [q for q in order(a) if same_die(a, q) == near], 2, three, lambda q: T.kr[:, at(q), 0:3], "kr")
     vw(a_z, "a")
+    V(vec.tensor_scalar(T.cot[:], T.cx[:], T.eb[:, 0:1], 3 * me - 13 - WHOLE, A.add, A.add))
+    vw(i)
+
+    def steps(a):
+        o = N // 2 if a < N // 2 else 0
+        return [(o, o + 1), (o + 1, o + N // 2), (N // 2 - o, N - o)]
+
+    def turned(q0, q1):
+        return V(vec.transpose(T.tw[:, 2 * q0:2 * q1, :], T.win[:, PITCH * q0:PITCH * q1]))
+
+    def two(q):
+        return T.ab[:, 2 * q:2 * q + 2]
+
+    def met(q0, q1, i_t):
+        vw(i_t)
+        return V(vec.tensor_tensor(T.ab[:, 2 * q0:2 * q1], T.tw[:, 2 * q0:2 * q1, 1], T.tw[:, 2 * q0:2 * q1, 17], A.min))
+
+    def deal(a, k):
+        other = list(range(steps(a)[0][0], steps(a)[1][1]))
+        own = [q for q in order(a) if q not in other]
+        every = topo.engines(T.cores[a], T.cores[other[0]])
+        four = [(every[1::2] + every[0::2])[4 * n:4 * n + 4] for n in range(4)]
+        return [{other[0]: four[0]}, {other[1]: four[1], other[2]: four[2], other[3]: four[0]},
+                {own[0]: four[3], own[1]: four[1], own[2]: four[2]}][k]
+
+    def lists(k, i):
+        gw(i, "v")
+        send(lambda a: deal(a, k), two, lambda q: T.kr[:, (at(q) + q) % N, 0:2], "kr")
+    q0, q1 = steps(me)[1]
+    i = turned(*steps(me)[0])
+    turned(q0, q0 + 1)
+    lists(0, met(*steps(me)[0], i))
+    i = turned(q0 + 1, q1)
+    i_t = turned(*steps(me)[2])
+    lists(1, met(q0, q1, i))
+    V(vec.tensor_scalar(T.x2[:, 0:8], T.po[:], float(-WIN // 2), None, A.add))
+    lists(2, met(*steps(me)[2], i_t))
     for po, c0, pi in ((quad(0, 2), 1, quad(0, 2)), (quad(0), 0, quad(1)), (quad(1), 2, quad(0))):
         i = V(vec.tensor_tensor(T.z[po, c0:c0 + 2 * NB:2], T.tw[pi, :, 0], T.tw[pi, :, 16], A.min))
     vw(16, "ld_x")
     V(vec.quantize_mx(T.xq[:, 0:128], T.xs[:, 0:128], T.xb[:, 0:512]))
     vw(i)
-    i = V(vec.tensor_scalar(T.co[:], T.z[:, 0:32].indirect(T.cot[:, 0:2]), float(S - 1), None, A.min))
+    i = V(vec.tensor_scalar(T.co[:], T.z[:, 0:40].indirect(T.cot[:, 0:2]), float(S - 1), None, A.min))
     V(vec.quantize_mx(T.xq[:, 128:256], T.xs[:, 128:256], T.xb[:, 512:1024]))
     vw(i)
     i_co = V(vec.tensor_copy(T.co[quad(2, 2)], T.co[quad(0, 2)]))
+    V(vec.tensor_copy(T.kr[:, me, 0:2], two(me)))
+    V(vec.tensor_scalar(T.fot[:], T.zz[:, 0:2], T.l2[:, 0:1], None, A.add))
 
     vw(i_co)
     aw(i_co, "v")
-    i_pk = codes(T.pk_q[:], T.xq[:, 0:S], T.co[:, 4:25])
-    a_pk = scales(T.pk_s[:], T.xs[:, 0:S], T.co[:, 4:25])
-    gw(i_pk, "v")
-    send(order, 4, lambda q: T.pk_q[:, part((q - me) % N)].bitcast(dt.uint8), lambda q: T.in_q[:, slot(at(q))].bitcast(dt.uint8), "q1")
-    gw(a_pk, "a")
-    send(order, 4, lambda q: T.pk_s[:, part((q - me) % N)], lambda q: T.in_s[:, slot(at(q))], "s1")
+    for k0, k1 in ((FIRST, N - 1), (0, FIRST)):
+        off = T.co[:, 4 + 3 * k0:4 + 3 * k1]
+        i_pk = codes(T.pk_q[:, CAP * k0:CAP * k1], T.xq[:, 0:S], off)
+        a_pk = scales(T.pk_s[:, CAP * k0:CAP * k1], T.xs[:, 0:S], off)
 
-    i_own = V(vec.tensor_copy(T.kr[:, 0, 0:3], three(me)))
-    i_own1 = codes(T.in_q[:, 0:64], T.xq[:, 0:S], T.co[:, 0:4])
+        def ahead(a):
+            return [(a + 1 + k) % N for k in range(k0, k1)]
+        gw(i_pk, "v")
+        send(lambda a: spread(a, ahead(a), False), lambda q: T.pk_q[:, part((q - me) % N)].bitcast(dt.uint8),
+             lambda q: T.in_q[:, slot(at(q))].bitcast(dt.uint8), "q1")
+        gw(a_pk, "a")
+        send(lambda a: spread(a, ahead(a), True), lambda q: T.pk_s[:, part((q - me) % N)], lambda q: T.in_s[:, slot(at(q))], "s1")
+
     a_own = scales(T.in_s[:, 0:64], T.xs[:, 0:S], T.co[:, 0:4])
+    i_own1 = codes(T.in_q[:, 0:64], T.xq[:, 0:S], T.co[:, 0:4])
 
-    vw(i_own)
+    vw(i_co + 1)
     vw(a_tab, "a")
     vw(lands["kr"], "kr")
-    for n_op, (bo, bi, n, j) in enumerate(kops):
-        i = V(vec.tensor_scalar(T.kofs[quad(bo, n)], T.kr[quad(bi, n), :, j], T.fd[quad(bi, n), n_op:n_op + 1], None, A.add))
+    for j in (1, 0):
+        i = V(vec.tensor_copy(T.kofs[quad(2 - 2 * j, 2)], T.kr[quad(0, 2), :, j]))
     for b in (0, 2):
         V(vec.tensor_copy(T.rofs[quad(b, 2)], T.kr[quad(2, 2), :, 0:2]))
     vw(i)
-    i = V(vec.tensor_copy(T.tab[:, 0:2 * TAB].indirect(T.kofs[:, 0:8]), T.sv[:]))
+    i = V(vec.tensor_copy(T.tab[:, 0:TAB].indirect(T.kofs[:, 0:8]), T.sv[:]))
     aw(i, "v")
     a_g = C(act.activation(T.d_s[:, 16 + RL // 2:16 + RL], T.tab[:, 0:TAB].indirect(T.rofs[:, 8:16]), F.Copy))
-    i_c3 = V(vec.tensor_scalar(T.c3[:], T.cv[:], 1.0 / 3, -2.0 / 3, A.mult, A.add))
+    V(vec.tensor_scalar(T.sot[:], T.cx[:], T.ev2[:, 0:1], 3 * me - 13 - WHOLE, A.add, A.add))
     vw(i)
     i = V(vec.tensor_copy(T.d_s[:, 16:16 + RL // 2], T.tab[:, 0:TAB].indirect(T.rofs[:, 0:8])))
-    vw(i_c3)
-    i_c4 = V(vec.tensor_tensor(T.c4[:], T.cv[:], T.c3[:], A.add))
+    i_f = V(vec.tensor_scalar(T.x2[:, 16:24], T.po[:], float(-WIN // 2), None, A.add))
     vw(i)
     vw(a_g, "a")
     V(vec.transpose(T.t_s[:, 0:2 * N + 2:2, :], T.d_s[:]))
     i = V(vec.transpose(T.t_s[:, 1:2 * N:2, :], T.d_s[:, 16:16 + RL]))
-    vw(i_c4)
-    V(vec.tensor_scalar(T.sot[:], T.c4[:], T.ev2[:, 0:1], None, A.add))
+    vw(i_f)
+    V(vec.transpose(T.x2t[:], T.x2[:]))
     vw(i)
     i = V(vec.tensor_tensor(T.mx1[quad(0, 2)], T.t_s[quad(0, 2), 0:2 * N + 1, 0:32:16], T.t_s[quad(2, 2), 0:2 * N + 1, 0:32:16], A.max))
     vw(i)
     for b in range(4):
         i = V(vec.tensor_tensor(T.mx2[quad(b), 0:4 * N + 2], T.mx1[quad(0)], T.mx1[quad(1)], A.max))
     vw(i)
-    i_so = V(vec.tensor_scalar(T.so[:], T.mx2[:, 0:48].indirect(T.sot[:, 0:2]), float(MID), None, A.add))
+    i_so = V(vec.tensor_scalar(T.so[:], T.mx2[:, 0:48].indirect(T.sot[:, 0:2]), float(MID), float(LAND - 1), A.add, A.min))
+    i_f = V(vec.tensor_copy(T.x3[:], T.x2t[:, 0:32].indirect(T.fot[:, 0:2])))
 
     vw(max(i_so, i_own1))
     vw(lands["q1"], "q1")
@@ -327,47 +351,44 @@ def rank_program(g, core, T, topo):
         return buf[:, part(order(me).index(r) + 1)]
 
     def back(buf, r):
-        return buf[:, slot((me - r) % N)]
-    for k0, k1 in ((0, FIRST), (FIRST, N - 1)):
+        c0 = 16 + PITCH * ((me - r) % N)
+        return buf[:, c0:c0 + CAP]
+    for k0, k1 in ((FIRST, N - 1), (0, FIRST)):
         off = T.so[:, 4 + 3 * k0:4 + 3 * k1]
         i_p2 = codes(T.p2_q[:, CAP * k0:CAP * k1], T.in_q[:, 0:LAND], off)
         a_p2 = scales(T.p2_s[:, CAP * k0:CAP * k1], T.in_s[:, 0:LAND], off)
         gw(i_p2, "v")
-        send(lambda a: order(a)[k0:k1], 8, lambda r: answer(T.p2_q, r).bitcast(dt.uint8), lambda r: back(T.bk_q, r).bitcast(dt.uint8), "q2")
+        send(lambda a: spread(a, order(a)[k0:k1], False), lambda r: answer(T.p2_q, r).bitcast(dt.uint8),
+             lambda r: back(T.bk_q, r).bitcast(dt.uint8), "q2")
         gw(a_p2, "a")
-        send(lambda a: order(a)[k0:k1], 8, lambda r: answer(T.p2_s, r), lambda r: back(T.bk_s, r), "s2", swap=True)
-    V(vec.tensor_scalar(T.fot[:], T.zz[:, 0:2], T.l2[:, 0:1], None, A.add))
-    for c0 in (0, 16):
-        i = V(vec.tensor_scalar(T.x2[:, c0:c0 + 8], T.po[:], float(-MID), None, A.add))
+        send(lambda a: spread(a, order(a)[k0:k1], True), lambda r: answer(T.p2_s, r), lambda r: back(T.bk_s, r), "s2")
+    vw(i_f)
+    i = V(vec.transpose(T.x3t[:], T.x3[:]))
     i_own2 = codes(T.bk_q[:, 0:64], T.in_q[:, 0:LAND], T.so[:, 0:4])
     a_own2 = scales(T.bk_s[:, 0:64], T.in_s[:, 0:LAND], T.so[:, 0:4])
     vw(i)
-    i = V(vec.transpose(T.x2t[:], T.x2[:]))
+    i = V(vec.tensor_scalar(T.fom[:], T.x3t[:, :, 0:8], float(PITCH * me - WIN // 2), float(WIN), A.is_lt, A.mult))
     vw(16, "ld_w")
     V(vec.quantize_mx(T.wq[:, 0:128], T.ws[:, 0:128], T.wb[:, 0:512]))
     vw(i)
-    i = V(vec.tensor_copy(T.x3[:], T.x2t[:, 0:32].indirect(T.fot[:, 0:2])))
+    i = V(vec.tensor_tensor(T.fos[:], T.x3t[:, :, 0:8], T.fom[:], A.add))
     V(vec.quantize_mx(T.wq[:, 128:256], T.ws[:, 128:256], T.wb[:, 512:1024]))
     vw(i)
-    i = V(vec.transpose(T.x3t[:], T.x3[:]))
-    vw(i)
-    i = V(vec.tensor_scalar(T.fom[:], T.x3t[:, :, 0:8], float(CAP * me - MID), float(SL), A.is_lt, A.mult))
-    vw(i)
-    i = V(vec.tensor_tensor(T.fos[:], T.x3t[:, :, 0:8], T.fom[:], A.add))
-    vw(i)
     for b in (0, 2):
-        i_fo = V(vec.tensor_scalar(T.fo[quad(b, 2)], T.fos[quad(2, 2)], float(MID + 16 - CAP * me), None, A.add))
+        i_fo = V(vec.tensor_scalar(T.fo[quad(b, 2)], T.fos[quad(2, 2)], float(WIN // 2 + 16 - PITCH * me), None, A.add))
 
     vw(max(i_own2, i_fo))
     vw(lands["q2"], "q2")
     aw(i_fo, "v")
     aw(a_own2)
     aw(lands["s2"], "s2")
-    done = []
-    for f in range(2):
-        c = slice(128 * f, 128 * f + 128)
-        off = T.fo[:, 8 * f:8 * f + 8]
-        done.append((codes(T.fp_q[:, c], T.bk_q[:, 0:LAND], off), scales(T.fp_s[:, c], T.bk_s[:, 0:LAND], off)))
+    codes(T.fp_q[:, 0:64], T.bk_q[:, 0:WIN], T.fo[:, 0:4])
+    codes(T.fp_q[:, 64:128], T.bk_q[:, 0:WIN], T.fo[:, 4:8])
+    vw(a_own2, "a")
+    vw(lands["s2"], "s2")
+    done = [(V(vec.tensor_copy(T.fp_s[:, 64:128], T.bk_s[:, 0:WIN].indirect(T.fo[:, 4:8]))),
+             scales(T.fp_s[:, 0:64], T.bk_s[:, 0:WIN], T.fo[:, 0:4])),
+            (codes(T.fp_q[:, 128:256], T.bk_q[:, 0:WIN], T.fo[:, 8:16]), scales(T.fp_s[:, 128:256], T.bk_s[:, 0:WIN], T.fo[:, 8:16]))]
     for f in range(2):
         c = slice(128 * f, 128 * f + 128)
         W(ten, "t", "v", done[f][0])

@@ -10,35 +10,34 @@ LAND = SL + 16
 MID = LAND // 2
 TAB = K + 16 * N
 RL = N * 32
+RV = 3
 WHOLE = 3.0 * 2 ** 22
-FIRST = 4
+PARTS = ((7, 8), (5, 7), (1, 5))
+BIG = 2 ** 13
+LO, HI = 12, 4
 F8, F32, BF, F16, I32, U16 = "float8_e4m3fn_x4", "float32", "bfloat16", "float16", "int32", "uint16"
 
 SCRATCH = {
     "xb": ("sbuf", [128, 4 * S], BF), "wb": ("sbuf", [128, 512 * O], BF),
     "xq": ("sbuf", [128, S], F8), "xs": ("sbuf", [128, S], "uint8"),
     "wq": ("sbuf", [128, 128 * O], F8), "ws": ("sbuf", [128, 128 * O], "uint8"),
-    "kt": ("sbuf", [128, 8], I32), "ko": ("sbuf", [128, 8], I32),
-    "kf": ("sbuf", [128, 128], I32), "kp": ("sbuf", [128, 128], I32), "pl": ("sbuf", [128, 128], F32),
-    "cc0": ("sbuf", [128, 128], F32), "cc": ("sbuf", [128, 128], F32),
-    "b8": ("sbuf", [128, 1], F32), "od8": ("sbuf", [128, 1], F32),
-    "pio": ("sbuf", [128, 1], I32), "lane": ("sbuf", [128, 1], I32), "hh": ("sbuf", [128, 1], I32),
-    "cq0": ("sbuf", [128, 64], F32), "cqn": ("sbuf", [128, 64], F32), "cq": ("sbuf", [128, 64], F32),
-    "lanef": ("sbuf", [128, 1], F32), "lane8": ("sbuf", [128, 1], F32), "h3": ("sbuf", [128, 1], F32),
-    "c64": ("sbuf", [128, 4], U16), "turn": ("sbuf", [128, 8], U16),
-    "od": ("sbuf", [128, 1], F32), "eb": ("sbuf", [128, 1], F32),
-    "tb": ("sbuf", [128, 1], F32), "ini": ("sbuf", [128, 1], F32),
-    "cv": ("sbuf", [128, 2], F32), "cm": ("sbuf", [128, 2], F32), "cw": ("sbuf", [128, 2], F32), "cot": ("sbuf", [128, 2], U16),
-    "zz": ("sbuf", [128, TAB // 4], BF), "sv0": ("sbuf", [128, 128], F32), "sv": ("sbuf", [128, 128], BF),
-    "e": ("sbuf", [128, 128], BF), "ef": ("sbuf", [128, 128], BF), "cu": ("sbuf", [128, 128], BF),
-    "ct": ("sbuf", [128, 128], BF), "big": ("sbuf", [128, 64], BF), "rk": ("sbuf", [128, 64], BF),
-    "po": ("sbuf", [128, 8], U16), "win": ("sbuf", [128, WIN], F32), "tw": ("sbuf", [128, NB, 32], F32),
-    "ev2": ("sbuf", [128, 1], F32), "sot": ("sbuf", [128, 2], U16),
-    "ab": ("sbuf", [128, 16], F16), "z": ("sbuf", [128, 40], F32), "c3": ("sbuf", [128, 2], F32), "cr": ("sbuf", [128, 2], F32), "cx": ("sbuf", [128, 2], F32), "co": ("sbuf", [128, 32], U16),
-    "x2": ("sbuf", [128, 32], BF), "x2t": ("sbuf", [128, 32], BF), "l2": ("sbuf", [128, 1], F32), "fot": ("sbuf", [128, 2], U16),
-    "x3": ("sbuf", [128, 32], BF), "x3t": ("sbuf", [128, 2, 16], BF),
-    "fom": ("sbuf", [128, 16], F32), "fos": ("sbuf", [128, 16], F32), "fo": ("sbuf", [128, 16], U16),
-    "kr": ("sbuf", [128, N, 8], F16), "kofs": ("sbuf", [128, 8], U16), "rofs": ("sbuf", [128, 16], U16),
+    "kt": ("sbuf", [128, 8], I32), "ko": ("sbuf", [128, 8], I32), "k16": ("sbuf", [128, 8], U16),
+    "kp": ("sbuf", [128, 16], I32), "pp": ("sbuf", [128, 128], BF), "pl": ("sbuf", [128, 128], BF),
+    "pio": ("sbuf", [128, 1], I32), "ci": ("sbuf", [128, 7], I32), "cf": ("sbuf", [128, 6], F32),
+    "seat": ("sbuf", [128, N], F32), "c16": ("sbuf", [128, 8], F32), "cfo": ("sbuf", [128, 4], F32), "pat": ("sbuf", [128, 128], F32),
+    "val": ("sbuf", [128, 1], F32), "oh": ("sbuf", [128, N], BF), "keep": ("sbuf", [128, 128], BF),
+    "negc": ("sbuf", [128, 1], F32), "dm": ("sbuf", [128, 56], F32), "raw": ("sbuf", [128, PITCH], BF), "rawt": ("sbuf", [128, PITCH], BF),
+    "eb": ("sbuf", [128, 1], F32), "tb": ("sbuf", [128, 1], F32), "ini": ("sbuf", [128, 1], F32),
+    "cv": ("sbuf", [128, 2], F32), "cot": ("sbuf", [128, 2], U16),
+    "zz": ("sbuf", [128, 192], BF), "sv0": ("sbuf", [128, 128], F32), "sv": ("sbuf", [128, 128], BF),
+    "e": ("sbuf", [128, 128], BF), "cu": ("sbuf", [128, 128], BF), "ct": ("sbuf", [128, 128], BF), "rk": ("sbuf", [128, 64], BF),
+    "po": ("sbuf", [128, 8], U16), "win": ("sbuf", [128, WIN], BF), "tw": ("sbuf", [128, WIN], BF),
+    "ev2": ("sbuf", [128, 1], F32), "sot": ("sbuf", [128, 4], U16),
+    "ab": ("sbuf", [128, 8 * N], F16), "z": ("sbuf", [128, 48], F32), "c3": ("sbuf", [128, 2], F32), "cr": ("sbuf", [128, 2], F32),
+    "cx": ("sbuf", [128, 2], F32), "co": ("sbuf", [128, 32], U16),
+    "x2": ("sbuf", [128, 64], BF), "x2t": ("sbuf", [128, 64], BF), "l1": ("sbuf", [128, 1], F32), "l2": ("sbuf", [128, 1], F32),
+    "fot": ("sbuf", [128, 4], U16), "x3": ("sbuf", [128, 64], BF), "x3t": ("sbuf", [128, 4, 16], BF), "fo": ("sbuf", [128, 16], U16),
+    "kr": ("sbuf", [128, 8 * N], F16), "kofs": ("sbuf", [128, 10], U16), "rofs": ("sbuf", [128, 16], U16),
     "tab": ("sbuf", [128, TAB], BF), "d_s": ("sbuf", [128, RL + 32], BF), "t_s": ("sbuf", [128, 2 * N + 2, 32], BF),
     "mx1": ("sbuf", [128, 4 * N + 2], F32), "mx2": ("sbuf", [128, 48], F32), "so": ("sbuf", [128, 32], U16),
     "pk_q": ("sbuf", [128, SL - CAP], F8), "pk_s": ("sbuf", [128, SL - CAP], "uint8"),
@@ -48,7 +47,7 @@ SCRATCH = {
     "fp_q": ("sbuf", [128, S], F8), "fp_s": ("sbuf", [128, S], "uint8"),
     "ps": ("psum", [128, 2048], F32), "yb": ("sbuf", [128, S * O], F32),
 }
-SEMAPHORES = ["v", "a", "t", "gi", "ld_x", "ld_w", "ld_t", "ld_f", "kr", "q1", "s1", "q2", "s2", "out", "st"]
+SEMAPHORES = ["v", "a", "t", "gi", "ld_x", "ld_w", "ld_t", "kw", "kr", "q1", "s1", "q2", "s2", "out", "st"]
 
 
 def rank_program(g, core, T, topo):
@@ -93,29 +92,29 @@ def rank_program(g, core, T, topo):
     def same_die(a, b):
         return topo.die(T.cores[a]) == topo.die(T.cores[b])
 
-    def order(a):
-        near = [(a + i) % N for i in range(1, N) if same_die(a, (a + i) % N)]
-        far = [(a + i) % N for i in range(1, N) if not same_die(a, (a + i) % N)]
-        return far[:1] + near[:1] + far[1:2] + near[1:2] + far[2:] + near[2:]
+    bits = sorted((1, 2, 4), key=lambda b: same_die(0, b))
+    weight = {b: 1 << k for k, b in enumerate(bits)}
 
-    def spread(a, ranks, swap):
-        every = topo.engines(T.cores[a], T.cores[ranks[0]])
-        free = (every[1::2] + every[0::2])[::-1 if swap else 1]
+    def peer(w):
+        return me ^ sum(b for b in bits if w & weight[b])
+
+    every = topo.engines(core, T.cores[peer(1)])
+    ends = every[1::2] + every[0::2]
+
+    def spread(seats, swap):
+        free = ends[::-1 if swap else 1]
         out = {}
-        for k, q in enumerate(sorted(ranks, key=lambda q: same_die(a, q))):
-            n = len(every) // 4 * (2 if len(ranks) == 3 and k == 2 else 1)
-            out[q], free = free[:n], free[n:]
+        for k, w in enumerate(sorted(seats, key=lambda w: same_die(me, peer(w)))):
+            n = len(every) // len(seats) if len(seats) != 3 else len(every) // 4 * (2 if k == 2 else 1)
+            out[w], free = free[:n], free[n:]
         return out
 
     def send(plan, src, dst, s):
-        g.remote_dma_fused([RemoteDMATransfer(dst_ids=[DstId(rid=topo.addr(T.cores[q])[0], pnc=topo.addr(T.cores[q])[1])],
-                                              dma_engine_mask=sum(1 << e for e in es), remote_sem=sem[s], src=src(q), dst=dst(q))
-                            for q, es in plan(me).items()], local_sem=sem.out)
-        sent[0] += sum(len(es) for es in plan(me).values())
-        lands[s] = lands.get(s, 0) + sum(len(plan(a).get(me, [])) for a in range(N))
-
-    def at(q):
-        return order(q).index(me) + 1
+        g.remote_dma_fused([RemoteDMATransfer(dst_ids=[DstId(rid=topo.addr(T.cores[peer(w)])[0], pnc=topo.addr(T.cores[peer(w)])[1])],
+                                              dma_engine_mask=sum(1 << e for e in es), remote_sem=sem[s], src=src(w), dst=dst(w))
+                            for w, es in plan.items()], local_sem=sem.out)
+        sent[0] += sum(len(es) for es in plan.values())
+        lands[s] = lands.get(s, 0) + sum(len(es) for es in plan.values())
 
     def codes(out, win, off):
         return V(vec.tensor_copy(out.bitcast(dt.uint32), win.bitcast(dt.uint32).indirect(off)))
@@ -123,259 +122,238 @@ def rank_program(g, core, T, topo):
     def scales(out, win, off):
         return C(act.activation(out, win.indirect(off), F.Copy))
 
-    def slot(i):
-        return slice(16 + CAP * i, 16 + CAP * i + CAP)
+    def slot(w):
+        return slice(16 + CAP * w, 16 + CAP * w + CAP)
 
-    def part(i):
-        return slice(CAP * (i - 1), CAP * i)
+    def part(w):
+        return slice(CAP * (w - 1), CAP * w)
+
+    def back(w):
+        return slice(16 + PITCH * w, PITCH * (w + 1))
 
     def iota(ap, pattern, base, cm=0, small=True):
         (g.iota(ap, pattern, base, cm, allow_small_or_imprecise_dtypes=True) if small else g.iota(ap, pattern, base, cm)).then_inc(sem.gi, 1)
 
     for b in range(4):
         (syn if b < 2 else act).dma_start(T.kt[quad(b)], (T.ky if b < 2 else T.lk)[:]).then_inc(sem.ld_t, 16)
-    iota(T.pio[:], [[0, 1]], 0, 1, small=False)
-    iota(T.cq0[:], [[0, 4], [1 - N, 2], [1, 8]], 0)
-    iota(T.cc0[:], [[16, 8], [1, 8], [128, 2]], 0)
-    iota(T.win[:], [[0, WIN // 16], [1, 16]], K + 16 * me)
-    iota(T.sv0[:, 16 * me:128], [[CAP, N - me], [1, 16]], 16 - MID, 1)
-    if me:
-        iota(T.sv0[:, 0:16 * me], [[CAP, me], [1, 16]], 16 - MID + CAP * (N - me), 1)
-    G_P, G_CQ, G_CC, G_WIN, G_SV = 1, 2, 3, 4, 6 if me else 5
-    i_kf = V(vec.memset(T.kf[:], 0))
-    V(vec.memset(T.e[:], 0.0))
-    aw(i_kf, "v")
-    sw(i_kf, "v")
-    for b in range(4):
-        (syn if b < 2 else act).dma_start(T.kf[32 * b + 1:32 * b + 32:16, :], (T.ky if b < 2 else T.lk)[:]).then_inc(sem.ld_f, 16)
     syn.dma_start(T.xb[:], T.x[:]).then_inc(sem.ld_x, 16)
     syn.dma_start(T.wb[:], T.w[:]).then_inc(sem.ld_w, 16)
+    iota(T.pio[:], [[0, 1]], 0, 1 + 2 ** 8 + 2 ** 16, small=False)
+    iota(T.seat[:], [[-weight[b] if me & b else weight[b], 2] for b in (4, 2, 1)], sum(weight[b] for b in bits if me & b))
+    iota(T.c16[:], [[16, 8]], 0)
+    iota(T.pat[:], [[0, 8], [1, 16]], 16 * me - K)
+    iota(T.sv0[:], [[CAP, N], [1, 16]], 16 - MID, 1)
+    iota(T.cfo[:], [[16, 2], [0, 2]], 0)
+    iota(T.tab[:, 0:TAB // 2], [[0, TAB // 2]], -MID)
+    G_P, G_SEAT, G_C16, G_PAT, G_SV, G_CFO, G_TAB = range(1, 8)
 
+    lanef, od, par, cb, h3, own = (T.cf[:, k:k + 1] for k in range(6))
+    V(vec.memset(T.zz[:], 0.0))
+    V(vec.memset(T.pp[:], 0.0))
+    V(vec.memset(T.dm[:], 4.0 * K))
     vw(G_P, "gi")
-    V(vec.tensor_scalar(T.lane[:], T.pio[:], 15, None, A.bitwise_and))
-    i = V(vec.tensor_scalar(T.hh[:], T.pio[:], 4, 1, A.logical_shift_right, A.bitwise_and))
-    i_zz = V(vec.memset(T.zz[:], 0.0))
+    for k, sh, mask in ((6, 3, BIG + 2), (0, 0, 15), (1, 4, 1), (2, 0, 1), (3, 1, 128 + 15), (4, 3, 1), (5, 1, N - 1)):
+        i = V(vec.tensor_scalar(T.ci[:, k:k + 1], T.pio[:], sh, mask, A.logical_shift_right, A.bitwise_and))
+    vw(i - 6)
+    V(vec.tensor_scalar(T.val[:], T.ci[:, 6:7], -1.0, BIG + 1.0, A.mult, A.add))
     vw(i)
-    i = V(vec.tensor_scalar(T.h3[:], T.lane[:], 8.0, None, A.is_ge))
-    vw(G_CQ, "gi")
-    i_cq = V(vec.tensor_scalar(T.cqn[:], T.cq0[:], -1.0, None, A.mult))
-    i_od = V(vec.tensor_copy(T.od[:], T.hh[:]))
-    vw(i)
-    V(vec.tensor_scalar(T.c64[:], T.cq0[:, 0:8:2], T.h3[:, 0:1], None, A.add))
-    vw(i_cq)
-    V(vec.tensor_tensor(T.cq[:], T.cq0[:], T.cqn[:], A.max))
-    i_lane = V(vec.tensor_copy(T.lanef[:], T.lane[:]))
-    aw(i_od, "v")
+    i_cf = V(vec.tensor_copy(T.cf[:], T.ci[:, 0:6]))
+    aw(i_cf, "v")
     for b, n, sh in ((0, 1, 0), (1, 1, 16), (2, 2, 0)):
-        i = C(act.activation(T.tb[quad(b, n)], T.od[quad(b, n)], F.Identity, bias=float(sh - WIN // 2 - 1), scale=float(PITCH - CAP - 2 * sh + 1)))
-    i = C(act.activation(T.od8[:], T.od[:], F.Identity, scale=8.0))
-    aw(i_lane, "v")
-    aw(i - 1)
-    C(act.activation(T.ini[:], T.lanef[:], F.Identity, bias=T.tb[:, 0:1], scale=float(PITCH // 2)))
+        i = C(act.activation(T.tb[quad(b, n)], T.cf[quad(b, n), 1:2], F.Identity, bias=float(sh - WIN // 2 - 1 - PITCH // 2), scale=float(CAP + 1)))
+    C(act.activation(T.keep[:], T.zz[:, 0:128], F.Identity, bias=par))
     aw(i)
-    i = C(act.activation(T.b8[:], T.lanef[:], F.Identity, bias=T.od8[:, 0:1], scale=float(-S)))
-    aw(G_CC, "gi")
+    C(act.activation(T.ini[:], lanef, F.Identity, bias=T.tb[:, 0:1], scale=float(PITCH // 2)))
+    aw(G_C16, "gi")
+    a_pp = C(act.activation(T.pp[:, 0:128:16], T.c16[:], F.Identity, bias=cb))
+    I_K16 = i_cf + 3
+    aw(I_K16, "v")
+    a_e = C(act.activation(T.e[:, 64:128], T.oh[:, 0:N].indirect(T.k16[:, 4:8]), F.Copy))
+    i = C(act.activation(T.negc[:], lanef, F.Identity, bias=float(-K - 16 * me), scale=-1.0))
+    aw(G_PAT, "gi")
+    for c0 in range(0, WIN, 128):
+        a_win = C(act.activation(T.win[:, c0:c0 + 128], T.pat[:], F.Identity, bias=float(K), scale=h3))
     aw(i)
-    a_cc = C(act.activation(T.cc[:], T.cc0[:], F.Identity, bias=T.b8[:, 0:1]))
-    i = C(act.activation(T.cv[:], T.cq0[:, 0:2], F.Identity, bias=T.lanef[:, 0:1], scale=16.0))
-    I_EQ = i_lane + 4
-    aw(I_EQ, "v")
-    a_big = C(act.activation(T.big[:], T.e[:, 0:128:2], F.Identity, scale=2.0 * WIN))
-    aw(i)
-    i = C(act.activation(T.cm[:], T.cv[:], F.Sign, bias=3 * me - 24.5))
+    a_dm = C(act.activation(T.dm[:, 0:56:4], T.zz[:, 0:14], F.Identity, bias=T.negc[:, 0:1]))
+    i = C(act.activation(T.cv[:], T.c16[:, 0:2], F.Identity, bias=lanef))
+    aw(a_dm)
+    C(act.activation(T.dm[:, 48:56], T.dm[:, 48:56], F.Identity, bias=16.0 * (me - peer(N - 1))))
     for b, n, sh in ((0, 1, 0), (1, 1, 1), (2, 2, 0)):
-        C(act.activation(T.eb[quad(b, n)], T.od[quad(b, n)], F.Identity, bias=float(1 + sh), scale=-1.0))
+        C(act.activation(T.eb[quad(b, n)], T.cf[quad(b, n), 1:2], F.Identity, bias=float(1 + sh), scale=-1.0))
     aw(i)
-    for m in range(2):
-        i = C(act.activation(T.cw[:, m:m + 1], T.cm[:, m:m + 1], F.Identity, bias=T.cv[:, m:m + 1], scale=-12.0))
-    aw(i)
-    i = C(act.activation(T.c3[:], T.cw[:], F.Identity, bias=(3 * me - 14) / 3, scale=1.0 / 3))
-    C(act.activation(T.ev2[:], T.od[:], F.Identity, bias=2.0, scale=-2.0))
+    i = C(act.activation(T.c3[:], T.cv[:], F.Identity, bias=-2.0 / 3, scale=1.0 / 3))
+    C(act.activation(T.ev2[:], od, F.Identity, bias=2.0, scale=-2.0))
+    i_l1 = C(act.activation(T.l1[:], lanef, F.Identity, bias=od, scale=2.0))
     aw(i)
     i = C(act.activation(T.cr[:], T.c3[:], F.Identity, bias=WHOLE))
-    C(act.activation(T.l2[:], T.lanef[:], F.Identity, bias=T.od[:, 0:1], scale=2.0))
+    C(act.activation(T.d_s[:, 16 + RL:32 + RL], T.zz[:, 0:16], F.Identity, bias=float(-MID)))
+    aw(i_l1)
+    C(act.activation(T.l2[:], h3, F.Identity, bias=T.l1[:, 0:1], scale=16.0))
     aw(i)
     for m in range(2):
-        a_cx = C(act.activation(T.cx[:, m:m + 1], T.cr[:, m:m + 1], F.Identity, bias=T.cw[:, m:m + 1]))
-    C(act.activation(T.x2[:], T.zz[:, 0:32], F.Copy))
-    a_z = C(act.activation(T.z[:], T.zz[:, 0:40], F.Copy))
-    for ap in (T.d_s[:, 0:16], T.d_s[:, 16 + RL:32 + RL], T.mx2[:, 32:48]):
-        C(act.activation(ap, T.zz[:, 0:16], F.Identity, bias=float(-MID)))
-    for c0 in range(0, TAB, TAB // 4):
-        C(act.activation(T.tab[:, c0:c0 + TAB // 4], T.zz[:], F.Identity, bias=float(-MID)))
+        a_cx = C(act.activation(T.cx[:, m:m + 1], T.cr[:, m:m + 1], F.Identity, bias=T.cv[:, m:m + 1]))
+    C(act.activation(T.tab[:, TAB // 2:TAB // 2 + 128], T.zz[:, 0:128], F.Identity, bias=float(-MID)))
+    for c0, c1 in ((256, 416), (416, 576)):
+        C(act.activation(T.tab[:, TAB // 2 + c0:TAB // 2 + c1], T.zz[:, 0:c1 - c0], F.Identity, bias=float(-MID)))
     aw(G_SV, "gi")
     for b, u in enumerate((2, 1, 0, -1)):
         a_tab = C(act.activation(T.sv[quad(b)], T.sv0[quad(b)], F.Identity, bias=float(16 * u - 32 * b)))
 
-    V(vec.tensor_scalar(T.lane8[:], T.lane[:], 8.0, None, A.mult))
     vw(64, "ld_t")
     i = V(vec.tensor_scalar(T.ko[:], T.kt[:], N - 1, None, A.bitwise_and))
-    vw(i - 1)
-    V(vec.tensor_scalar(T.turn[:], T.cq0[:, 0:8], T.lane8[:, 0:1], None, A.add))
+    vw(i_cf)
+    vw(G_SEAT, "gi")
+    V(vec.tensor_scalar(T.oh[:], T.seat[:], own, T.val[:, 0:1], A.is_equal, A.mult))
     vw(i)
-    i = V(vec.tensor_tensor(T.e[:, 0:128:2], T.ko[:, 0:8].indirect(T.c64[:, 0:4]), T.cq[:], A.is_equal))
-    assert i == I_EQ
-    vw(64, "ld_f")
-    V(vec.tensor_scalar(T.kp[:, 0:64], T.kf[:, 0:64], 3, K - 1, A.logical_shift_right, A.bitwise_and))
+    i = V(vec.tensor_copy(T.k16[:], T.ko[:]))
+    assert i == I_K16
+    V(vec.tensor_scalar(T.kp[:, 1:16:2], T.kt[:], 3, 255, A.logical_shift_right, A.bitwise_and))
     vw(i)
-    i = V(vec.transpose(T.ef[:], T.e[:]))
-    i_pl = V(vec.tensor_scalar(T.kp[:, 64:128], T.kf[:, 64:128], 3, K - 1, A.logical_shift_right, A.bitwise_and))
+    i = V(vec.tensor_copy(T.e[:, 0:64], T.oh[:, 0:N].indirect(T.k16[:, 0:4])))
+    i_kp = V(vec.tensor_scalar(T.kp[:, 0:16:2], T.kt[:], 3, K - 256, A.logical_shift_right, A.bitwise_and))
     vw(i)
-    vw(a_cc, "a")
-    i = V(vec.tensor_tensor_scan(T.cu[:], T.ef[:], T.zz[:, 0:128], T.ini[:, 0:1], A.add, A.add))
-    vw(i_pl)
-
-    def places(m0, m1):
-        c = slice(16 * m0, 16 * m1)
-        V(vec.tensor_tensor(T.pl[:, c], T.kp[:, 0:128].indirect(T.turn[:, m0:m1]), T.cc[:, c], A.max))
-    places(0, 4)
+    vw(a_e, "a")
+    i = V(vec.tensor_tensor_scan(T.cu[:], T.keep[:], T.e[:], T.ini[:, 0:1], A.mult, A.add))
+    vw(i_kp)
+    i_pp = V(vec.tensor_copy(T.pp[:, HI:128:LO - HI], T.kp[:]))
     vw(i)
     i = V(vec.transpose(T.ct[:], T.cu[:]))
-    places(4, 6)
+    vw(i_pp)
+    vw(a_pp, "a")
+    V(vec.transpose(T.pl[:], T.pp[:]))
     vw(i)
-    vw(a_big, "a")
-    i = V(vec.tensor_tensor_scan(T.rk[:], T.big[:], T.ct[:, 0:128:2], 0.0, A.add, A.min))
-    places(6, 8)
-    vw(i)
-    V(vec.tensor_scalar(T.po[:, 0:8:2], T.rk[:, 7:64:16], float(WIN // 2), None, A.add))
-    i = V(vec.tensor_scalar(T.po[:, 1:8:2], T.rk[:, 15:64:16], -1.0, float(WIN // 2), A.mult, A.add))
+    i_rk = V(vec.tensor_tensor_scan(T.rk[:], T.ct[:, 0:128:2], T.ct[:, 1:128:2], 0.0, A.add, A.min))
+
+    def empty(k):
+        V(vec.memset(T.tab[:, TAB // 2 + 128 * k:TAB // 2 + 128 * (k + 1)], float(-MID)))
+    V(vec.memset(T.z[:], 0.0))
+    V(vec.memset(T.x2[:], 0.0))
+    vw(i_rk)
+    i = V(vec.tensor_scalar(T.po[:], T.rk[:, 7:64:8], float(WIN // 2), None, A.add))
+    empty(1)
 
     vw(i)
-    vw(G_WIN, "gi")
+    vw(a_win, "a")
     i = V(vec.tensor_copy(T.win[:, 0:WIN].indirect(T.po[:, 0:8]), T.pl[:]))
-    vw(a_z, "a")
-    V(vec.tensor_scalar(T.cot[:], T.cx[:], T.eb[:, 0:1], 3 * me - 13 - WHOLE, A.add, A.add))
-    vw(i)
-
-    def steps(a):
-        o = N // 2 if a < N // 2 else 0
-        return [(o, o + 1), (o + 1, o + N // 2), (N // 2 - o, N - o)]
-
-    def turned(q0, q1):
-        return V(vec.transpose(T.tw[:, 2 * q0:2 * q1, :], T.win[:, PITCH * q0:PITCH * q1]))
-
-    def two(q):
-        return T.ab[:, 2 * q:2 * q + 2]
-
-    def met(q0, q1, i_t):
-        vw(i_t)
-        return V(vec.tensor_tensor(T.ab[:, 2 * q0:2 * q1], T.tw[:, 2 * q0:2 * q1, 1], T.tw[:, 2 * q0:2 * q1, 17], A.min))
-
-    def deal(a, k):
-        other = list(range(steps(a)[0][0], steps(a)[1][1]))
-        own = [q for q in order(a) if q not in other]
-        every = topo.engines(T.cores[a], T.cores[other[0]])
-        four = [(every[1::2] + every[0::2])[4 * n:4 * n + 4] for n in range(4)]
-        return [{other[0]: four[0]}, {other[1]: four[1], other[2]: four[2], other[3]: four[0]},
-                {own[0]: four[3], own[1]: four[1], own[2]: four[2]}][k]
-
-    def lists(k, i):
-        gw(i, "v")
-        send(lambda a: deal(a, k), two, lambda q: T.kr[:, (at(q) + q) % N, 0:2], "kr")
-    q0, q1 = steps(me)[1]
-    i = turned(*steps(me)[0])
-    turned(q0, q0 + 1)
-    lists(0, met(*steps(me)[0], i))
-    i = turned(q0 + 1, q1)
-    i_t = turned(*steps(me)[2])
-    lists(1, met(q0, q1, i))
-    V(vec.tensor_scalar(T.x2[:, 0:8], T.po[:], float(-WIN // 2), None, A.add))
-    lists(2, met(*steps(me)[2], i_t))
-    for po, c0, pi in ((quad(0, 2), 1, quad(0, 2)), (quad(0), 0, quad(1)), (quad(1), 2, quad(0))):
-        i = V(vec.tensor_tensor(T.z[po, c0:c0 + 2 * NB:2], T.tw[pi, :, 0], T.tw[pi, :, 16], A.min))
+    gw(i, "v")
+    send({N - 1: ends[0:8]}, lambda w: T.win[:, PITCH * w:PITCH * (w + 1)], lambda w: T.raw[:], "kw")
     vw(16, "ld_x")
     V(vec.quantize_mx(T.xq[:, 0:128], T.xs[:, 0:128], T.xb[:, 0:512]))
     vw(i)
-    i = V(vec.tensor_scalar(T.co[:], T.z[:, 0:40].indirect(T.cot[:, 0:2]), float(S - 1), None, A.min))
+
+    def met(out, fill, turned):
+        return V(vec.tensor_tensor_scan(out, fill, turned, 0.0, A.min, A.add))
+    i = V(vec.transpose(T.tw[:], T.win[:]))
+    vw(a_cx, "a")
+    V(vec.tensor_scalar(T.cot[:], T.cx[:], T.eb[:, 0:1], -1 - WHOLE, A.add, A.add))
+    vw(i)
+    gw(met(T.ab[:, 8:56], T.dm[:, 0:48], T.tw[:, PITCH + HI:PITCH * (N - 1):LO - HI]), "v")
+    for seats, swap in (((1, 3, 5), False), ((2, 4, 6), True)):
+        send(spread(seats, swap), lambda w: T.ab[:, 8 * w + 3:8 * w + 8], lambda w: T.kr[:, 8 * w + 3:8 * w + 8], "kr")
+    for po, c0, pi in ((quad(0, 2), 1, quad(0, 2)), (quad(0), 0, quad(1)), (quad(1), 2, quad(0))):
+        i = V(vec.tensor_tensor(T.z[po, c0:c0 + 2 * NB:2], T.tw[pi, 0:WIN:32], T.tw[pi, 16:WIN:32], A.min))
     V(vec.quantize_mx(T.xq[:, 128:256], T.xs[:, 128:256], T.xb[:, 512:1024]))
     vw(i)
+    i = V(vec.tensor_scalar(T.co[:], T.z[:, 0:48].indirect(T.cot[:, 0:2]), float(S - 1), None, A.min))
+    i_kr = met(T.kr[:, 0:8], T.dm[:, 0:8], T.tw[:, HI:PITCH:LO - HI])
+    V(vec.memset(T.d_s[:, 0:16], float(-MID)))
+    vw(i)
     i_co = V(vec.tensor_copy(T.co[quad(2, 2)], T.co[quad(0, 2)]))
-    V(vec.tensor_copy(T.kr[:, me, 0:2], two(me)))
-    V(vec.tensor_scalar(T.fot[:], T.zz[:, 0:2], T.l2[:, 0:1], None, A.add))
+
+    def offsets(c0, w0, w1):
+        for j in (1, 0):
+            i = V(vec.tensor_copy(T.kofs[quad(2 - 2 * j, 2), c0:c0 + w1 - w0], T.kr[quad(0, 2), 8 * w0 + 4 * j + 3:8 * w1:8]))
+        return i
+
+    def enter(c0, w0, w1):
+        return V(vec.tensor_copy(T.tab[:, 0:TAB].indirect(T.kofs[:, c0:c0 + w1 - w0]), T.sv[:, 16 * w0:16 * w1]))
+    vw(i_kr)
+    offsets(0, 0, 1)
 
     vw(i_co)
     aw(i_co, "v")
-    for k0, k1 in ((FIRST, N - 1), (0, FIRST)):
-        off = T.co[:, 4 + 3 * k0:4 + 3 * k1]
-        i_pk = codes(T.pk_q[:, CAP * k0:CAP * k1], T.xq[:, 0:S], off)
-        a_pk = scales(T.pk_s[:, CAP * k0:CAP * k1], T.xs[:, 0:S], off)
 
-        def ahead(a):
-            return [(a + 1 + k) % N for k in range(k0, k1)]
-        gw(i_pk, "v")
-        send(lambda a: spread(a, ahead(a), False), lambda q: T.pk_q[:, part((q - me) % N)].bitcast(dt.uint8),
-             lambda q: T.in_q[:, slot(at(q))].bitcast(dt.uint8), "q1")
-        gw(a_pk, "a")
-        send(lambda a: spread(a, ahead(a), True), lambda q: T.pk_s[:, part((q - me) % N)], lambda q: T.in_s[:, slot(at(q))], "s1")
+    def pick(w0, w1):
+        off, to = T.co[:, 1 + 3 * w0:1 + 3 * w1], slice(CAP * (w0 - 1), CAP * (w1 - 1))
+        return codes(T.pk_q[:, to], T.xq[:, 0:S], off), scales(T.pk_s[:, to], T.xs[:, 0:S], off)
 
+    def columns(w0, w1, picked):
+        gw(picked[0], "v")
+        send(spread(range(w0, w1), False), lambda w: T.pk_q[:, part(w)].bitcast(dt.uint8), lambda w: T.in_q[:, slot(w)].bitcast(dt.uint8), "q1")
+        gw(picked[1], "a")
+        send(spread(range(w0, w1), True), lambda w: T.pk_s[:, part(w)], lambda w: T.in_s[:, slot(w)], "s1")
+    columns(5, N, pick(5, N))
+    pick(3, 5)
+    vw(lands["kw"], "kw")
+    i = V(vec.transpose(T.rawt[:], T.raw[:]))
+    columns(1, 5, pick(1, 3))
     a_own = scales(T.in_s[:, 0:64], T.xs[:, 0:S], T.co[:, 0:4])
-    i_own1 = codes(T.in_q[:, 0:64], T.xq[:, 0:S], T.co[:, 0:4])
+    for gg in range(2):
+        for c0 in (0, 16):
+            a_x2 = C(act.activation(T.x2[:, 32 * gg + c0:32 * gg + c0 + 4], T.rk[:, 7 + 8 * gg:64:16], F.Copy))
 
-    vw(i_co + 1)
+    vw(i)
+    i = met(T.kr[:, 56:64], T.dm[:, 48:56], T.rawt[:, HI:PITCH:LO - HI])
     vw(a_tab, "a")
+    vw(G_TAB, "gi")
+    enter(0, 0, 1)
+    vw(i)
     vw(lands["kr"], "kr")
-    for j in (1, 0):
-        i = V(vec.tensor_copy(T.kofs[quad(2 - 2 * j, 2)], T.kr[quad(0, 2), :, j]))
+    i = offsets(2, 1, N)
     for b in (0, 2):
-        V(vec.tensor_copy(T.rofs[quad(b, 2)], T.kr[quad(2, 2), :, 0:2]))
+        V(vec.tensor_copy(T.rofs[quad(b, 2)], T.kr[quad(2, 2), 3:8 * N:4]))
     vw(i)
-    i = V(vec.tensor_copy(T.tab[:, 0:TAB].indirect(T.kofs[:, 0:8]), T.sv[:]))
+    i = enter(2, 1, N)
     aw(i, "v")
-    a_g = C(act.activation(T.d_s[:, 16 + RL // 2:16 + RL], T.tab[:, 0:TAB].indirect(T.rofs[:, 8:16]), F.Copy))
-    V(vec.tensor_scalar(T.sot[:], T.cx[:], T.ev2[:, 0:1], 3 * me - 13 - WHOLE, A.add, A.add))
+    a_g = C(act.activation(T.d_s[:, 16 + 32 * RV:16 + RL], T.tab[:, 0:TAB].indirect(T.rofs[:, 2 * RV:16]), F.Copy))
+    i_own1 = codes(T.in_q[:, 0:64], T.xq[:, 0:S], T.co[:, 0:4])
     vw(i)
-    i = V(vec.tensor_copy(T.d_s[:, 16:16 + RL // 2], T.tab[:, 0:TAB].indirect(T.rofs[:, 0:8])))
-    i_f = V(vec.tensor_scalar(T.x2[:, 16:24], T.po[:], float(-WIN // 2), None, A.add))
-    vw(i)
-    vw(a_g, "a")
-    V(vec.transpose(T.t_s[:, 0:2 * N + 2:2, :], T.d_s[:]))
-    i = V(vec.transpose(T.t_s[:, 1:2 * N:2, :], T.d_s[:, 16:16 + RL]))
-    vw(i_f)
+    i = V(vec.tensor_copy(T.d_s[:, 16:16 + 32 * RV], T.tab[:, 0:TAB].indirect(T.rofs[:, 0:2 * RV])))
+    vw(G_CFO, "gi")
+    vw(a_x2, "a")
     V(vec.transpose(T.x2t[:], T.x2[:]))
+    aw(V(vec.tensor_scalar(T.fot[:], T.cfo[:], T.l2[:, 0:1], None, A.add)), "v")
+    a_x3 = C(act.activation(T.x3[:], T.x2t[:, 0:64].indirect(T.fot[:, 0:4]), F.Copy))
+    vw(i)
+    V(vec.transpose(T.t_s[:, 0:2 * RV:2, :], T.d_s[:, 0:32 * RV]))
+    V(vec.transpose(T.t_s[:, 1:2 * RV:2, :], T.d_s[:, 16:16 + 32 * RV]))
+    vw(a_g, "a")
+    V(vec.transpose(T.t_s[:, 2 * RV:2 * N + 2:2, :], T.d_s[:, 32 * RV:RL + 32]))
+    i = V(vec.transpose(T.t_s[:, 2 * RV + 1:2 * N:2, :], T.d_s[:, 16 + 32 * RV:16 + RL]))
+    V(vec.tensor_scalar(T.sot[:, 0:4:2], T.cx[:], T.ev2[:, 0:1], -1 - WHOLE, A.add, A.add))
     vw(i)
     i = V(vec.tensor_tensor(T.mx1[quad(0, 2)], T.t_s[quad(0, 2), 0:2 * N + 1, 0:32:16], T.t_s[quad(2, 2), 0:2 * N + 1, 0:32:16], A.max))
+    V(vec.memset(T.mx2[:, 34:48], float(-MID)))
     vw(i)
     for b in range(4):
         i = V(vec.tensor_tensor(T.mx2[quad(b), 0:4 * N + 2], T.mx1[quad(0)], T.mx1[quad(1)], A.max))
     vw(i)
-    i_so = V(vec.tensor_scalar(T.so[:], T.mx2[:, 0:48].indirect(T.sot[:, 0:2]), float(MID), float(LAND - 1), A.add, A.min))
-    i_f = V(vec.tensor_copy(T.x3[:], T.x2t[:, 0:32].indirect(T.fot[:, 0:2])))
+    i_so = [V(vec.tensor_scalar(T.so[:, 16 * m:16 * m + 16], T.mx2[:, 0:48].indirect(T.sot[:, 2 * m:2 * m + 1]), float(MID), float(LAND - 1), A.add, A.min))
+            for m in (1, 0)]
+    vw(a_x3, "a")
+    i_x3 = V(vec.transpose(T.x3t[:], T.x3[:]))
 
-    vw(max(i_so, i_own1))
     vw(lands["q1"], "q1")
-    aw(i_so, "v")
     aw(a_own)
     aw(lands["s1"], "s1")
-
-    def answer(buf, r):
-        return buf[:, part(order(me).index(r) + 1)]
-
-    def back(buf, r):
-        c0 = 16 + PITCH * ((me - r) % N)
-        return buf[:, c0:c0 + CAP]
-    for k0, k1 in ((FIRST, N - 1), (0, FIRST)):
-        off = T.so[:, 4 + 3 * k0:4 + 3 * k1]
-        i_p2 = codes(T.p2_q[:, CAP * k0:CAP * k1], T.in_q[:, 0:LAND], off)
-        a_p2 = scales(T.p2_s[:, CAP * k0:CAP * k1], T.in_s[:, 0:LAND], off)
+    for w0, w1 in PARTS:
+        vw(i_so[1 + 3 * w0 < 16])
+        aw(i_so[1 + 3 * w0 < 16], "v")
+        off, to = T.so[:, 1 + 3 * w0:1 + 3 * w1], slice(CAP * (w0 - 1), CAP * (w1 - 1))
+        i_p2 = codes(T.p2_q[:, to], T.in_q[:, 0:LAND], off)
+        a_p2 = scales(T.p2_s[:, to], T.in_s[:, 0:LAND], off)
         gw(i_p2, "v")
-        send(lambda a: spread(a, order(a)[k0:k1], False), lambda r: answer(T.p2_q, r).bitcast(dt.uint8),
-             lambda r: back(T.bk_q, r).bitcast(dt.uint8), "q2")
+        send(spread(range(w0, w1), False), lambda w: T.p2_q[:, part(w)].bitcast(dt.uint8), lambda w: T.bk_q[:, back(w)].bitcast(dt.uint8), "q2")
         gw(a_p2, "a")
-        send(lambda a: spread(a, order(a)[k0:k1], True), lambda r: answer(T.p2_s, r), lambda r: back(T.bk_s, r), "s2")
-    vw(i_f)
-    i = V(vec.transpose(T.x3t[:], T.x3[:]))
-    i_own2 = codes(T.bk_q[:, 0:64], T.in_q[:, 0:LAND], T.so[:, 0:4])
-    a_own2 = scales(T.bk_s[:, 0:64], T.in_s[:, 0:LAND], T.so[:, 0:4])
-    vw(i)
-    i = V(vec.tensor_scalar(T.fom[:], T.x3t[:, :, 0:8], float(PITCH * me - WIN // 2), float(WIN), A.is_lt, A.mult))
-    vw(16, "ld_w")
-    V(vec.quantize_mx(T.wq[:, 0:128], T.ws[:, 0:128], T.wb[:, 0:512]))
-    vw(i)
-    i = V(vec.tensor_tensor(T.fos[:], T.x3t[:, :, 0:8], T.fom[:], A.add))
-    V(vec.quantize_mx(T.wq[:, 128:256], T.ws[:, 128:256], T.wb[:, 512:1024]))
-    vw(i)
+        send(spread(range(w0, w1), True), lambda w: T.p2_s[:, part(w)], lambda w: T.bk_s[:, back(w)], "s2")
+    vw(i_x3)
     for b in (0, 2):
-        i_fo = V(vec.tensor_scalar(T.fo[quad(b, 2)], T.fos[quad(2, 2)], float(WIN // 2 + 16 - PITCH * me), None, A.add))
+        for h in range(2):
+            i_fo = V(vec.tensor_scalar(T.fo[quad(b, 2), h:16:2], T.x3t[quad(2, 2), 2 * h:2 * h + 2, 0:4], float(WIN // 2 + 16), None, A.add))
+    i_own2 = codes(T.bk_q[:, 0:PITCH], T.in_q[:, 0:LAND], T.so[:, 0:4])
+    a_own2 = scales(T.bk_s[:, 0:PITCH], T.in_s[:, 0:LAND], T.so[:, 0:4])
+    vw(16, "ld_w")
+    V(vec.quantize_mx(T.wq[:], T.ws[:], T.wb[:]))
 
     vw(max(i_own2, i_fo))
     vw(lands["q2"], "q2")

from concourse.bass import DstId, RemoteDMATransfer
from concourse.mybir import dt, AluOpType, ActivationFunctionType

N, S, CAP, K, O = 8, 256, 48, 1024, 2
SL = N * CAP
PITCH = CAP + 16
WIN = N * PITCH
NB = WIN // 32
LAND = SL + 16
MID = LAND // 2
TAB = K + 16 * N
RL = N * 32
RV = 3
WHOLE = 3.0 * 2 ** 22
PARTS = ((7, 8), (5, 7), (1, 5))
BIG = 2 ** 13
LO, HI = 12, 4
F8, F32, BF, F16, I32, U16 = "float8_e4m3fn_x4", "float32", "bfloat16", "float16", "int32", "uint16"

SCRATCH = {
    "xb": ("sbuf", [128, 4 * S], BF), "wb": ("sbuf", [128, 512 * O], BF),
    "xq": ("sbuf", [128, S], F8), "xs": ("sbuf", [128, S], "uint8"),
    "wq": ("sbuf", [128, 128 * O], F8), "ws": ("sbuf", [128, 128 * O], "uint8"),
    "kt": ("sbuf", [128, 8], I32), "ko": ("sbuf", [128, 8], I32), "k16": ("sbuf", [128, 8], U16),
    "kp": ("sbuf", [128, 16], I32), "pp": ("sbuf", [128, 128], BF), "pl": ("sbuf", [128, 128], BF),
    "pio": ("sbuf", [128, 1], I32), "ci": ("sbuf", [128, 7], I32), "cf": ("sbuf", [128, 6], F32),
    "seat": ("sbuf", [128, N], F32), "c16": ("sbuf", [128, 8], F32), "cfo": ("sbuf", [128, 4], F32), "pat": ("sbuf", [128, 128], F32),
    "val": ("sbuf", [128, 1], F32), "oh": ("sbuf", [128, N], BF), "keep": ("sbuf", [128, 128], BF),
    "negc": ("sbuf", [128, 1], F32), "dm": ("sbuf", [128, 56], F32), "raw": ("sbuf", [128, PITCH], BF), "rawt": ("sbuf", [128, PITCH], BF),
    "eb": ("sbuf", [128, 1], F32), "tb": ("sbuf", [128, 1], F32), "ini": ("sbuf", [128, 1], F32),
    "cv": ("sbuf", [128, 2], F32), "cot": ("sbuf", [128, 2], U16),
    "zz": ("sbuf", [128, 192], BF), "sv0": ("sbuf", [128, 128], F32), "sv": ("sbuf", [128, 128], BF),
    "e": ("sbuf", [128, 128], BF), "cu": ("sbuf", [128, 128], BF), "ct": ("sbuf", [128, 128], BF), "rk": ("sbuf", [128, 64], BF),
    "po": ("sbuf", [128, 8], U16), "win": ("sbuf", [128, WIN], BF), "tw": ("sbuf", [128, WIN], BF),
    "ev2": ("sbuf", [128, 1], F32), "sot": ("sbuf", [128, 4], U16),
    "ab": ("sbuf", [128, 8 * N], F16), "z": ("sbuf", [128, 48], F32), "c3": ("sbuf", [128, 2], F32), "cr": ("sbuf", [128, 2], F32),
    "cx": ("sbuf", [128, 2], F32), "co": ("sbuf", [128, 32], U16),
    "x2": ("sbuf", [128, 64], BF), "x2t": ("sbuf", [128, 64], BF), "l1": ("sbuf", [128, 1], F32), "l2": ("sbuf", [128, 1], F32),
    "fot": ("sbuf", [128, 4], U16), "x3": ("sbuf", [128, 64], BF), "x3t": ("sbuf", [128, 4, 16], BF), "fo": ("sbuf", [128, 16], U16),
    "kr": ("sbuf", [128, 8 * N], F16), "kofs": ("sbuf", [128, 10], U16), "rofs": ("sbuf", [128, 16], U16),
    "tab": ("sbuf", [128, TAB], BF), "d_s": ("sbuf", [128, RL + 32], BF), "t_s": ("sbuf", [128, 2 * N + 2, 32], BF),
    "mx1": ("sbuf", [128, 4 * N + 2], F32), "mx2": ("sbuf", [128, 48], F32), "so": ("sbuf", [128, 32], U16),
    "pk_q": ("sbuf", [128, SL - CAP], F8), "pk_s": ("sbuf", [128, SL - CAP], "uint8"),
    "in_q": ("sbuf", [128, LAND], F8), "in_s": ("sbuf", [128, LAND], "uint8"),
    "p2_q": ("sbuf", [128, SL - CAP], F8), "p2_s": ("sbuf", [128, SL - CAP], "uint8"),
    "bk_q": ("sbuf", [128, WIN], F8), "bk_s": ("sbuf", [128, WIN], "uint8"),
    "fp_q": ("sbuf", [128, S], F8), "fp_s": ("sbuf", [128, S], "uint8"),
    "ps": ("psum", [128, 2048], F32), "yb": ("sbuf", [128, S * O], F32),
}
SEMAPHORES = ["v", "a", "t", "gi", "ld_x", "ld_w", "ld_t", "kw", "kr", "q1", "s1", "q2", "s2", "out", "st"]


def rank_program(g, core, T, topo):
    me = T.rank_of(core)
    if me is None:
        return
    A = AluOpType
    F = ActivationFunctionType
    vec, act, ten, syn, sem = g.vector, g.scalar, g.tensor, g.sync, T.sem
    nv, na, sent, seen, lands = [0], [0], [0], {}, {}

    def V(ins):
        ins.then_inc(sem.v, 1)
        nv[0] += 1
        return nv[0]

    def C(ins):
        ins.then_inc(sem.a, 1)
        na[0] += 1
        return na[0]

    def W(q, name, s, k):
        if seen.get((name, s), 0) < k:
            q.wait_ge(sem[s], k)
            seen[(name, s)] = k

    def vw(k, s="v"):
        W(vec, "v", s, k)

    def aw(k, s="a"):
        W(act, "a", s, k)

    def sw(k, s):
        W(syn, "s", s, k)

    def gw(k, s):
        W(g, "g", s, k)

    def quad(b, n=1):
        return slice(32 * b, 32 * (b + n))

    def same_die(a, b):
        return topo.die(T.cores[a]) == topo.die(T.cores[b])

    bits = sorted((1, 2, 4), key=lambda b: same_die(0, b))
    weight = {b: 1 << k for k, b in enumerate(bits)}

    def peer(w):
        return me ^ sum(b for b in bits if w & weight[b])

    every = topo.engines(core, T.cores[peer(1)])
    ends = every[1::2] + every[0::2]

    def spread(seats, swap):
        free = ends[::-1 if swap else 1]
        out = {}
        for k, w in enumerate(sorted(seats, key=lambda w: same_die(me, peer(w)))):
            n = len(every) // len(seats) if len(seats) != 3 else len(every) // 4 * (2 if k == 2 else 1)
            out[w], free = free[:n], free[n:]
        return out

    def send(plan, src, dst, s):
        g.remote_dma_fused([RemoteDMATransfer(dst_ids=[DstId(rid=topo.addr(T.cores[peer(w)])[0], pnc=topo.addr(T.cores[peer(w)])[1])],
                                              dma_engine_mask=sum(1 << e for e in es), remote_sem=sem[s], src=src(w), dst=dst(w))
                            for w, es in plan.items()], local_sem=sem.out)
        sent[0] += sum(len(es) for es in plan.values())
        lands[s] = lands.get(s, 0) + sum(len(es) for es in plan.values())

    def codes(out, win, off):
        return V(vec.tensor_copy(out.bitcast(dt.uint32), win.bitcast(dt.uint32).indirect(off)))

    def scales(out, win, off):
        return C(act.activation(out, win.indirect(off), F.Copy))

    def slot(w):
        return slice(16 + CAP * w, 16 + CAP * w + CAP)

    def part(w):
        return slice(CAP * (w - 1), CAP * w)

    def back(w):
        return slice(16 + PITCH * w, PITCH * (w + 1))

    def iota(ap, pattern, base, cm=0, small=True):
        (g.iota(ap, pattern, base, cm, allow_small_or_imprecise_dtypes=True) if small else g.iota(ap, pattern, base, cm)).then_inc(sem.gi, 1)

    for b in range(4):
        (syn if b < 2 else act).dma_start(T.kt[quad(b)], (T.ky if b < 2 else T.lk)[:]).then_inc(sem.ld_t, 16)
    syn.dma_start(T.xb[:], T.x[:]).then_inc(sem.ld_x, 16)
    syn.dma_start(T.wb[:], T.w[:]).then_inc(sem.ld_w, 16)
    iota(T.pio[:], [[0, 1]], 0, 1 + 2 ** 8 + 2 ** 16, small=False)
    iota(T.seat[:], [[-weight[b] if me & b else weight[b], 2] for b in (4, 2, 1)], sum(weight[b] for b in bits if me & b))
    iota(T.c16[:], [[16, 8]], 0)
    iota(T.pat[:], [[0, 8], [1, 16]], 16 * me - K)
    iota(T.sv0[:], [[CAP, N], [1, 16]], 16 - MID, 1)
    iota(T.cfo[:], [[16, 2], [0, 2]], 0)
    iota(T.tab[:, 0:TAB // 2], [[0, TAB // 2]], -MID)
    G_P, G_SEAT, G_C16, G_PAT, G_SV, G_CFO, G_TAB = range(1, 8)

    lanef, od, par, cb, h3, own = (T.cf[:, k:k + 1] for k in range(6))
    V(vec.memset(T.zz[:], 0.0))
    V(vec.memset(T.pp[:], 0.0))
    V(vec.memset(T.dm[:], 4.0 * K))
    vw(G_P, "gi")
    for k, sh, mask in ((6, 3, BIG + 2), (0, 0, 15), (1, 4, 1), (2, 0, 1), (3, 1, 128 + 15), (4, 3, 1), (5, 1, N - 1)):
        i = V(vec.tensor_scalar(T.ci[:, k:k + 1], T.pio[:], sh, mask, A.logical_shift_right, A.bitwise_and))
    vw(i - 6)
    V(vec.tensor_scalar(T.val[:], T.ci[:, 6:7], -1.0, BIG + 1.0, A.mult, A.add))
    vw(i)
    i_cf = V(vec.tensor_copy(T.cf[:], T.ci[:, 0:6]))
    aw(i_cf, "v")
    for b, n, sh in ((0, 1, 0), (1, 1, 16), (2, 2, 0)):
        i = C(act.activation(T.tb[quad(b, n)], T.cf[quad(b, n), 1:2], F.Identity, bias=float(sh - WIN // 2 - 1 - PITCH // 2), scale=float(CAP + 1)))
    C(act.activation(T.keep[:], T.zz[:, 0:128], F.Identity, bias=par))
    aw(i)
    C(act.activation(T.ini[:], lanef, F.Identity, bias=T.tb[:, 0:1], scale=float(PITCH // 2)))
    aw(G_C16, "gi")
    a_pp = C(act.activation(T.pp[:, 0:128:16], T.c16[:], F.Identity, bias=cb))
    I_K16 = i_cf + 3
    aw(I_K16, "v")
    a_e = C(act.activation(T.e[:, 64:128], T.oh[:, 0:N].indirect(T.k16[:, 4:8]), F.Copy))
    i = C(act.activation(T.negc[:], lanef, F.Identity, bias=float(-K - 16 * me), scale=-1.0))
    aw(G_PAT, "gi")
    for c0 in range(0, WIN, 128):
        a_win = C(act.activation(T.win[:, c0:c0 + 128], T.pat[:], F.Identity, bias=float(K), scale=h3))
    aw(i)
    a_dm = C(act.activation(T.dm[:, 0:56:4], T.zz[:, 0:14], F.Identity, bias=T.negc[:, 0:1]))
    i = C(act.activation(T.cv[:], T.c16[:, 0:2], F.Identity, bias=lanef))
    aw(a_dm)
    C(act.activation(T.dm[:, 48:56], T.dm[:, 48:56], F.Identity, bias=16.0 * (me - peer(N - 1))))
    for b, n, sh in ((0, 1, 0), (1, 1, 1), (2, 2, 0)):
        C(act.activation(T.eb[quad(b, n)], T.cf[quad(b, n), 1:2], F.Identity, bias=float(1 + sh), scale=-1.0))
    aw(i)
    i = C(act.activation(T.c3[:], T.cv[:], F.Identity, bias=-2.0 / 3, scale=1.0 / 3))
    C(act.activation(T.ev2[:], od, F.Identity, bias=2.0, scale=-2.0))
    i_l1 = C(act.activation(T.l1[:], lanef, F.Identity, bias=od, scale=2.0))
    aw(i)
    i = C(act.activation(T.cr[:], T.c3[:], F.Identity, bias=WHOLE))
    C(act.activation(T.d_s[:, 16 + RL:32 + RL], T.zz[:, 0:16], F.Identity, bias=float(-MID)))
    aw(i_l1)
    C(act.activation(T.l2[:], h3, F.Identity, bias=T.l1[:, 0:1], scale=16.0))
    aw(i)
    for m in range(2):
        a_cx = C(act.activation(T.cx[:, m:m + 1], T.cr[:, m:m + 1], F.Identity, bias=T.cv[:, m:m + 1]))
    C(act.activation(T.tab[:, TAB // 2:TAB // 2 + 128], T.zz[:, 0:128], F.Identity, bias=float(-MID)))
    for c0, c1 in ((256, 416), (416, 576)):
        C(act.activation(T.tab[:, TAB // 2 + c0:TAB // 2 + c1], T.zz[:, 0:c1 - c0], F.Identity, bias=float(-MID)))
    aw(G_SV, "gi")
    for b, u in enumerate((2, 1, 0, -1)):
        a_tab = C(act.activation(T.sv[quad(b)], T.sv0[quad(b)], F.Identity, bias=float(16 * u - 32 * b)))

    vw(64, "ld_t")
    i = V(vec.tensor_scalar(T.ko[:], T.kt[:], N - 1, None, A.bitwise_and))
    vw(i_cf)
    vw(G_SEAT, "gi")
    V(vec.tensor_scalar(T.oh[:], T.seat[:], own, T.val[:, 0:1], A.is_equal, A.mult))
    vw(i)
    i = V(vec.tensor_copy(T.k16[:], T.ko[:]))
    assert i == I_K16
    V(vec.tensor_scalar(T.kp[:, 1:16:2], T.kt[:], 3, 255, A.logical_shift_right, A.bitwise_and))
    vw(i)
    i = V(vec.tensor_copy(T.e[:, 0:64], T.oh[:, 0:N].indirect(T.k16[:, 0:4])))
    i_kp = V(vec.tensor_scalar(T.kp[:, 0:16:2], T.kt[:], 3, K - 256, A.logical_shift_right, A.bitwise_and))
    vw(i)
    vw(a_e, "a")
    i = V(vec.tensor_tensor_scan(T.cu[:], T.keep[:], T.e[:], T.ini[:, 0:1], A.mult, A.add))
    vw(i_kp)
    i_pp = V(vec.tensor_copy(T.pp[:, HI:128:LO - HI], T.kp[:]))
    vw(i)
    i = V(vec.transpose(T.ct[:], T.cu[:]))
    vw(i_pp)
    vw(a_pp, "a")
    V(vec.transpose(T.pl[:], T.pp[:]))
    vw(i)
    i_rk = V(vec.tensor_tensor_scan(T.rk[:], T.ct[:, 0:128:2], T.ct[:, 1:128:2], 0.0, A.add, A.min))

    def empty(k):
        V(vec.memset(T.tab[:, TAB // 2 + 128 * k:TAB // 2 + 128 * (k + 1)], float(-MID)))
    V(vec.memset(T.z[:], 0.0))
    V(vec.memset(T.x2[:], 0.0))
    vw(i_rk)
    i = V(vec.tensor_scalar(T.po[:], T.rk[:, 7:64:8], float(WIN // 2), None, A.add))
    empty(1)

    vw(i)
    vw(a_win, "a")
    i = V(vec.tensor_copy(T.win[:, 0:WIN].indirect(T.po[:, 0:8]), T.pl[:]))
    gw(i, "v")
    send({N - 1: ends[0:8]}, lambda w: T.win[:, PITCH * w:PITCH * (w + 1)], lambda w: T.raw[:], "kw")
    vw(16, "ld_x")
    V(vec.quantize_mx(T.xq[:, 0:128], T.xs[:, 0:128], T.xb[:, 0:512]))
    vw(i)

    def met(out, fill, turned):
        return V(vec.tensor_tensor_scan(out, fill, turned, 0.0, A.min, A.add))
    i = V(vec.transpose(T.tw[:], T.win[:]))
    vw(a_cx, "a")
    V(vec.tensor_scalar(T.cot[:], T.cx[:], T.eb[:, 0:1], -1 - WHOLE, A.add, A.add))
    vw(i)
    gw(met(T.ab[:, 8:56], T.dm[:, 0:48], T.tw[:, PITCH + HI:PITCH * (N - 1):LO - HI]), "v")
    for seats, swap in (((1, 3, 5), False), ((2, 4, 6), True)):
        send(spread(seats, swap), lambda w: T.ab[:, 8 * w + 3:8 * w + 8], lambda w: T.kr[:, 8 * w + 3:8 * w + 8], "kr")
    for po, c0, pi in ((quad(0, 2), 1, quad(0, 2)), (quad(0), 0, quad(1)), (quad(1), 2, quad(0))):
        i = V(vec.tensor_tensor(T.z[po, c0:c0 + 2 * NB:2], T.tw[pi, 0:WIN:32], T.tw[pi, 16:WIN:32], A.min))
    V(vec.quantize_mx(T.xq[:, 128:256], T.xs[:, 128:256], T.xb[:, 512:1024]))
    vw(i)
    i = V(vec.tensor_scalar(T.co[:], T.z[:, 0:48].indirect(T.cot[:, 0:2]), float(S - 1), None, A.min))
    i_kr = met(T.kr[:, 0:8], T.dm[:, 0:8], T.tw[:, HI:PITCH:LO - HI])
    V(vec.memset(T.d_s[:, 0:16], float(-MID)))
    vw(i)
    i_co = V(vec.tensor_copy(T.co[quad(2, 2)], T.co[quad(0, 2)]))

    def offsets(c0, w0, w1):
        for j in (1, 0):
            i = V(vec.tensor_copy(T.kofs[quad(2 - 2 * j, 2), c0:c0 + w1 - w0], T.kr[quad(0, 2), 8 * w0 + 4 * j + 3:8 * w1:8]))
        return i

    def enter(c0, w0, w1):
        return V(vec.tensor_copy(T.tab[:, 0:TAB].indirect(T.kofs[:, c0:c0 + w1 - w0]), T.sv[:, 16 * w0:16 * w1]))
    vw(i_kr)
    offsets(0, 0, 1)

    vw(i_co)
    aw(i_co, "v")

    def pick(w0, w1):
        off, to = T.co[:, 1 + 3 * w0:1 + 3 * w1], slice(CAP * (w0 - 1), CAP * (w1 - 1))
        return codes(T.pk_q[:, to], T.xq[:, 0:S], off), scales(T.pk_s[:, to], T.xs[:, 0:S], off)

    def columns(w0, w1, picked):
        gw(picked[0], "v")
        send(spread(range(w0, w1), False), lambda w: T.pk_q[:, part(w)].bitcast(dt.uint8), lambda w: T.in_q[:, slot(w)].bitcast(dt.uint8), "q1")
        gw(picked[1], "a")
        send(spread(range(w0, w1), True), lambda w: T.pk_s[:, part(w)], lambda w: T.in_s[:, slot(w)], "s1")
    columns(5, N, pick(5, N))
    pick(3, 5)
    vw(lands["kw"], "kw")
    i = V(vec.transpose(T.rawt[:], T.raw[:]))
    columns(1, 5, pick(1, 3))
    a_own = scales(T.in_s[:, 0:64], T.xs[:, 0:S], T.co[:, 0:4])
    for gg in range(2):
        for c0 in (0, 16):
            a_x2 = C(act.activation(T.x2[:, 32 * gg + c0:32 * gg + c0 + 4], T.rk[:, 7 + 8 * gg:64:16], F.Copy))

    vw(i)
    i = met(T.kr[:, 56:64], T.dm[:, 48:56], T.rawt[:, HI:PITCH:LO - HI])
    vw(a_tab, "a")
    vw(G_TAB, "gi")
    enter(0, 0, 1)
    vw(i)
    vw(lands["kr"], "kr")
    i = offsets(2, 1, N)
    for b in (0, 2):
        V(vec.tensor_copy(T.rofs[quad(b, 2)], T.kr[quad(2, 2), 3:8 * N:4]))
    vw(i)
    i = enter(2, 1, N)
    aw(i, "v")
    a_g = C(act.activation(T.d_s[:, 16 + 32 * RV:16 + RL], T.tab[:, 0:TAB].indirect(T.rofs[:, 2 * RV:16]), F.Copy))
    i_own1 = codes(T.in_q[:, 0:64], T.xq[:, 0:S], T.co[:, 0:4])
    vw(i)
    i = V(vec.tensor_copy(T.d_s[:, 16:16 + 32 * RV], T.tab[:, 0:TAB].indirect(T.rofs[:, 0:2 * RV])))
    vw(G_CFO, "gi")
    vw(a_x2, "a")
    V(vec.transpose(T.x2t[:], T.x2[:]))
    aw(V(vec.tensor_scalar(T.fot[:], T.cfo[:], T.l2[:, 0:1], None, A.add)), "v")
    a_x3 = C(act.activation(T.x3[:], T.x2t[:, 0:64].indirect(T.fot[:, 0:4]), F.Copy))
    vw(i)
    V(vec.transpose(T.t_s[:, 0:2 * RV:2, :], T.d_s[:, 0:32 * RV]))
    V(vec.transpose(T.t_s[:, 1:2 * RV:2, :], T.d_s[:, 16:16 + 32 * RV]))
    vw(a_g, "a")
    V(vec.transpose(T.t_s[:, 2 * RV:2 * N + 2:2, :], T.d_s[:, 32 * RV:RL + 32]))
    i = V(vec.transpose(T.t_s[:, 2 * RV + 1:2 * N:2, :], T.d_s[:, 16 + 32 * RV:16 + RL]))
    V(vec.tensor_scalar(T.sot[:, 0:4:2], T.cx[:], T.ev2[:, 0:1], -1 - WHOLE, A.add, A.add))
    vw(i)
    i = V(vec.tensor_tensor(T.mx1[quad(0, 2)], T.t_s[quad(0, 2), 0:2 * N + 1, 0:32:16], T.t_s[quad(2, 2), 0:2 * N + 1, 0:32:16], A.max))
    V(vec.memset(T.mx2[:, 34:48], float(-MID)))
    vw(i)
    for b in range(4):
        i = V(vec.tensor_tensor(T.mx2[quad(b), 0:4 * N + 2], T.mx1[quad(0)], T.mx1[quad(1)], A.max))
    vw(i)
    i_so = [V(vec.tensor_scalar(T.so[:, 16 * m:16 * m + 16], T.mx2[:, 0:48].indirect(T.sot[:, 2 * m:2 * m + 1]), float(MID), float(LAND - 1), A.add, A.min))
            for m in (1, 0)]
    vw(a_x3, "a")
    i_x3 = V(vec.transpose(T.x3t[:], T.x3[:]))

    vw(lands["q1"], "q1")
    aw(a_own)
    aw(lands["s1"], "s1")
    for w0, w1 in PARTS:
        vw(i_so[1 + 3 * w0 < 16])
        aw(i_so[1 + 3 * w0 < 16], "v")
        off, to = T.so[:, 1 + 3 * w0:1 + 3 * w1], slice(CAP * (w0 - 1), CAP * (w1 - 1))
        i_p2 = codes(T.p2_q[:, to], T.in_q[:, 0:LAND], off)
        a_p2 = scales(T.p2_s[:, to], T.in_s[:, 0:LAND], off)
        gw(i_p2, "v")
        send(spread(range(w0, w1), False), lambda w: T.p2_q[:, part(w)].bitcast(dt.uint8), lambda w: T.bk_q[:, back(w)].bitcast(dt.uint8), "q2")
        gw(a_p2, "a")
        send(spread(range(w0, w1), True), lambda w: T.p2_s[:, part(w)], lambda w: T.bk_s[:, back(w)], "s2")
    vw(i_x3)
    for b in (0, 2):
        for h in range(2):
            i_fo = V(vec.tensor_scalar(T.fo[quad(b, 2), h:16:2], T.x3t[quad(2, 2), 2 * h:2 * h + 2, 0:4], float(WIN // 2 + 16), None, A.add))
    i_own2 = codes(T.bk_q[:, 0:PITCH], T.in_q[:, 0:LAND], T.so[:, 0:4])
    a_own2 = scales(T.bk_s[:, 0:PITCH], T.in_s[:, 0:LAND], T.so[:, 0:4])
    vw(16, "ld_w")
    V(vec.quantize_mx(T.wq[:], T.ws[:], T.wb[:]))

    vw(max(i_own2, i_fo))
    vw(lands["q2"], "q2")
    aw(i_fo, "v")
    aw(a_own2)
    aw(lands["s2"], "s2")
    codes(T.fp_q[:, 0:64], T.bk_q[:, 0:WIN], T.fo[:, 0:4])
    codes(T.fp_q[:, 64:128], T.bk_q[:, 0:WIN], T.fo[:, 4:8])
    vw(a_own2, "a")
    vw(lands["s2"], "s2")
    done = [(V(vec.tensor_copy(T.fp_s[:, 64:128], T.bk_s[:, 0:WIN].indirect(T.fo[:, 4:8]))),
             scales(T.fp_s[:, 0:64], T.bk_s[:, 0:WIN], T.fo[:, 0:4])),
            (codes(T.fp_q[:, 128:256], T.bk_q[:, 0:WIN], T.fo[:, 8:16]), scales(T.fp_s[:, 128:256], T.bk_s[:, 0:WIN], T.fo[:, 8:16]))]
    for f in range(2):
        c = slice(128 * f, 128 * f + 128)
        W(ten, "t", "v", done[f][0])
        W(ten, "t", "a", done[f][1])
        for o in range(O):
            ws = slice(128 * o, 128 * o + 128)
            b0 = 512 * (O * f + o)
            ten.matmul_mx(T.ps[:, b0:b0 + 128], T.wq[:, ws], T.ws[:, ws], T.fp_q[:, c], T.fp_s[:, c], True, True).then_inc(sem.t, 1)
    for f in range(2):
        vw(O * f + 1, "t")
        iv = V(vec.tensor_copy(T.yb[:, 128 * f:128 * f + 128], T.ps[:, 1024 * f:1024 * f + 128]))
        aw(O * f + 2, "t")
        ia = C(act.activation(T.yb[:, S + 128 * f:S + 128 * f + 128], T.ps[:, 1024 * f + 512:1024 * f + 640], F.Copy))
        sw(iv, "v")
        syn.dma_start(T.y[:, 128 * f:128 * f + 128], T.yb[:, 128 * f:128 * f + 128]).then_inc(sem.st, 16)
        if f == 0:
            sw(ia, "a")
        else:
            aw(ia)
        (syn if f == 0 else act).dma_start(T.y[:, S + 128 * f:S + 128 * f + 128], T.yb[:, S + 128 * f:S + 128 * f + 128]).then_inc(sem.st, 16)
    sw(64, "st")
    gw(sent[0], "out")
